import numpy as np, ml_dtypes
CORES = [113,118,241,246]
N = 4
BF = ml_dtypes.bfloat16
def gentries(a):
    return np.ascontiguousarray(a.reshape(8, 16, -1).transpose(0, 2, 1)).reshape(8, -1)
def gtable(e):
    e = np.asarray(e); return np.ascontiguousarray(e.reshape(8, -1, 16).transpose(0, 2, 1)).reshape(128, -1).astype(np.int32)
W, M, B, T, P, QU, TH = 2048, 512, 256, 4, 1, 12, 254
def parts(rng):
    d = {}
    d["pr"] = (224 * rng.random((N, 8, 1, W)) ** 3 + 32 * rng.random((N, 8, 16, W))).astype(np.int64)
    d["ad"] = (np.exp2(rng.integers(2, 8, (N, 8, 1, W))) * rng.random((N, 8, 16, W))).astype(np.int64)
    d["mc"] = rng.integers(0, W, (N, 8, 16, M))
    d["gl"] = (224 * rng.random((N, 8, 1, M)) + 32 * rng.random((N, 8, 16, M))).astype(np.int64)
    d["z"] = (224 * rng.random((N, 8, 1, B)) + 32 * rng.random((N, 8, 16, B))).astype(np.int64)
    d["m"] = rng.integers(0, M, (N, 8, B))
    d["dv"] = (np.exp2(rng.integers(2, 8, (N, 8, 1, T * P))) * rng.random((N, 8, 16, T * P))).astype(np.int64)
    d["wt"] = rng.integers(0, 256, (N, 8, 16, 1))
    return d
def flat(a):
    return np.ascontiguousarray(np.reshape(a, (N, 128, -1)))
def pack(d):
    h = {k: flat(d[k]).astype(np.float32).astype(BF) for k in ("pr", "ad", "gl", "z", "dv", "wt")}
    return {"pr": h["pr"], "ad": h["ad"], "mc": flat(d["mc"]).astype(np.int32), "gl": h["gl"], "z0": h["z"], "m0": np.stack([gtable(a) for a in d["m"]]), "dv": h["dv"], "wt": h["wt"]}
def setup_inputs(rng):
    return pack(parts(rng))
def sized(rng, hi, *shape):
    return np.minimum((float(hi + 1) ** rng.random(shape[:-2] + (1, shape[-1])) * rng.random(shape)).astype(np.int64), hi)
def setup_inputs_spread(rng):
    d = parts(rng)
    d["pr"] = sized(rng, 255, N, 8, 16, W); d["ad"] = sized(rng, 127, N, 8, 16, W); d["dv"] = sized(rng, 255, N, 8, 16, T * P); d["wt"] = sized(rng, 255, N, 8, 16, 1)
    a = sized(rng, 255, N, 8, 16, M); d["gl"] = np.where(rng.random((N, 8, 1, M)) < 0.5, 255 - a, a)
    a = sized(rng, 255, N, 8, 16, B); d["z"] = np.where(rng.random((N, 8, 1, B)) < 0.6, rng.integers(0, 256, (N, 8, 16, B)), a)
    d["mc"] = np.minimum((W * rng.random((N, 8, 16, M)) ** 3).astype(np.int64), W - 1)
    d["m"] = np.minimum((M * rng.random((N, 8, B)) ** 2).astype(np.int64), M - 1)
    return pack(d)
def mix(rng, hi, *shape):
    q = rng.choice(np.array([0.0, 0.1, 0.5, 0.8, 0.9, 1.0]), shape[:-2] + (1, shape[-1]))
    return (rng.random(shape) < q).astype(np.int64) * hi
def setup_inputs_ends(rng):
    d = {"pr": mix(rng, 255, N, 8, 16, W), "ad": mix(rng, 127, N, 8, 16, W), "mc": mix(rng, W - 1, N, 8, 16, M), "gl": mix(rng, 255, N, 8, 16, M), "z": mix(rng, 255, N, 8, 16, B),
         "m": (M - 1) * rng.integers(0, 2, (N, 8, B)), "dv": mix(rng, 255, N, 8, 16, T * P), "wt": mix(rng, 255, N, 8, 16, 1)}
    pr, ad, mc, gl, z, m, dv, wt = [d[k] for k in ("pr", "ad", "mc", "gl", "z", "m", "dv", "wt")]; a = N - 1
    wt[:, 0, :8] = 0; wt[:, 0, 8:] = 255
    gl[0, :, :, 0] = 0; gl[0, :, :, M - 1] = 0
    gl[1, :, :, 0] = 0; gl[1, :, :, M - 1] = 255; m[1] = 0; m[1, 7, B - 1] = M - 1; z[1, 7, :, B - 1] = 0; dv[1, 7, :, :P] = 0
    pr[a, 7, :, 0] = 255; ad[a, 7, :, 0] = 127; ad[a, 7, :, W - 1] = 0; gl[a, 7, :, 0] = 255; gl[a, 7, :, M - 1] = 255
    mc[a, 7, :, 0] = 0; mc[a, 7, :, M - 1] = W - 1
    wt[a, 7] = 0; wt[a, 7, 15] = 255; wt[a, 7, 13:15] = 1
    for i in (0, 1, B - 2, B - 1): z[a, 7, :, i] = 255
    m[a, 7, 1] = 0; m[a, 7, B - 2] = 0; m[a, 7, B - 1] = M - 1
    m[a, 7, :B - 1] = np.where(np.all(z[a, 7, 13:, :B - 1] == 255, axis=0), 0, m[a, 7, :B - 1])
    wt[a, 6] = 255; gl[a, 6, :, 0] = 0; z[a, 6, :, 0] = 255; z[a, 6, :, B - 1] = 255; z[a, 6, :, 1] = 0; z[a, 6, :, B - 2] = 0
    m[a, 6, 0] = 0; m[a, 6, 1] = 0; m[a, 6, B - 2] = 0; m[a, 6, B - 1] = M - 1
    return pack(d)
def setup_inputs_corners(rng):
    d = parts(rng); pr, ad, mc, gl, z, m, dv, wt = [d[k] for k in ("pr", "ad", "mc", "gl", "z", "m", "dv", "wt")]
    m[:, 0] = 0; m[:, 1] = M - 1; m[:, 2] = np.arange(B); m[:, 3] = M - 1 - np.arange(B)
    wt[:, 0] = 0; wt[:, 1] = 255; dv[:, 4] = 255; dv[:, 5] = 0
    one = rng.integers(0, W, (N, 1, M)); one[:, 0, 0] = 0; one[:, 0, M - 1] = W - 1; mc[:, 4] = one; m[:, 4, 0] = 0; m[:, 4, B - 1] = M - 1
    gl[:, 5] = np.maximum(gl[:, 5], 1); goal = np.take_along_axis(gl[:, 5], m[:, 5][:, None, :], 2)
    c = rng.choice(np.array([0, QU - 1, QU, QU + 1, 16]), (N, 1, B)); place = np.argsort(np.argsort(rng.random((N, 16, B)), axis=1), axis=1)
    z[:, 5] = goal - (place >= c)
    ad[:, 6] = TH // 16; ad[:, 6, 15] = TH - 15 * (TH // 16) + rng.integers(-1, 2, (N, W))
    pr[:, 6] = np.maximum(pr[:, 6], 40); gl[:, 6] = np.maximum(gl[:, 6], 200); z[:, 6] = np.where(rng.random((N, 1, B)) < 0.7, 255, z[:, 6])
    pr[:, 7] = 255; gl[:, 7] = 255; z[:, 7] = 255 * rng.integers(0, 2, (N, 1, B)); wt[:, 7] = (255 * (np.arange(N) & 1)).reshape(N, 1, 1)
    return pack(d)
def setup_inputs_crowd(rng):
    d = parts(rng); pr, gl, z, m, dv, wt = [d[k] for k in ("pr", "gl", "z", "m", "dv", "wt")]
    gl[:, :6] = 0; m[:, :4] = np.argsort(rng.random((N, 4, M)), axis=-1)[..., :B]
    wt[:, :4] = 0; wt[:, :4, 0] = 1; wt[:, :4, 1] = 255
    c = np.full((N, 4, B), M - 1); c[:, 1, 0] = 0; c[:, 3] = rng.choice(np.array([0, 1, M // 2, M - 1]), (N, B))
    v = (c - 37 * m[:, :4]) & (M - 1); z[:, :4, 0] = v - 255 * (v // 255); z[:, :4, 1] = v // 255
    for i in range(N): gl[i, 2, :, m[i, 2, 0]] = 255
    z[:, 2, 2:, 0] = 100; dv[:, 2, :, :P] = 1
    for g in (4, 5):
        z[:, g] = z[:, g, :, :1].copy(); m[:, g] = m[:, g, :1].copy()
    z[:, 5, :, B - 1] = 255 - z[:, 5, :, 0]
    gl[:, 6] = 255
    pr[:, 7] = 255; gl[:, 7] = 255; z[:, 7] = 0; z[:, 7, :, B - 1] = 255; m[:, 7] = m[:, 7, :1].copy()
    return pack(d)
def setup_inputs_few(rng):
    d = parts(rng); d["z"] = np.minimum(d["z"], 254); d["dv"] = np.maximum(d["dv"], 1)
    mc, gl, z, m, wt = [d[k] for k in ("mc", "gl", "z", "m", "wt")]
    gl[1::2] = 255; z[1::2, 7, :, B - 1] = 255
    full = rng.permutation(np.array([0, 1, 3, 4]))
    for i in range(0, N, 2):
        g = int(full[(i // 2) & 3]); gl[i, g] = 0; m[i, g] = rng.permutation(M)[:B]
        wt[i, g] = 0; wt[i, g, 0] = 1; wt[i, g, 1] = 255
        a = rng.choice(np.array([11, 13, 23, 25, 27, 29]), B); u = W - 32 + a
        z[i, g, 1] = u // 255; z[i, g, 0] = u - 255 * (u // 255)
        mc[i, g, 15, m[i, g]] = W - 32 + ((-(a ** 7)) & 31)
    return pack(d)
def check_inputs(d):
    bad = []
    for k, hi in (("pr", 255), ("ad", 127), ("mc", W - 1), ("gl", 255), ("z0", 255), ("m0", M - 1), ("dv", 255), ("wt", 255)):
        a = np.asarray(d[k]).astype(np.float64)
        if not (np.min(a) >= 0 and np.max(a) <= hi): bad.append("range of " + k)
        elif np.any(a != np.floor(a)): bad.append("whole numbers of " + k)
    return bad
def reference(pr, ad, mc, gl, z0, m0, dv, wt):
    need_of, add_of, goal_of, z, dist, weight = [a.astype(np.float32).astype(np.int64).reshape(N, 8, 16, -1) for a in (pr, ad, gl, z0, dv, wt)]
    tb = mc.astype(np.int64).reshape(N, 8, 16, M); m = np.stack([gentries(a) for a in m0]).astype(np.int64)
    seen = [0] * N
    for t in range(T):
        for q in range(N):
            s = (q - t) % N; zz = z[s]; mm = m[s]
            o = np.take_along_axis(tb[q], mm[:, None, :], 2)
            ix = o.reshape(8, 1, 16 * B)
            p = np.take_along_axis(need_of[q], ix, 2).reshape(8, 16, 16, B); a = np.take_along_axis(add_of[q], ix, 2).reshape(8, 16, 16, B)
            K = [None] * 16 + [np.take_along_axis(goal_of[q], mm[:, None, :], 2)]
            for k in range(15, -1, -1): K[k] = np.maximum(p[:, :, k], K[k + 1] - a[:, :, k])
            K = np.stack(K)
            for j in range(P):
                met = np.add.reduce((zz[None] >= K).astype(np.int64), axis=2)
                best = np.max(np.where(met >= QU + (seen[q] & 1), np.arange(17).reshape(17, 1, 1), -1), axis=0)
                ak = np.take_along_axis(a, np.clip(best, 0, 15)[:, None, None, :], 2)[:, :, 0]
                new = np.abs(np.minimum(255, zz + ak) - dist[q, :, :, t * P + j][:, :, None])
                zz = np.where(((best >= 0) & (best < 16))[:, None, :], new, zz)
            goal = best == 16
            u = np.add.reduce(weight[q] * zz, axis=1) & (W - 1); to = (u + 37 * mm) & (M - 1)
            use = np.add.reduce(np.minimum(a, K[1:].transpose(1, 2, 0, 3)), axis=1)
            fresh = (((o * u[:, None, :]) >> 5) + o + 37 * np.arange(16).reshape(1, 16, 1)) & (W - 1)
            o = np.where(use < TH, fresh, o)
            for g in range(8):
                who = np.flatnonzero(goal[g]); where, first = np.unique(to[g, who], return_index=True)
                tb[q, g][:, where] = o[g][:, who[first]]
            z[s] = zz; m[s] = np.where(goal | (best < 0), to, mm); seen[q] = int(np.count_nonzero(goal))
    back = [(q - (T - 1)) % N for q in range(N)]
    return {"ymc": tb.reshape(N, 128, M).astype(np.float32), "yz": z[back].reshape(N, 128, B).astype(np.float32), "ym": np.stack([gtable(m[s]) for s in back]).astype(np.float32)}

@@ -1,0 +1,510 @@
+from concourse.mybir import dt, AluOpType, AxisListType, ActivationFunctionType
+A = AluOpType
+F = ActivationFunctionType
+
+T_STEPS, W, M, B, QU, TH = 4, 2048, 512, 256, 12, 254
+BIG = 131072.0
+HALF = [(0, 128), (128, 256)]
+VPR = [32, 16]
+CMPV = ["VVVS", "SSSS"]
+ORDER = ("ml o16:1 prs:0 GB:1 zs c16 prs:1 prv:0 gw:0 scan:0 prv:1 xq of bit br ble use:0 grep ui d0:3 toL d0:2 glt d0:1 d0:0 ad:1 blo fl "
+         "ok:0 p0 gw:1 oh:0 p1 scan:1 vl:0 p2 dl:0 p3 p4 sm:0 oP p5 uu fq d1:3 ft fr td t1:0 df use:1 conf t2:0 low ldf cx d1:2 t3:0 wr "
+         "d1:1 d1:0 fl +o16:0 ok:1 oh:1 vl:1 dl:1 sz:0 sm:1 +ad:0 t1:1 as t2:1 par t3:1 +GB:0 sz:1").split()
+SB, PS = "sbuf", "psum"
+BF, F4, I4, U2 = "bfloat16", "float32", "int32", "uint16"
+SCRATCH = {"CMP": (SB, [128, B, 16], BF), "EQ0": (SB, [128, 16, 128], BF), "EQ1": (SB, [128, 8, 128], BF),
+           "bD0": (PS, [128, 128, 4], F4), "bD1": (PS, [128, 128, 4], F4), "bG0": (PS, [128, 16, 32], F4), "bG1": (PS, [128, 16, 32], F4)}
+for _n, _w, _d in ([(x, 512, F4) for x in ("bM", "bL", "bF", "bO")]
+                   + [("PRW", W, BF), ("ADW", W, BF), ("GLW", M, BF), ("MCI", M, I4), ("MC", M + B, F4), ("WI", M, I4), ("WJI", M, I4), ("W37", M, BF),
+                      ("M0", 16, I4), ("DV", 4, BF), ("WT", 1, BF), ("O16", B, U2), ("D0", 32 * B, BF), ("D1", 32 * B, BF), ("KR", 32 * B, BF),
+                      ("AOFF", 16, U2), ("OFF", 16, U2), ("GLT", 32, BF), ("CX", 128, F4), ("LI", 64, I4), ("LF", 144, F4), ("CI", 4, I4),
+                      ("CF", 24, F4), ("THR", 8, F4), ("AI", 2, I4), ("DG", 512, BF), ("DT", 512, BF), ("IOT", B, F4), ("TB", 64, F4), ("SL", 48, F4), ("B32", 8, BF)]
+                   + [(x, 144, BF) for x in ("E1", "E2", "E0", "EH", "NE", "WE", "WJ")]
+                   + [(x, B, BF) for x in ("GB", "MB", "C16", "P0", "BLE", "BLO", "BR", "GREP", "OK", "OH")]
+                   + [(x, B, I4) for x in ("UI", "UU", "FQ", "FT", "FR", "XQ", "BIT")]
+                   + [(x, B, F4) for x in ("OF", "DF", "LDF", "T1", "T2", "T3", "ZF")]
+                   + [(x, 128, F4) for x in ("DX1", "DX2", "DX")]
+                   + [(x, 128, BF) for x in ("ONE", "BO1", "BO", "IDN", "NID", "NBO", "U1", "UP", "NEG", "BW")]):
+    SCRATCH[_n] = (PS if _n in ("bM", "bL", "bF", "bO") else SB, [128, _w], _d)
+LOADS = ["m0", "mc", "z0", "gl", "wt", "dv", "pr", "ad"]
+OUTS = ["ymc", "yz0", "yz1", "ym"]
+SEMAPHORES = ["V", "S", "T", "G"] + ["l_" + n for n in LOADS] + ["o_" + n for n in OUTS]
+for _t in range(T_STEPS):
+    SCRATCH["Z%d" % _t] = (SB, [128, B], BF)
+    SCRATCH["ML%d" % _t] = (SB, [128, 16], U2)
+    if _t:
+        SCRATCH["ZO%d" % _t] = (SB, [128, B], BF)
+        SCRATCH["MO%d" % _t] = (SB, [128, 16], U2)
+        SEMAPHORES += ["%s%s%d%d" % (a, b, _t, h) for a in "rs" for b in "mz" for h in (0, 1)]
+
+
+def rank_program(g, core, T, topo):
+    rank = T.rank_of(core)
+    if rank is None:
+        return
+    n = len(T.cores)
+    nxt, prv = T.cores[(rank + 1) % n], T.cores[(rank - 1) % n]
+    V, S, P = g.vector, g.scalar, g.tensor
+    QS = {"V": V, "S": S, "T": P, "G": g, "Y": g.sync}
+    cnt = {e: 0 for e in QS}
+    clock = {e: {} for e in QS}
+    snap = {}
+    wrote, read, bank = {}, {}, {}
+
+    def need(e, pairs):
+        want = {}
+        for s, v in pairs:
+            want[s] = max(want.get(s, 0), v)
+        for s, v in want.items():
+            if clock[e].get(s, 0) < v:
+                QS[e].wait_ge(T.sem[s], v)
+                clock[e][s] = v
+                for s2, v2 in snap.get((s, v), {}).items():
+                    clock[e][s2] = max(clock[e].get(s2, 0), v2)
+
+    def deps(e, r, w, b):
+        p = [wrote[x] for x in r]
+        for x in w:
+            q = ([wrote[x]] if x in wrote else []) + list(read.get(x, {}).items())
+            p += [y for y in q if not (e == "T" and y[0] == "T")]
+        for x in b:
+            p += [q for q in bank.get(x, {}).items() if q[0] != e]
+        need(e, p)
+
+    def mark(tag, r, w, b):
+        for x in r:
+            d = read.setdefault(x, {})
+            d[tag[0]] = max(d.get(tag[0], 0), tag[1])
+        for x in w:
+            wrote[x] = tag
+            read[x] = {}
+        for x in b:
+            bank.setdefault(x, {})[tag[0]] = tag[1]
+
+    def op(e, fn, r="", w="", b=""):
+        r, w, b = r.split(), w.split(), b.split()
+        deps(e, r, w, b)
+        cnt[e] += 1
+        fn().then_inc(T.sem[e], 1)
+        snap[(e, cnt[e])] = dict(clock[e])
+        mark((e, cnt[e]), r, w, b)
+
+    def dma(e, out, in_, sem, r="", w=""):
+        r, w = r.split(), w.split()
+        deps(e, r, w, [])
+        QS[e].dma_start(out, in_).then_inc(T.sem[sem], 16)
+        mark((sem, 16), r, w, [])
+
+    eng = lambda a, b: topo.engines(a, b)[:8]
+
+    def send(buf, t, h, c0, c1, src, r):
+        rid, pid = topo.addr(nxt, core)
+        deps("G", [r], [], [])
+        k = ("m" if buf == "ML" else "z") + "%d%d" % (t, h)
+        g.remote_dma(T[buf + str(t)][:, c0:c1], src[:, c0:c1], T.sem["r" + k], T.sem["s" + k], pid, rid, sum(1 << e for e in eng(core, nxt)))
+        mark(("s" + k, len(eng(core, nxt))), [r], [], [])
+        wrote["%s%d_%d" % (buf, t, h)] = ("r" + k, len(eng(prv, core)))
+
+    def mm(out, l, rr, r, w, b, st=True, sp=True):
+        op("T", lambda: P.matmul(out, l, rr, st, sp), r, w, b)
+
+    def tt(out, a, c, o, r, w, b=""):
+        op("V", lambda: V.tensor_tensor(out, a, c, o), r, w, b)
+
+    def ts(out, a, s1, s2, o1, o2, r, w, b=""):
+        if o2 is None:
+            op("V", lambda: V.tensor_scalar(out, a, s1, None, o1), r, w, b)
+        else:
+            op("V", lambda: V.tensor_scalar(out, a, s1, s2, o1, o2), r, w, b)
+
+    def tc(out, a, r, w, b=""):
+        op("V", lambda: V.tensor_copy(out, a), r, w, b)
+
+    def ms(out, c, w):
+        op("V", lambda: V.memset(out, c), "", w)
+
+    def act(out, a, f, r, w, b="", **kw):
+        op("S", lambda: S.activation(out, a, f, **kw), r, w, b)
+
+    def aff(o, i, pat, cmp, fill, base, cm, r, w):
+        op("G", lambda: g.affine_select(o[:], i[:], pat, cmp, fill, base, cm), r, w)
+
+    def slot(pad, k):
+        return pad[:, 15 - k:143 - k]
+
+    cf = lambda i: T.CF[:, i:i + 1]
+    li = lambda i: T.LI[:, 16 * i:16 * i + 16]
+    lf = lambda i: T.LF[:, 16 * i:16 * i + 16]
+    lh = lambda i, h: T.LF[:, 16 * i + 8 * h:16 * i + 8 * h + 8]
+    L = lambda i: T.bL[:, i:i + 16]
+
+    dma("Y", T.M0[:], T.m0[:], "l_m0", "", "M0")
+    dma("Y", T.MCI[:], T.mc[:], "l_mc", "", "MCI")
+    dma("S", T.GLW[:], T.gl[:], "l_gl", "", "GLW")
+    dma("S", T.ADW[:], T.ad[:], "l_ad", "", "ADW")
+    dma("Y", T.PRW[:], T.pr[:], "l_pr", "", "PRW")
+    dma("Y", T.Z0[:], T.z0[:], "l_z0", "", "Z0_0 Z0_1")
+    dma("Y", T.WT[:], T.wt[:], "l_wt", "", "WT")
+    dma("Y", T.DV[:], T.dv[:], "l_dv", "", "DV")
+
+    ms(T.ONE[:], 1.0, "ONE")
+    ms(T.E1[:], 0.0, "E1")
+    ms(T.E1[:, 15::16], 1.0, "E1")
+    op("G", lambda: g.iota(T.CI[:, 0:1], [[0, 1]], 0, 1), "", "pc")
+    op("G", lambda: g.iota(T.IOT[:], [[1, B]], 0, 0, allow_small_or_imprecise_dtypes=True), "", "IOT")
+    aff(T.E2, T.E1, [[-16, 9], [0, 16]], A.is_ge, 0.0, 0, 1, "E1", "E2")
+    aff(T.E0, T.E2, [[16, 9], [0, 16]], A.is_ge, 0.0, 15, -1, "E2", "E0")
+    aff(T.BO1, T.ONE, [[-16, 8], [0, 16]], A.is_ge, 0.0, 0, 1, "ONE", "BO1")
+    aff(T.BO, T.BO1, [[16, 8], [0, 16]], A.is_ge, 0.0, 15, -1, "BO1", "BO")
+    aff(T.IDN, T.ONE, [[-1, 128]], A.is_equal, 0.0, 0, 1, "ONE", "IDN")
+    op("G", lambda: g.iota(T.WI[:], [[37, M]], 0, 0), "", "WI")
+    ts(T.CI[:, 1:2], T.CI[:, 0:1], 15, None, A.bitwise_and, None, "pc", "kc")
+    ts(T.CI[:, 2:3], T.CI[:, 0:1], 4, None, A.arith_shift_right, None, "pc", "gc")
+    ts(T.CI[:, 3:4], T.CI[:, 0:1], 4, 1, A.arith_shift_right, A.bitwise_and, "pc", "oc")
+    ms(T.TB[:, 0:16], 0.5, "tba")
+    ms(T.TB[:, 16:32], 0.0, "tbb")
+    tc(cf(0), T.CI[:, 1:2], "kc", "kf")
+    tc(cf(1), T.CI[:, 2:3], "gc", "gf")
+    tc(cf(2), T.CI[:, 3:4], "oc", "odd")
+    tc(cf(3), T.CI[:, 0:1], "pc", "pf")
+    op("V", lambda: V.tensor_tensor_scan(T.TB[:, 32:48], T.TB[:, 0:16], T.TB[:, 16:32], 2.0, A.mult, A.add), "tba tbb", "tbc")
+    ts(cf(5), cf(0), 8.5, None, A.is_le, None, "kf", "le8")
+    ts(cf(6), cf(0), 9.0, None, A.is_equal, None, "kf", "is9")
+    ts(T.TB[:, 48:64], T.IOT[:, 0:16], cf(0), None, A.is_equal, None, "IOT kf", "tbm")
+    ts(cf(4), cf(2), -1.0, 1.0, A.mult, A.add, "odd", "even")
+    ts(cf(7), cf(5), -0.5, cf(6), A.mult, A.add, "le8 is9", "base")
+    ts(cf(12), cf(6), 2.0 ** -9, None, A.mult, None, "is9", "c9")
+    ts(cf(13), cf(5), -0.5, None, A.mult, None, "le8", "nle8")
+    tt(T.TB[:, 0:16], T.TB[:, 32:48], T.TB[:, 48:64], A.mult, "tbc tbm", "tba")
+
+    def zeros(c):
+        lo, hi = 32 * HALF[c][0], 32 * HALF[c][1]
+        ms(T.D0[:, lo:hi:2], 0.0, "d0z%d" % c)
+        ms(T.D0[:, lo:hi:32], -512.0, "d0z%d" % c)
+        if c:
+            ms(T.D1[:, lo + 1:hi:2], 0.0, "d1z%d" % c)
+        else:
+            act(T.D1[:, lo + 1:hi:2], T.D0[:, lo:hi:2], F.Copy, "d0z0", "d1z0", scale=0.0)
+
+    zeros(0)
+    ms(cf(21), 0.5, "half")
+    ms(cf(22), 255.0, "c255")
+    ms(cf(23), -255.0, "cm255")
+    ms(T.THR[:, 0:1], float(2 * QU - 16), "thd0")
+    ms(T.THR[:, 4:5], 17.0 - 2 * QU, "thb0")
+    op("V", lambda: V.tensor_reduce(cf(14), T.TB[:, 0:16], AxisListType.X, A.add), "tba", "cb0")
+    ts(cf(8), cf(5), cf(4), None, A.mult, None, "le8 even", "e1")
+    ts(cf(9), cf(7), cf(4), None, A.mult, None, "base even", "e2")
+    ts(cf(10), cf(5), cf(2), None, A.mult, None, "le8 odd", "o1")
+    ts(cf(11), cf(7), cf(2), None, A.mult, None, "base odd", "o2")
+    ts(cf(15), cf(14), cf(5), None, A.mult, None, "cb0 le8", "cb")
+    ts(cf(5), cf(14), 0.5, -0.5, A.mult, A.add, "cb0 cb", "cb2 le8")
+    ts(cf(17), cf(0), 2.0, -1.0, A.mult, A.add, "kf", "cj")
+    tc(T.ML0[:], T.M0[:], "M0", "ML0_0 ML0_1")
+    ms(T.MC[:, M:M + B], 0.0, "MC")
+    tc(T.MC[:, 0:M], T.MCI[:], "MCI", "MC")
+
+    def later_const():
+        ts(T.NID[:], T.IDN[:], -1.0, None, A.mult, None, "IDN", "NID")
+        ts(T.BW[:], T.BO[:], T.WT[:, 0:1], None, A.mult, None, "BO WT", "BW")
+        ts(T.WE[:], T.E0[:], T.WT[:, 0:1], None, A.mult, None, "E0 WT", "WE")
+        ts(T.WJI[:], T.WI[:], M - 1, None, A.bitwise_and, None, "WI", "WJI")
+        ts(T.W37[:], T.WJI[:], -256.0, None, A.add, None, "WJI", "W37")
+        ts(T.bM[:, B:2 * B], T.IOT[:], cf(12), cf(13), A.mult, A.add, "IOT c9 nle8", "CONST", "bM")
+        ts(cf(16), cf(0), 1184.0, None, A.mult, None, "kf", "c1184")
+        ts(cf(18), cf(1), -BIG, 7 * BIG + 0.5, A.mult, A.add, "gf", "nb")
+        ts(cf(19), cf(3), -1.0, -1152.0, A.mult, A.add, "pf", "bias0")
+        ts(cf(20), cf(3), -1.0, -1280.0, A.mult, A.add, "pf", "bias1")
+        ts(T.SL[:, 32:48], T.IOT[:, 0:16], 16.0, cf(0), A.mult, A.add, "IOT kf", "sl")
+        ms(T.DX1[:], -16.0 * BIG, "DX1")
+        ts(T.NBO[:], T.BO[:], -1.0, None, A.mult, None, "BO", "NBO")
+        ts(T.NEG[:], T.BO[:], -0.03125, None, A.mult, None, "BO", "NEG")
+        ts(T.NE[:], T.E0[:], -1.0, None, A.mult, None, "E0", "NE")
+        ts(T.EH[:], T.E0[:], 2.0, None, A.mult, None, "E0", "EH")
+        ts(T.WJ[:], T.E0[:], cf(17), None, A.mult, None, "E0 cj", "WJ")
+        ts(T.SL[:, 0:16], T.SL[:, 32:48], 32.0, None, A.mult, None, "sl", "b32f")
+        ts(T.SL[:, 16:32], T.SL[:, 32:48], float(M), None, A.add, None, "sl", "b512")
+        tc(T.B32[:], T.SL[:, 0:8], "b32f", "B32")
+        aff(T.U1, T.NBO, [[-1, 128]], A.not_equal, 1.0, 0, 1, "NBO", "U1")
+        aff(T.UP, T.U1, [[-1, 128]], A.is_ge, 0.0, 0, 1, "U1", "UP")
+        aff(T.DX2, T.DX1, [[0, 16], [-16, 8]], A.is_ge, BIG, 0, 1, "DX1", "DX2")
+        aff(T.DX, T.DX2, [[0, 16], [16, 8]], A.is_ge, BIG, 15, -1, "DX2", "DX")
+
+    def passes():
+        for t in range(T_STEPS):
+            ts(T.DG[:, 128 * t:128 * t + 128], T.IDN[:], T.DV[:, t:t + 1], None, A.mult, None, "IDN DV", "DG%d" % t)
+        mm(T.bF[:], T.BO[:], T.DG[:], "BO DG0 DG1 DG2 DG3", "dtp", "bF")
+        tc(T.DT[:], T.bF[:], "dtp", "DT", "bF")
+
+    def step(t):
+        last = t == T_STEPS - 1
+        Z, ML = T["Z%d" % t], T["ML%d" % t]
+        zh, mh = ["Z%d_0" % t, "Z%d_1" % t], ["ML%d_0" % t, "ML%d_1" % t]
+        zr, mr, thd = " ".join(zh), " ".join(mh), "thd%d" % t
+        thdc = T.THR[:, t:t + 1]
+        pend = []
+        for x in ("d1v0", "d1v1", "d1s0", "d1s1"):
+            wrote.setdefault(x, ("V", 1))
+
+        def kr(c, i):
+            return T.KR[:, 32 * HALF[c][0] + i:32 * HALF[c][1]:32]
+
+        def o16(c):
+            s0, s1 = HALF[c]
+            tc(T.O16[:, s0:s1], T.MC[:, 0:M].indirect(ML[:, 8 * c:8 * c + 8]), "MC " + mh[c], "O16%d" % c)
+
+        def GB(c):
+            s0, s1 = HALF[c]
+            act(T.GB[:, s0:s1], T.GLW[:].indirect(ML[:, 8 * c:8 * c + 8]), F.Copy, "GLW " + mh[c], "GB%d" % c)
+
+        def ad(c):
+            s0, s1 = HALF[c]
+            act(T.D0[:, 32 * s0 + 1:32 * s1:2], T.ADW[:].indirect(T.O16[:, s0:s1]), F.Copy, "ADW O16%d" % c, "d0a%d" % c, scale=-1.0)
+
+        def prs(c):
+            s0, s1 = HALF[c]
+            s0 += VPR[c]
+            if s1 > s0:
+                act(T.D1[:, 32 * s0:32 * s1:2], T.PRW[:].indirect(T.O16[:, s0:s1]), F.Copy, "PRW O16%d" % c, "d1s%d" % c)
+
+        def prv_(c):
+            s0 = HALF[c][0]
+            s1 = s0 + VPR[c]
+            if s1 > s0:
+                tc(T.D1[:, 32 * s0:32 * s1:2], T.PRW[:].indirect(T.O16[:, s0:s1]), "PRW O16%d" % c, "d1v%d" % c)
+
+        def gw(c):
+            s0, s1 = HALF[c]
+            tc(T.P0[:, s0:s1], T.D1[:, 32 * s0:32 * s1:32], "d1v%d d1s%d" % (c, c), "P0%d" % c)
+            tc(T.D1[:, 32 * s0 + 32:32 * s1:32], T.GB[:, s0:s1 - 1], "GB%d" % c, "d1v%d d1s%d" % (c, c))
+
+        def scan(c):
+            s0, s1 = HALF[c]
+            hi, lo = 32 * s1 - 1, 32 * s0 - 1 if s0 else None
+            op("V", lambda: V.tensor_tensor_scan(T.KR[:, hi:lo:-1], T.D0[:, hi:lo:-1], T.D1[:, hi:lo:-1], T.GB[:, s1 - 1:s1], A.add, A.max),
+               "GB{0} d0a{0} d0z{0} d1v{0} d1s{0} d1z{0}".format(c), "KR%d" % c)
+            tt(kr(c, 0), T.P0[:, s0:s1], kr(c, 1), A.max, "P0%d KR%d" % (c, c), "K0%d" % c)
+
+        def diff(c, q):
+            s0, s1 = HALF[c]
+            bn = "bD%d" % (q & 1)
+            bd = T[bn]
+            e = CMPV[c][q]
+            for j in range(4):
+                mm(bd[:, :, j], T.NID[:], kr(c, 8 * q + 2 * j), "NID KR%d K0%d" % (c, c), bn, bn, True, False)
+                mm(bd[:, :, j], T.IDN[:], Z[:, s0:s1], "IDN " + zh[c], bn, bn, False, True)
+            name = "cmp%d%d" % (c, q)
+            if e == "S":
+                act(T.CMP[:, s0:s1, 4 * q:4 * q + 4], bd[:], F.Sign, bn + " half", name, bn, bias=cf(21))
+            else:
+                ts(T.CMP[:, s0:s1, 4 * q:4 * q + 4], bd[:], 0.0, 0.5, A.is_ge, A.subtract, bn, name, bn)
+            flush()
+            pend.append((c, q, e, name))
+
+        def flush():
+            for c, q, e, name in pend:
+                s0, s1 = HALF[c]
+                for k in range(4 * q + 3, 4 * q - 1, -1):
+                    mm(T.bM[:, s0:s1], slot(T.E0 if e == "S" else T.EH, k), T.CMP[:, s0:s1, k], "E0 EH " + name, "met%d" % c, "bM", k == 15, k == 0)
+            del pend[:]
+
+        def use(c):
+            s0, s1 = HALF[c]
+            for k in range(15, -1, -1):
+                up = kr(c, 2 * k + 2) if k < 15 else T.GB[:, s0:s1]
+                mm(T.bL[:, B + s0:B + s1], slot(T.E0, k), up, "E0 GB%d KR%d" % (c, c), "use%d" % c, "bL", k == 15, False)
+                mm(T.bL[:, B + s0:B + s1], slot(T.NE, k), kr(c, 2 * k + 1), "NE KR%d" % c, "use%d" % c, "bL", False, k == 0)
+
+        def zs():
+            act(T.MB[:], T.W37[:].indirect(ML[:]), F.Copy, "W37 " + mr, "MB")
+            mm(T.bO[:, 0:B], T.BW[:], Z[:], "BW " + zr, "uR", "bO")
+            mm(T.bO[:, B:2 * B], T.BW[:], Z[:], "BW " + zr, "xR", "bO", True, False)
+            mm(T.bO[:, B:2 * B], T.IDN[:], T.MB[:], "IDN MB", "xR", "bO", False, True)
+            mm(T.bF[:, 0:B], T.IDN[:], Z[:], "IDN " + zr, "d16", "bF", True, False)
+            mm(T.bF[:, 0:B], T.NID[:], T.GB[:], "NID GB0 GB1", "d16", "bF", False, True)
+            for r in range(16):
+                mm(L(0), slot(T.WE, r), Z[:, r::16], "WE " + zr, "uL", "bL", r == 0, r == 15)
+
+        def c16():
+            if t == 0:
+                zeros(1)
+            act(T.C16[:], T.bF[:, 0:B], F.Sign, "d16 half", "C16", "bF", bias=cf(21))
+            for r in range(16):
+                mm(L(16), slot(T.E0, r), T.C16[:, r::16], "E0 C16", "gL", "bL", r == 0, r == 15)
+            for h in range(2):
+                mm(T.bL[:, 32 + 8 * h:40 + 8 * h], T.C16[:, 128 * h:128 * h + 128], T.E0[:, 15:128:16], "E0 C16", "gT%d" % h, "bL")
+            mm(T.bF[:, B:2 * B], T.BO[:], T.C16[:], "BO C16", "gR", "bF")
+
+        def pairs(i):
+            bn = "bG%d" % (i & 1)
+            bg = T[bn]
+            if i < 4:
+                for h in range(2):
+                    mm(bg[:, :, 16 * h:16 * h + 16], T["BLO" if h else "BLE"][32 * i:32 * i + 32, 0:128], T.BR[32 * i:32 * i + 32, :], "BLE BLO BR", bn, bn)
+                act(T.EQ0[:, :, 32 * i:32 * i + 32], bg[:], F.Relu, bn + " bias0", "EQ0%d" % i, bn, bias=cf(19), scale=512.0)
+                return
+            two = (2 * (i - 4), 2 * (i - 4) + 1)
+            for q, a in enumerate(two):
+                if q:
+                    need("T", [("T", cnt["T"])])
+                for h in range(2):
+                    mm(bg[:, 8 * q:8 * q + 8, 16 * h:16 * h + 16], T["BLO" if h else "BLE"][32 * a:32 * a + 32, 128:256],
+                       T.BR[32 * a:32 * a + 32, 128:256], "BLE BLO BR", bn, bn)
+            for q, a in enumerate(two):
+                act(T.EQ1[:, :, 32 * a:32 * a + 32], bg[:, 8 * q:8 * q + 8, :], F.Relu, bn + " bias1", "EQ1%d" % a, bn, bias=cf(20), scale=512.0)
+
+        def ok(h):
+            s0, s1 = HALF[h]
+            ts(T.OK[:, s0:s1], T.bM[:, s0:s1], thdc, None, A.is_ge, None, "met%d %s" % (h, thd), "OK%d" % h, "bM")
+
+        def oh(h):
+            s0, s1 = HALF[h]
+            mm(T.bF[:, s0:s1], T.UP[:], T.OK[:, s0:s1], "UP OK%d C16" % h, "first%d" % h, "bF", True, False)
+            mm(T.bF[:, s0:s1], T.NEG[:], T.GREP[:, s0:s1], "NEG GREP", "first%d" % h, "bF", False, True)
+            ts(T.OH[:, s0:s1], T.bF[:, s0:s1], 1.0, None, A.is_ge, None, "first%d" % h, "OH%d" % h, "bF")
+
+        def vl(h):
+            s0, s1 = HALF[h]
+            o = T.bL[:, 64 + 8 * h:72 + 8 * h]
+            mm(o, T.IDN[:], T.B32[:], "IDN B32", "vl%d" % h, "bL", True, False)
+            for r in range(16):
+                mm(o, slot(T.WJ, r), T.OH[:, s0 + r:s1:16], "WJ OH%d" % h, "vl%d" % h, "bL", False, r == 15)
+            mm(T.bF[:, B + s0:B + s1], T.DT[:, 128 * t:128 * t + 128], T.OH[:, s0:s1], "DT OH%d GREP" % h, "de%d" % h, "bF")
+
+        def dl(h):
+            o = T.bL[:, 64 + 8 * h:72 + 8 * h]
+            tt(lh(1, h), o, T.SL[:, 0:8], A.not_equal, "vl%d b32f" % h, "any%d" % h, "bL")
+            ts(T.AOFF[:, 8 * h:8 * h + 8], o, 2.0, None, A.add, None, "vl%d" % h, "AOFF%d" % h, "bL")
+            tt(lh(2, h), lh(1, h), lh(0, h), A.mult, "any%d dm" % h, "mmx%d" % h)
+            tt(lh(3, h), lh(2, h), T.LI[:, 48 + 8 * h:56 + 8 * h], A.add, "mmx%d to" % h, "mn%d" % h)
+
+        def sm(h):
+            if not last:
+                c0, c1 = 8 * h, 8 * h + 8
+                tc(T["MO%d" % (t + 1)][:, c0:c1], lh(3, h), "mn%d" % h, "MO%d" % h)
+                send("ML", t + 1, h, c0, c1, T["MO%d" % (t + 1)], "MO%d" % h)
+            elif h:
+                dma("Y", T.ym[:], lf(3), "o_ym", "mn0 mn1", "")
+
+        def t1(h):
+            s0, s1 = HALF[h]
+            tt(T.T1[:, s0:s1], T.D0[:, 32 * s0:32 * s1].indirect(T.AOFF[:, 8 * h:8 * h + 8]), Z[:, s0:s1], A.subtract,
+               "AOFF%d d0a%d d0z%d %s" % (h, h, h, zh[h]), "T1%d" % h)
+
+        def t2(h):
+            s0, s1 = HALF[h]
+            act(T.T2[:, s0:s1], T.T1[:, s0:s1], F.Relu, "T1%d c255" % h, "T2%d" % h, bias=cf(22))
+
+        def t3(h):
+            s0, s1 = HALF[h]
+            tt(T.T3[:, s0:s1], T.T2[:, s0:s1], T.bF[:, B + s0:B + s1], A.add, "T2%d de%d" % (h, h), "T3%d" % h, "bF")
+
+        def sz(h):
+            s0, s1 = HALF[h]
+            out = T.ZF if last else T["ZO%d" % (t + 1)]
+            act(out[:, s0:s1], T.T3[:, s0:s1], F.Abs, "T3%d cm255" % h, "ZO%d" % h, bias=cf(23))
+            if last:
+                dma("Y", T.yz[:, s0:s1], out[:, s0:s1], "o_yz%d" % h, "ZO%d" % h, "")
+            else:
+                send("Z", t + 1, h, s0, s1, out, "ZO%d" % h)
+
+        def conf():
+            e0 = " ".join("EQ0%d" % a for a in range(4))
+            e1 = " ".join("EQ1%d" % a for a in range(4))
+            for c in range(16):
+                o = T.bL[:, 128 + 8 * c:136 + 8 * c]
+                mm(o, T.EQ0[:, c, :], T.GLT[:, 16:24], "GLT " + e0, "CT", "bL", True, c < 8)
+                if c >= 8:
+                    mm(o, T.EQ1[:, c - 8, :], T.GLT[:, 24:32], "GLT " + e1, "CT", "bL", False, True)
+
+        def asum():
+            if not last:
+                for j in range(16):
+                    mm(T.bL[:, 80:81], T.ONE[:], T.GLT[:, j:j + 1], "ONE GLT", "as0", "bL", j == 0, j == 15)
+
+        def par():
+            if not last:
+                tc(T.AI[:, 0:1], T.bL[:, 80:81], "as0", "as2", "bL")
+                ts(T.AI[:, 1:2], T.AI[:, 0:1], 1, None, A.bitwise_and, None, "as2", "as3")
+                ts(T.THR[:, t + 1:t + 2], T.AI[:, 1:2], 2.0, float(2 * QU - 16), A.mult, A.add, "as3", "thd%d" % (t + 1))
+                ts(T.THR[:, t + 5:t + 6], T.AI[:, 1:2], -2.0, 17.0 - 2 * QU, A.mult, A.add, "as3", "thb%d" % (t + 1))
+
+        def cx():
+            op("V", lambda: V.tensor_tensor_scan(T.CX[:], T.DX[:], T.bL[:, 128:256], 0.0, A.add, A.max), "DX CT", "CX", "bL")
+            ts(lf(6), T.CX[:, 7::8], cf(18), None, A.is_le, None, "CX nb", "free")
+            tt(lf(7), lf(6), lf(5), A.mult, "free gd", "w2")
+            tt(lf(8), lf(7), T.SL[:, 16:32], A.add, "w2 b512", "off")
+            tc(T.OFF[:], lf(8), "off", "OFF")
+
+        def ml():
+            tc(li(0), ML[:], mr, "mI")
+            ts(li(1), li(0), 37.0, None, A.mult, None, "mI", "m37")
+            if t == 0:
+                later_const()
+
+        def toL():
+            tt(li(2), L(0), li(1), A.add, "uL m37", "to0", "bL")
+            ts(li(3), li(2), M - 1, None, A.bitwise_and, None, "to0", "to")
+            tt(lf(0), li(0), li(3), A.subtract, "mI to", "dm")
+
+        def td():
+            tt(lf(4), li(3), T.SL[:, 16:32], A.subtract, "to b512", "td")
+            tt(lf(5), lf(4), T.GLT[:, 0:16], A.mult, "td GLT", "gd")
+
+        def oP():
+            act(T.bO[:, 0:B], T.OF[:], F.Copy, "OF UI", "oP", "bO")
+            act(T.bO[:, B:2 * B], T.OF[:], F.Identity, "OF XQ c1184", "oK", "bO", bias=cf(16), scale=32.0)
+
+        one = {
+            "of": lambda: tc(T.OF[:], T.O16[:], "O160 O161", "OF"),
+            "ui": lambda: tc(T.UI[:], T.bO[:, 0:B], "uR", "UI", "bO"),
+            "uu": lambda: ts(T.UU[:], T.UI[:], W - 1, None, A.bitwise_and, None, "UI", "UU"),
+            "xq": lambda: ts(T.XQ[:], T.bO[:, B:2 * B], cf(15), cf(5), A.mult, A.add, "xR cb cb2", "XQ", "bO"),
+            "bit": lambda: ts(T.BIT[:], T.XQ[:], 1, None, A.bitwise_and, None, "XQ", "BIT"),
+            "br": lambda: tt(T.BR[:], T.BIT[:], T.bM[:, B:2 * B], A.add, "BIT CONST", "BR", "bM"),
+            "ble": lambda: ts(T.BLE[:], T.BIT[:], cf(8), cf(9), A.mult, A.add, "BIT e1 e2", "BLE"),
+            "blo": lambda: ts(T.BLO[:], T.BIT[:], cf(10), cf(11), A.mult, A.add, "BIT o1 o2", "BLO"),
+            "glt": lambda: ts(T.GLT[:], T.bL[:, 16:48], thdc, None, A.is_ge, None, "gL gT0 gT1 " + thd, "GLT", "bL"),
+            "grep": lambda: act(T.GREP[:], T.bF[:, B:2 * B], F.Sign, "gR thb%d" % t, "GREP", "bF", bias=T.THR[:, 4 + t:5 + t]),
+            "fq": lambda: tt(T.FQ[:], T.bO[:, 0:B], T.UU[:], A.mult, "oP UU", "FQ", "bO"),
+            "ft": lambda: tt(T.FT[:], T.FQ[:], T.bO[:, B:2 * B], A.add, "FQ oK", "FT", "bO"),
+            "fr": lambda: ts(T.FR[:], T.FT[:], 5, W - 1, A.arith_shift_right, A.bitwise_and, "FT", "FR"),
+            "df": lambda: tt(T.DF[:], T.FR[:], T.bO[:, 0:B], A.subtract, "FR oP", "DF", "bO"),
+            "low": lambda: ts(T.bO[:, B:2 * B], T.bL[:, B:2 * B], float(TH), None, A.is_lt, None, "use0 use1", "oK", "bL bO"),
+            "ldf": lambda: tt(T.LDF[:], T.bO[:, B:2 * B], T.DF[:], A.mult, "oK DF", "LDF", "bO"),
+            "wr": lambda: tt(T.MC[:, 0:M + B].indirect(T.OFF[:]), T.LDF[:], T.OF[:], A.add, "LDF OF OFF", "MC"),
+            "ml": ml, "zs": zs, "c16": c16, "toL": toL, "oP": oP, "conf": conf, "td": td, "cx": cx, "as": asum, "par": par, "fl": flush}
+        per = {"o16": o16, "GB": GB, "ad": ad, "prs": prs, "prv": prv_, "gw": gw, "scan": scan, "use": use, "ok": ok, "oh": oh, "vl": vl, "dl": dl,
+               "sm": sm, "t1": t1, "t2": t2, "t3": t3, "sz": sz}
+
+        def run(x):
+            a, _, b = x.partition(":")
+            if a in per:
+                per[a](int(b))
+            elif b:
+                diff(int(a[1:]), int(b))
+            elif a in one:
+                one[a]()
+            else:
+                pairs(int(a[1:]))
+            if t == 0 and x == "grep":
+                passes()
+        return run
+
+    runs = [step(t) for t in range(T_STEPS)]
+    for x in ORDER:
+        if x[0] == "+":
+            runs[0](x[1:])
+    for t in range(T_STEPS):
+        for x in ORDER:
+            if x[0] != "+":
+                runs[t](x)
+            elif t + 1 < T_STEPS:
+                runs[t + 1](x[1:])
+    dma("Y", T.ymc[:], T.MC[:, 0:M], "o_ymc", "MC", "")
+    need("G", [(s, cnt[s]) for s in ("V", "S", "T", "G")])
+    need("G", [("l_" + x, 16) for x in LOADS] + [("o_" + x, 16) for x in OUTS])
+    for t in range(1, T_STEPS):
+        for h in range(2):
+            for b in "mz":
+                need("G", [("r%s%d%d" % (b, t, h), len(eng(prv, core))), ("s%s%d%d" % (b, t, h), len(eng(core, nxt)))])

@@ -3,29 +3,30 @@ A = AluOpType
 F = ActivationFunctionType
 
 T_STEPS, W, M, B, QU, TH = 4, 2048, 512, 256, 12, 254
-BIG = 131072.0
-HALF = [(0, 128), (128, 256)]
-VPR = [32, 16]
-CMPV = ["VVVS", "SSSS"]
-ORDER = ("ml o16:1 prs:0 GB:1 zs c16 prs:1 prv:0 gw:0 scan:0 prv:1 xq of bit br ble use:0 grep ui d0:3 toL d0:2 glt d0:1 d0:0 ad:1 blo fl "
-         "ok:0 p0 gw:1 oh:0 p1 scan:1 vl:0 p2 dl:0 p3 p4 sm:0 oP p5 uu fq d1:3 ft fr td t1:0 df use:1 conf t2:0 low ldf cx d1:2 t3:0 wr "
-         "d1:1 d1:0 fl +o16:0 ok:1 oh:1 vl:1 dl:1 sz:0 sm:1 +ad:0 t1:1 as t2:1 par t3:1 +GB:0 sz:1").split()
+QS_ = 64
+CMPV = "VVVS"
+RATIO = 3.2
+LPC = 896
+P0B = "bL"
+ORDER = ("k0:12 use:12 ad:23 to0 to gr p0:23 grep cl:12 pr:34 ui dm ad:34 met:01 of:24 u xu met:12 #8 fq ok:02 tof use:01 gw:23 g first:02 oh:02 scan:23 zp:23 as +#1 p0:34 gw:34 vl:02 any:02 use:23 gm code ai ms:02 k0:23 mo:02 xh:1 xh:0 scan:34 cl:23 xl:0 use:34 hh:0 k0:34 zm sm:02 hs:0 ch:23 lw:0 tm:0 n0:34 xl:1 hh:1 ao:02 lw:1 n0:03 hs:1 ch:34 tm:1 nn:03 cl:34 t1:02 met:23 nn:34 +gb:02 rec ap rt rm ok:23 off nb mc zz:02 ab:02 met:34 ok:34 +o16:02 +#3 first:24 oh:24 vl:24 sz:02 ao:24 +ad:01 +#5 +pr:01 any:24 t1:24 +#7 ms:24 zz:24 ab:24 +#2 +#4 +#9 +zp:01 +pr:12 +of:02 +ad:12 +p0:01 +zp:12 +#6 mo:24 +p0:12 sm:24 +gw:01 +scan:01 +k0:01 +ch:01 +gw:12 +o16:24 sz:24 +mi +scan:12 +cl:01 +gb:24 +m37 +pr:23 +d16 +ul +ch:12 +c16").split()
+SENDS = [(0, 2), (2, 4)]
 SB, PS = "sbuf", "psum"
-BF, F4, I4, U2 = "bfloat16", "float32", "int32", "uint16"
-SCRATCH = {"CMP": (SB, [128, B, 16], BF), "EQ0": (SB, [128, 16, 128], BF), "EQ1": (SB, [128, 8, 128], BF),
-           "bD0": (PS, [128, 128, 4], F4), "bD1": (PS, [128, 128, 4], F4), "bG0": (PS, [128, 16, 32], F4), "bG1": (PS, [128, 16, 32], F4)}
-for _n, _w, _d in ([(x, 512, F4) for x in ("bM", "bL", "bF", "bO")]
-                   + [("PRW", W, BF), ("ADW", W, BF), ("GLW", M, BF), ("MCI", M, I4), ("MC", M + B, F4), ("WI", M, I4), ("WJI", M, I4), ("W37", M, BF),
-                      ("M0", 16, I4), ("DV", 4, BF), ("WT", 1, BF), ("O16", B, U2), ("D0", 32 * B, BF), ("D1", 32 * B, BF), ("KR", 32 * B, BF),
-                      ("AOFF", 16, U2), ("OFF", 16, U2), ("GLT", 32, BF), ("CX", 128, F4), ("LI", 64, I4), ("LF", 144, F4), ("CI", 4, I4),
-                      ("CF", 24, F4), ("THR", 8, F4), ("AI", 2, I4), ("DG", 512, BF), ("DT", 512, BF), ("IOT", B, F4), ("TB", 64, F4), ("SL", 48, F4), ("B32", 8, BF)]
-                   + [(x, 144, BF) for x in ("E1", "E2", "E0", "EH", "NE", "WE", "WJ")]
-                   + [(x, B, BF) for x in ("GB", "MB", "C16", "P0", "BLE", "BLO", "BR", "GREP", "OK", "OH")]
-                   + [(x, B, I4) for x in ("UI", "UU", "FQ", "FT", "FR", "XQ", "BIT")]
-                   + [(x, B, F4) for x in ("OF", "DF", "LDF", "T1", "T2", "T3", "ZF")]
-                   + [(x, 128, F4) for x in ("DX1", "DX2", "DX")]
-                   + [(x, 128, BF) for x in ("ONE", "BO1", "BO", "IDN", "NID", "NBO", "U1", "UP", "NEG", "BW")]):
-    SCRATCH[_n] = (PS if _n in ("bM", "bL", "bF", "bO") else SB, [128, _w], _d)
+BF, F4, I4, U2, H2 = "bfloat16", "float32", "int32", "uint16", "float16"
+SCRATCH = {"CMP": (SB, [128, 16 * B], BF), "HH": (SB, [128, 8, 64], BF), "bC0": (PS, [128, 512], F4), "bC1": (PS, [128, 512], F4),
+           "bX": (PS, [128, 16, 32], F4), "KR": (SB, [128, 32 * B], BF)}
+for _n, _w, _d in ([(x, 512, F4) for x in ("bM", "bL", "bF", "bU", "bG")]
+                   + [("PRW", W, BF), ("ADW", W, BF), ("GLW", M, BF), ("W0", M + B, I4), ("W1", M + B, I4), ("YM", M, F4), ("UT", W, F4),
+                      ("WI", M, I4), ("XQ", M, I4), ("BIT", M, I4), ("CT", M, BF), ("LP", 2048, BF), ("RH", B, BF),
+                      ("M0", 16, I4), ("DV", 4, BF), ("WT", 1, BF), ("O16", B, U2), ("OF", B, H2), ("I16", 128, H2), ("D0", 32 * B, BF), ("D1", 32 * B, BF),
+                      ("AOFF", 16, U2), ("OFF", 32, U2), ("XU", 32, U2), ("XI", 32, I4), ("LI", 80, I4), ("LF", 48, F4), ("DM", 32, F4), ("MN", 32, F4),
+                      ("RC", 64, F4), ("RT", 64, F4), ("CI", 4, I4), ("CF", 32, F4), ("NB", 4, F4), ("AC", 4, F4), ("AI", 2, I4), ("DG", 512, BF), ("DT", 512, BF),
+                      ("IOT", 8, F4), ("WS", 512, BF), ("B32", 8, BF), ("CB", 2, BF), ("SR1", 64, BF), ("SR2", 64, BF), ("HB", QS_, BF), ("O32", 128, F4)]
+                   + [(x, 144, BF) for x in ("E1", "E2", "E0", "EH", "EK", "ER", "WE", "WJ")]
+                   + [(x, B, BF) for x in ("GB", "C16", "CD", "GREP", "OK", "OH", "ZM", "T1")]
+                   + [(x, B, I4) for x in ("GI", "GM", "N0")]
+                   + [(x, B, F4) for x in ("FQ", "ZF")]
+                   + [(x, 128, BF) for x in ("ONE", "BO1", "BO", "IDN", "NID", "NBO", "U1", "UP", "NEG", "EI", "RL", "RG", "RG1", "S16")]):
+    SCRATCH[_n] = (PS if _n in ("bM", "bL", "bF", "bU", "bG") else SB, [128, _w], _d)
 LOADS = ["m0", "mc", "z0", "gl", "wt", "dv", "pr", "ad"]
 OUTS = ["ymc", "yz0", "yz1", "ym"]
 SEMAPHORES = ["V", "S", "T", "G"] + ["l_" + n for n in LOADS] + ["o_" + n for n in OUTS]
@@ -35,7 +36,7 @@ for _t in range(T_STEPS):
     if _t:
         SCRATCH["ZO%d" % _t] = (SB, [128, B], BF)
         SCRATCH["MO%d" % _t] = (SB, [128, 16], U2)
-        SEMAPHORES += ["%s%s%d%d" % (a, b, _t, h) for a in "rs" for b in "mz" for h in (0, 1)]
+        SEMAPHORES += ["%s%s%d%d" % (a, b, _t, q[0]) for a in "rs" for b in "mz" for q in SENDS]
 
 
 def rank_program(g, core, T, topo):
@@ -96,14 +97,16 @@ def rank_program(g, core, T, topo):
         mark((sem, 16), r, w, [])
 
     eng = lambda a, b: topo.engines(a, b)[:8]
+    N = lambda x, a, b: " ".join("%s_%d" % (x, q) for q in range(a, b))
 
-    def send(buf, t, h, c0, c1, src, r):
+    def send(buf, t, a, b, c0, c1, src, r):
         rid, pid = topo.addr(nxt, core)
-        deps("G", [r], [], [])
-        k = ("m" if buf == "ML" else "z") + "%d%d" % (t, h)
+        deps("G", r.split(), [], [])
+        k = ("m" if buf == "ML" else "z") + "%d%d" % (t, a)
         g.remote_dma(T[buf + str(t)][:, c0:c1], src[:, c0:c1], T.sem["r" + k], T.sem["s" + k], pid, rid, sum(1 << e for e in eng(core, nxt)))
-        mark(("s" + k, len(eng(core, nxt))), [r], [], [])
-        wrote["%s%d_%d" % (buf, t, h)] = ("r" + k, len(eng(prv, core)))
+        mark(("s" + k, len(eng(core, nxt))), r.split(), [], [])
+        for x in N("%s%d" % (buf, t), a, b).split():
+            wrote[x] = ("r" + k, len(eng(prv, core)))
 
     def mm(out, l, rr, r, w, b, st=True, sp=True):
         op("T", lambda: P.matmul(out, l, rr, st, sp), r, w, b)
@@ -120,8 +123,11 @@ def rank_program(g, core, T, topo):
     def tc(out, a, r, w, b=""):
         op("V", lambda: V.tensor_copy(out, a), r, w, b)
 
-    def ms(out, c, w):
-        op("V", lambda: V.memset(out, c), "", w)
+    def ms(out, c, w, b=""):
+        op("V", lambda: V.memset(out, c), "", w, b)
+
+    def sc(out, a, c, init, o0, o1, r, w, b=""):
+        op("V", lambda: V.tensor_tensor_scan(out, a, c, init, o0, o1), r, w, b)
 
     def act(out, a, f, r, w, b="", **kw):
         op("S", lambda: S.activation(out, a, f, **kw), r, w, b)
@@ -129,366 +135,348 @@ def rank_program(g, core, T, topo):
     def aff(o, i, pat, cmp, fill, base, cm, r, w):
         op("G", lambda: g.affine_select(o[:], i[:], pat, cmp, fill, base, cm), r, w)
 
+    def iota(o, pat, base, cm, w):
+        op("G", lambda: g.iota(o, pat, base, cm, allow_small_or_imprecise_dtypes=True), "", w)
+
     def slot(pad, k):
         return pad[:, 15 - k:143 - k]
 
     cf = lambda i: T.CF[:, i:i + 1]
-    li = lambda i: T.LI[:, 16 * i:16 * i + 16]
-    lf = lambda i: T.LF[:, 16 * i:16 * i + 16]
-    lh = lambda i, h: T.LF[:, 16 * i + 8 * h:16 * i + 8 * h + 8]
-    L = lambda i: T.bL[:, i:i + 16]
+    own = lambda j: T.E0[:, 15 + 16 * j:16 + 16 * j]
+    span = lambda a, b, i, st: slice(32 * QS_ * a + i, 32 * QS_ * b, st)
 
     dma("Y", T.M0[:], T.m0[:], "l_m0", "", "M0")
-    dma("Y", T.MCI[:], T.mc[:], "l_mc", "", "MCI")
-    dma("S", T.GLW[:], T.gl[:], "l_gl", "", "GLW")
+    dma("Y", T.W0[:, B:B + M], T.mc[:], "l_mc", "", "MC0")
     dma("S", T.ADW[:], T.ad[:], "l_ad", "", "ADW")
+    dma("S", T.GLW[:], T.gl[:], "l_gl", "", "GLW")
     dma("Y", T.PRW[:], T.pr[:], "l_pr", "", "PRW")
-    dma("Y", T.Z0[:], T.z0[:], "l_z0", "", "Z0_0 Z0_1")
+    dma("Y", T.Z0[:], T.z0[:], "l_z0", "", N("Z0", 0, 4))
     dma("Y", T.WT[:], T.wt[:], "l_wt", "", "WT")
     dma("Y", T.DV[:], T.dv[:], "l_dv", "", "DV")
 
+    ms(T.LP[:], 0.0, "LP")
     ms(T.ONE[:], 1.0, "ONE")
     ms(T.E1[:], 0.0, "E1")
+    ms(T.S16[:], 0.0625, "S16")
     ms(T.E1[:, 15::16], 1.0, "E1")
+    op("G", lambda: g.iota(T.WI[:], [[1, M]], 0, 0), "", "WI")
     op("G", lambda: g.iota(T.CI[:, 0:1], [[0, 1]], 0, 1), "", "pc")
-    op("G", lambda: g.iota(T.IOT[:], [[1, B]], 0, 0, allow_small_or_imprecise_dtypes=True), "", "IOT")
-    aff(T.E2, T.E1, [[-16, 9], [0, 16]], A.is_ge, 0.0, 0, 1, "E1", "E2")
-    aff(T.E0, T.E2, [[16, 9], [0, 16]], A.is_ge, 0.0, 15, -1, "E2", "E0")
-    aff(T.BO1, T.ONE, [[-16, 8], [0, 16]], A.is_ge, 0.0, 0, 1, "ONE", "BO1")
-    aff(T.BO, T.BO1, [[16, 8], [0, 16]], A.is_ge, 0.0, 15, -1, "BO1", "BO")
     aff(T.IDN, T.ONE, [[-1, 128]], A.is_equal, 0.0, 0, 1, "ONE", "IDN")
-    op("G", lambda: g.iota(T.WI[:], [[37, M]], 0, 0), "", "WI")
-    ts(T.CI[:, 1:2], T.CI[:, 0:1], 15, None, A.bitwise_and, None, "pc", "kc")
-    ts(T.CI[:, 2:3], T.CI[:, 0:1], 4, None, A.arith_shift_right, None, "pc", "gc")
-    ts(T.CI[:, 3:4], T.CI[:, 0:1], 4, 1, A.arith_shift_right, A.bitwise_and, "pc", "oc")
-    ms(T.TB[:, 0:16], 0.5, "tba")
-    ms(T.TB[:, 16:32], 0.0, "tbb")
-    tc(cf(0), T.CI[:, 1:2], "kc", "kf")
-    tc(cf(1), T.CI[:, 2:3], "gc", "gf")
-    tc(cf(2), T.CI[:, 3:4], "oc", "odd")
-    tc(cf(3), T.CI[:, 0:1], "pc", "pf")
-    op("V", lambda: V.tensor_tensor_scan(T.TB[:, 32:48], T.TB[:, 0:16], T.TB[:, 16:32], 2.0, A.mult, A.add), "tba tbb", "tbc")
-    ts(cf(5), cf(0), 8.5, None, A.is_le, None, "kf", "le8")
-    ts(cf(6), cf(0), 9.0, None, A.is_equal, None, "kf", "is9")
-    ts(T.TB[:, 48:64], T.IOT[:, 0:16], cf(0), None, A.is_equal, None, "IOT kf", "tbm")
-    ts(cf(4), cf(2), -1.0, 1.0, A.mult, A.add, "odd", "even")
-    ts(cf(7), cf(5), -0.5, cf(6), A.mult, A.add, "le8 is9", "base")
-    ts(cf(12), cf(6), 2.0 ** -9, None, A.mult, None, "is9", "c9")
-    ts(cf(13), cf(5), -0.5, None, A.mult, None, "le8", "nle8")
-    tt(T.TB[:, 0:16], T.TB[:, 32:48], T.TB[:, 48:64], A.mult, "tbc tbm", "tba")
+    aff(T.E2, T.E1, [[-16, 9], [0, 16]], A.is_ge, 0.0, 0, 1, "E1", "E2")
+    aff(T.BO1, T.ONE, [[-16, 8], [0, 16]], A.is_ge, 0.0, 0, 1, "ONE", "BO1")
+    aff(T.E0, T.E2, [[16, 9], [0, 16]], A.is_ge, 0.0, 15, -1, "E2", "E0")
+    aff(T.BO, T.BO1, [[16, 8], [0, 16]], A.is_ge, 0.0, 15, -1, "BO1", "BO")
+    iota(T.IOT[:], [[16, 8]], 0, 0, "IOT")
+    act(T.D1[:, span(0, 2, 1, 2)], T.LP[:], F.Copy, "LP", N("d1z", 0, 2))
+    act(T.D1[:, span(2, 4, 1, 2)], T.LP[:], F.Copy, "LP", N("d1z", 2, 4))
+    ms(T.D0[:, span(0, 2, 0, 2)], 0.0, N("d0z", 0, 2))
+    ms(T.WS[:, 0:128], 1.0 / RATIO, "wsa")
+    ms(cf(25), 2.0 ** 57, "big")
+    ms(cf(26), 2.0 ** -57, "tiny")
+    ms(T.D0[:, span(0, 2, 0, 32)], -512.0, N("d0z", 0, 2))
+    ts(T.WS[:, 128:256], T.E1[:, 15:143], -0.5, 0.5, A.mult, A.add, "E1", "wsb")
+    ts(cf(23), cf(25), RATIO * 2.0 ** 56, None, A.mult, None, "big", "top")
+    tc(T.ML0[:], T.M0[:], "M0", N("ML0", 0, 4))
 
-    def zeros(c):
-        lo, hi = 32 * HALF[c][0], 32 * HALF[c][1]
-        ms(T.D0[:, lo:hi:2], 0.0, "d0z%d" % c)
-        ms(T.D0[:, lo:hi:32], -512.0, "d0z%d" % c)
-        if c:
-            ms(T.D1[:, lo + 1:hi:2], 0.0, "d1z%d" % c)
-        else:
-            act(T.D1[:, lo + 1:hi:2], T.D0[:, lo:hi:2], F.Copy, "d0z0", "d1z0", scale=0.0)
-
-    zeros(0)
-    ms(cf(21), 0.5, "half")
-    ms(cf(22), 255.0, "c255")
-    ms(cf(23), -255.0, "cm255")
-    ms(T.THR[:, 0:1], float(2 * QU - 16), "thd0")
-    ms(T.THR[:, 4:5], 17.0 - 2 * QU, "thb0")
-    op("V", lambda: V.tensor_reduce(cf(14), T.TB[:, 0:16], AxisListType.X, A.add), "tba", "cb0")
-    ts(cf(8), cf(5), cf(4), None, A.mult, None, "le8 even", "e1")
-    ts(cf(9), cf(7), cf(4), None, A.mult, None, "base even", "e2")
-    ts(cf(10), cf(5), cf(2), None, A.mult, None, "le8 odd", "o1")
-    ts(cf(11), cf(7), cf(2), None, A.mult, None, "base odd", "o2")
-    ts(cf(15), cf(14), cf(5), None, A.mult, None, "cb0 le8", "cb")
-    ts(cf(5), cf(14), 0.5, -0.5, A.mult, A.add, "cb0 cb", "cb2 le8")
-    ts(cf(17), cf(0), 2.0, -1.0, A.mult, A.add, "kf", "cj")
-    tc(T.ML0[:], T.M0[:], "M0", "ML0_0 ML0_1")
-    ms(T.MC[:, M:M + B], 0.0, "MC")
-    tc(T.MC[:, 0:M], T.MCI[:], "MCI", "MC")
-
-    def later_const():
-        ts(T.NID[:], T.IDN[:], -1.0, None, A.mult, None, "IDN", "NID")
-        ts(T.BW[:], T.BO[:], T.WT[:, 0:1], None, A.mult, None, "BO WT", "BW")
-        ts(T.WE[:], T.E0[:], T.WT[:, 0:1], None, A.mult, None, "E0 WT", "WE")
-        ts(T.WJI[:], T.WI[:], M - 1, None, A.bitwise_and, None, "WI", "WJI")
-        ts(T.W37[:], T.WJI[:], -256.0, None, A.add, None, "WJI", "W37")
-        ts(T.bM[:, B:2 * B], T.IOT[:], cf(12), cf(13), A.mult, A.add, "IOT c9 nle8", "CONST", "bM")
-        ts(cf(16), cf(0), 1184.0, None, A.mult, None, "kf", "c1184")
-        ts(cf(18), cf(1), -BIG, 7 * BIG + 0.5, A.mult, A.add, "gf", "nb")
-        ts(cf(19), cf(3), -1.0, -1152.0, A.mult, A.add, "pf", "bias0")
-        ts(cf(20), cf(3), -1.0, -1280.0, A.mult, A.add, "pf", "bias1")
-        ts(T.SL[:, 32:48], T.IOT[:, 0:16], 16.0, cf(0), A.mult, A.add, "IOT kf", "sl")
-        ms(T.DX1[:], -16.0 * BIG, "DX1")
-        ts(T.NBO[:], T.BO[:], -1.0, None, A.mult, None, "BO", "NBO")
-        ts(T.NEG[:], T.BO[:], -0.03125, None, A.mult, None, "BO", "NEG")
-        ts(T.NE[:], T.E0[:], -1.0, None, A.mult, None, "E0", "NE")
-        ts(T.EH[:], T.E0[:], 2.0, None, A.mult, None, "E0", "EH")
-        ts(T.WJ[:], T.E0[:], cf(17), None, A.mult, None, "E0 cj", "WJ")
-        ts(T.SL[:, 0:16], T.SL[:, 32:48], 32.0, None, A.mult, None, "sl", "b32f")
-        ts(T.SL[:, 16:32], T.SL[:, 32:48], float(M), None, A.add, None, "sl", "b512")
-        tc(T.B32[:], T.SL[:, 0:8], "b32f", "B32")
-        aff(T.U1, T.NBO, [[-1, 128]], A.not_equal, 1.0, 0, 1, "NBO", "U1")
-        aff(T.UP, T.U1, [[-1, 128]], A.is_ge, 0.0, 0, 1, "U1", "UP")
-        aff(T.DX2, T.DX1, [[0, 16], [-16, 8]], A.is_ge, BIG, 0, 1, "DX1", "DX2")
-        aff(T.DX, T.DX2, [[0, 16], [16, 8]], A.is_ge, BIG, 15, -1, "DX2", "DX")
-
-    def passes():
-        for t in range(T_STEPS):
-            ts(T.DG[:, 128 * t:128 * t + 128], T.IDN[:], T.DV[:, t:t + 1], None, A.mult, None, "IDN DV", "DG%d" % t)
-        mm(T.bF[:], T.BO[:], T.DG[:], "BO DG0 DG1 DG2 DG3", "dtp", "bF")
-        tc(T.DT[:], T.bF[:], "dtp", "DT", "bF")
+    def const(i):
+        if i == 1:
+            sc(T.WS[:, 256:384], T.WS[:, 0:128], T.LP[:, 0:128], cf(23), A.mult, A.add, "wsa LP top", "wsc")
+            sc(T.WS[:, 384:512], T.WS[:, 128:256], T.E1[:, 15:143], 0.0, A.mult, A.add, "wsb E1", "wsd")
+            ts(T.CI[:, 1:2], T.CI[:, 0:1], 15, None, A.bitwise_and, None, "pc", "kc")
+            tc(cf(3), T.CI[:, 0:1], "pc", "pf")
+            mm(T.bG[:, 0:1], T.WS[:, 256:384], T.IDN[:, 0:1], "wsc IDN", "d16", "bG")
+            mm(T.bG[:, 1:2], T.WS[:, 384:512], T.IDN[:, 0:1], "wsd IDN", "d16", "bG")
+            tc(cf(0), T.CI[:, 1:2], "kc", "kf")
+            tc(T.CF[:, 10:12], T.bG[:, 0:2], "d16", "wcol cb", "bG")
+            for q in (2, 3):
+                iota(T.D0[:, span(q, q + 1, 0, 2)], [[0, 16 * QS_]], 0, 0, N("d0z", q, q + 1))
+                iota(T.D0[:, span(q, q + 1, 0, 32)], [[0, QS_]], -512, 0, N("d0z", q, q + 1))
+                if q == 2:
+                    ts(T.NBO[:], T.BO[:], -1.0, None, A.mult, None, "BO", "NBO")
+                    aff(T.RG1, T.S16, [[0, 16], [-16, 8]], A.is_ge, 0.0, 0, 1, "S16", "RG1")
+                    aff(T.U1, T.NBO, [[-1, 128]], A.not_equal, 1.0, 0, 1, "NBO", "U1")
+                    aff(T.RG, T.RG1, [[0, 16], [16, 8]], A.is_ge, 0.0, 15, -1, "RG1", "RG")
+                    aff(T.UP, T.U1, [[-1, 128]], A.is_ge, 0.0, 0, 1, "U1", "UP")
+                    iota(T.SR1[:, 32:64], [[16, 32]], B, 0, "SR1b")
+            iota(T.UT[:], [[1, W]], 32, 0, "UT")
+        if i == 2:
+            ts(T.EH[:], T.E0[:], 2.0, None, A.mult, None, "E0", "EH")
+            ts(T.EK[:], T.E0[:], -4096.0, None, A.mult, None, "E0", "EK")
+            ts(T.ER[:], T.E0[:], 4096.0, None, A.mult, None, "E0", "ER")
+            tc(T.I16[:], T.IDN[:], "IDN", "I16")
+            ms(T.HB[0:64, :], 8192.0, "HB0")
+            ms(T.HB[64:128, :], (TH - 0.5) * 64.0 - 8192.0, "HB1")
+        if i == 3:
+            ts(cf(15), cf(11), 0.5, -0.5, A.mult, A.add, "cb", "cb2")
+            ts(T.CB[:, 0:1], cf(0), 3.5, None, A.is_le, None, "kf", "le3")
+            ts(T.XQ[:], T.WI[:], cf(11), cf(15), A.mult, A.add, "WI cb cb2", "XQ")
+            ts(T.CB[:, 1:2], cf(0), 3.5, None, A.is_ge, None, "kf", "ge4")
+            ts(T.BIT[:], T.XQ[:], 1, None, A.bitwise_and, None, "XQ", "BIT")
+            ts(cf(12), cf(10), -4.0, None, A.mult, None, "wcol", "wbias")
+            ts(T.CT[:], T.BIT[:], 2.0, -1.0, A.mult, A.add, "BIT", "CT")
+        if i == 4:
+            ts(T.NID[:], T.IDN[:], -1.0, None, A.mult, None, "IDN", "NID")
+            ts(T.WE[:], T.E0[:], T.WT[:, 0:1], None, A.mult, None, "E0 WT", "WE")
+            ms(cf(21), 0.5, "half")
+            ms(T.NB[:, 0:1], 17.0 - 2 * QU, "nb0")
+        if i == 5:
+            ts(cf(17), cf(0), 2.0, -1.0, A.mult, A.add, "kf", "cj")
+            ts(T.LF[:, 32:40], T.IOT[:], cf(0), None, A.add, None, "IOT kf", "sl")
+            ts(T.NEG[:], T.BO[:], -0.03125, None, A.mult, None, "BO", "NEG")
+            ts(T.WJ[:], T.E0[:], cf(17), None, A.mult, None, "E0 cj", "WJ")
+            ts(T.B32[:], T.LF[:, 32:40], 32.0, None, A.mult, None, "sl", "B32")
+            ms(T.bL[:, 32:64], 0.0, N("any", 0, 4), "bL")
+        if i == 6:
+            for t in range(T_STEPS):
+                ts(T.DG[:, 128 * t:128 * t + 128], T.IDN[:], T.DV[:, t:t + 1], None, A.mult, None, "IDN DV", "DG%d" % t)
+            mm(T.bF[:], T.BO[:], T.DG[:], "BO DG0 DG1 DG2 DG3", "xl " + N("zz", 0, 4), "bF")
+            act(T.DT[:], T.bF[:], F.Copy, "xl", "DT", "bF")
+        if i == 7:
+            for j in range(8):
+                ts(T.RL[:, j::8], T.CT[:, 0:16], own(j), T.CB[:, 0:1], A.mult, A.mult, "CT E0 le3", "RL%d" % j)
+        if i == 8:
+            for j in range(8):
+                ts(T.RH[:, 32 * j:32 * j + 32], T.CT[:, 0::16], own(j), T.CB[:, 1:2], A.mult, A.mult, "CT E0 ge4", "RH%d" % j)
+        if i == 9:
+            ts(cf(24), cf(26), 2.0 ** -56, None, A.mult, None, "tiny", "eps")
+            ts(cf(16), cf(0), 37.0, -15.5 / 32, A.mult, A.add, "kf", "ck")
+            ts(cf(4), cf(3), 128.0, None, A.add, None, "pf", "pf1")
+            ms(cf(22), -11.0, "m11")
+            ts(T.EI[:], T.IDN[:], cf(24), None, A.mult, None, "IDN eps", "EI")
+            ms(T.SR1[:, 0:32], 1.0, "SR1a")
+            ms(T.SR2[:, 0:32], 0.0, "SR2a")
+            ts(T.SR2[:, 32:64], T.ONE[:, 0:32], cf(0), None, A.mult, None, "ONE kf", "SR2b")
+            ms(T.O32[:], 0.03125, "O32")
 
     def step(t):
         last = t == T_STEPS - 1
         Z, ML = T["Z%d" % t], T["ML%d" % t]
-        zh, mh = ["Z%d_0" % t, "Z%d_1" % t], ["ML%d_0" % t, "ML%d_1" % t]
-        zr, mr, thd = " ".join(zh), " ".join(mh), "thd%d" % t
-        thdc = T.THR[:, t:t + 1]
-        pend = []
-        for x in ("d1v0", "d1v1", "d1s0", "d1s1"):
-            wrote.setdefault(x, ("V", 1))
+        Wc, Wn = T["W%d" % (t & 1)], T["W%d" % (1 - (t & 1))]
+        mc, nw, nb = "MC%d" % (t & 1), "NW%d" % (t & 1), "nb%d" % t
+        zn = lambda a, b: N("Z%d" % t, a, b)
+        mn = lambda a, b: N("ML%d" % t, a, b)
+        sl = lambda a, b, o=0: slice(o + QS_ * a, o + QS_ * b)
+        lc = lambda a, b, o=0, k=1: slice(o + 4 * k * a, o + 4 * k * b)
+        p0 = lambda a, b: T[P0B][:, sl(a, b, B)]
 
-        def kr(c, i):
-            return T.KR[:, 32 * HALF[c][0] + i:32 * HALF[c][1]:32]
+        def kr(a, b, i):
+            return T.KR[:, span(a, b, i, 32)]
 
-        def o16(c):
-            s0, s1 = HALF[c]
-            tc(T.O16[:, s0:s1], T.MC[:, 0:M].indirect(ML[:, 8 * c:8 * c + 8]), "MC " + mh[c], "O16%d" % c)
+        def o16(a, b):
+            tc(T.O16[:, sl(a, b)], Wc[:, B:B + M].indirect(ML[:, lc(a, b)]), mc + " " + mn(a, b), N("O16", a, b))
 
-        def GB(c):
-            s0, s1 = HALF[c]
-            act(T.GB[:, s0:s1], T.GLW[:].indirect(ML[:, 8 * c:8 * c + 8]), F.Copy, "GLW " + mh[c], "GB%d" % c)
+        def gb(a, b):
+            act(T.GB[:, sl(a, b)], T.GLW[:].indirect(ML[:, lc(a, b)]), F.Copy, "GLW " + mn(a, b), N("GB", a, b))
 
-        def ad(c):
-            s0, s1 = HALF[c]
-            act(T.D0[:, 32 * s0 + 1:32 * s1:2], T.ADW[:].indirect(T.O16[:, s0:s1]), F.Copy, "ADW O16%d" % c, "d0a%d" % c, scale=-1.0)
+        def ad(a, b):
+            act(T.D0[:, span(a, b, 1, 2)], T.ADW[:].indirect(T.O16[:, sl(a, b)]), F.Copy, "ADW " + N("O16", a, b), N("d0a", a, b), scale=-1.0)
 
-        def prs(c):
-            s0, s1 = HALF[c]
-            s0 += VPR[c]
-            if s1 > s0:
-                act(T.D1[:, 32 * s0:32 * s1:2], T.PRW[:].indirect(T.O16[:, s0:s1]), F.Copy, "PRW O16%d" % c, "d1s%d" % c)
+        def pr(a, b):
+            act(T.D1[:, span(a, b, 0, 2)], T.PRW[:].indirect(T.O16[:, sl(a, b)]), F.Copy, "PRW " + N("O16", a, b), N("d1p", a, b))
 
-        def prv_(c):
-            s0 = HALF[c][0]
-            s1 = s0 + VPR[c]
-            if s1 > s0:
-                tc(T.D1[:, 32 * s0:32 * s1:2], T.PRW[:].indirect(T.O16[:, s0:s1]), "PRW O16%d" % c, "d1v%d" % c)
+        def pv(a, b):
+            tc(T.D1[:, span(a, b, 0, 2)], T.PRW[:].indirect(T.O16[:, sl(a, b)]), "PRW " + N("O16", a, b), N("d1p", a, b))
 
-        def gw(c):
-            s0, s1 = HALF[c]
-            tc(T.P0[:, s0:s1], T.D1[:, 32 * s0:32 * s1:32], "d1v%d d1s%d" % (c, c), "P0%d" % c)
-            tc(T.D1[:, 32 * s0 + 32:32 * s1:32], T.GB[:, s0:s1 - 1], "GB%d" % c, "d1v%d d1s%d" % (c, c))
+        def p0_(a, b):
+            mm(p0(a, b), T.IDN[:], T.D1[:, span(a, b, 0, 32)], "IDN " + N("d1p", a, b), N("P0", a, b), P0B)
 
-        def scan(c):
-            s0, s1 = HALF[c]
-            hi, lo = 32 * s1 - 1, 32 * s0 - 1 if s0 else None
-            op("V", lambda: V.tensor_tensor_scan(T.KR[:, hi:lo:-1], T.D0[:, hi:lo:-1], T.D1[:, hi:lo:-1], T.GB[:, s1 - 1:s1], A.add, A.max),
-               "GB{0} d0a{0} d0z{0} d1v{0} d1s{0} d1z{0}".format(c), "KR%d" % c)
-            tt(kr(c, 0), T.P0[:, s0:s1], kr(c, 1), A.max, "P0%d KR%d" % (c, c), "K0%d" % c)
+        def gw(a, b):
+            tc(T.D1[:, span(a, b, 32, 32)], T.GB[:, QS_ * a:QS_ * b - 1], N("GB", a, b), N("d1p", a, b))
 
-        def diff(c, q):
-            s0, s1 = HALF[c]
-            bn = "bD%d" % (q & 1)
-            bd = T[bn]
-            e = CMPV[c][q]
-            for j in range(4):
-                mm(bd[:, :, j], T.NID[:], kr(c, 8 * q + 2 * j), "NID KR%d K0%d" % (c, c), bn, bn, True, False)
-                mm(bd[:, :, j], T.IDN[:], Z[:, s0:s1], "IDN " + zh[c], bn, bn, False, True)
-            name = "cmp%d%d" % (c, q)
-            if e == "S":
-                act(T.CMP[:, s0:s1, 4 * q:4 * q + 4], bd[:], F.Sign, bn + " half", name, bn, bias=cf(21))
-            else:
-                ts(T.CMP[:, s0:s1, 4 * q:4 * q + 4], bd[:], 0.0, 0.5, A.is_ge, A.subtract, bn, name, bn)
-            flush()
-            pend.append((c, q, e, name))
+        def scan(a, b):
+            hi, lo = 32 * QS_ * b - 1, 32 * QS_ * a - 1 if a else None
+            sc(T.KR[:, hi:lo:-1], T.D0[:, hi:lo:-1], T.D1[:, hi:lo:-1], T.GB[:, QS_ * b - 1:QS_ * b], A.add, A.max,
+               " ".join(N(x, a, b) for x in ("GB", "d0a", "d0z", "d1p", "d1z")), N("KR", a, b) + " " + N("K0", a, b))
 
-        def flush():
-            for c, q, e, name in pend:
-                s0, s1 = HALF[c]
-                for k in range(4 * q + 3, 4 * q - 1, -1):
-                    mm(T.bM[:, s0:s1], slot(T.E0 if e == "S" else T.EH, k), T.CMP[:, s0:s1, k], "E0 EH " + name, "met%d" % c, "bM", k == 15, k == 0)
-            del pend[:]
+        def k0(a, b):
+            tt(kr(a, b, 0), p0(a, b), kr(a, b, 1), A.max, N("P0", a, b) + " " + N("KR", a, b), N("K0", a, b), P0B)
 
-        def use(c):
-            s0, s1 = HALF[c]
-            for k in range(15, -1, -1):
-                up = kr(c, 2 * k + 2) if k < 15 else T.GB[:, s0:s1]
-                mm(T.bL[:, B + s0:B + s1], slot(T.E0, k), up, "E0 GB%d KR%d" % (c, c), "use%d" % c, "bL", k == 15, False)
-                mm(T.bL[:, B + s0:B + s1], slot(T.NE, k), kr(c, 2 * k + 1), "NE KR%d" % c, "use%d" % c, "bL", False, k == 0)
+        def zp(a, b):
+            bn = "bC%d" % (a & 1)
+            if CMPV[a] == "V":
+                for j in range(8):
+                    mm(T[bn][:, j::8], T.IDN[:], Z[:, sl(a, b)], "IDN " + zn(a, b), bn, bn)
 
-        def zs():
-            act(T.MB[:], T.W37[:].indirect(ML[:]), F.Copy, "W37 " + mr, "MB")
-            mm(T.bO[:, 0:B], T.BW[:], Z[:], "BW " + zr, "uR", "bO")
-            mm(T.bO[:, B:2 * B], T.BW[:], Z[:], "BW " + zr, "xR", "bO", True, False)
-            mm(T.bO[:, B:2 * B], T.IDN[:], T.MB[:], "IDN MB", "xR", "bO", False, True)
-            mm(T.bF[:, 0:B], T.IDN[:], Z[:], "IDN " + zr, "d16", "bF", True, False)
-            mm(T.bF[:, 0:B], T.NID[:], T.GB[:], "NID GB0 GB1", "d16", "bF", False, True)
-            for r in range(16):
-                mm(L(0), slot(T.WE, r), Z[:, r::16], "WE " + zr, "uL", "bL", r == 0, r == 15)
-
-        def c16():
-            if t == 0:
-                zeros(1)
-            act(T.C16[:], T.bF[:, 0:B], F.Sign, "d16 half", "C16", "bF", bias=cf(21))
-            for r in range(16):
-                mm(L(16), slot(T.E0, r), T.C16[:, r::16], "E0 C16", "gL", "bL", r == 0, r == 15)
-            for h in range(2):
-                mm(T.bL[:, 32 + 8 * h:40 + 8 * h], T.C16[:, 128 * h:128 * h + 128], T.E0[:, 15:128:16], "E0 C16", "gT%d" % h, "bL")
-            mm(T.bF[:, B:2 * B], T.BO[:], T.C16[:], "BO C16", "gR", "bF")
-
-        def pairs(i):
-            bn = "bG%d" % (i & 1)
-            bg = T[bn]
-            if i < 4:
-                for h in range(2):
-                    mm(bg[:, :, 16 * h:16 * h + 16], T["BLO" if h else "BLE"][32 * i:32 * i + 32, 0:128], T.BR[32 * i:32 * i + 32, :], "BLE BLO BR", bn, bn)
-                act(T.EQ0[:, :, 32 * i:32 * i + 32], bg[:], F.Relu, bn + " bias0", "EQ0%d" % i, bn, bias=cf(19), scale=512.0)
+        def cmp_(a, b, h):
+            kn = N("KR", a, b) + ("" if h else " " + N("K0", a, b))
+            c0 = 8 * B * h + 8 * QS_ * a
+            out, name = T.CMP[:, c0:c0 + 8 * QS_], "cmp%d%d" % (a, h)
+            if CMPV[a] == "V":
+                bn = "bC%d" % (a & 1)
+                tt(out, T.KR[:, span(a, b, 2 * h, 4)], T[bn][:], A.is_le, kn + " " + bn, name, bn)
                 return
-            two = (2 * (i - 4), 2 * (i - 4) + 1)
-            for q, a in enumerate(two):
-                if q:
-                    need("T", [("T", cnt["T"])])
-                for h in range(2):
-                    mm(bg[:, 8 * q:8 * q + 8, 16 * h:16 * h + 16], T["BLO" if h else "BLE"][32 * a:32 * a + 32, 128:256],
-                       T.BR[32 * a:32 * a + 32, 128:256], "BLE BLO BR", bn, bn)
-            for q, a in enumerate(two):
-                act(T.EQ1[:, :, 32 * a:32 * a + 32], bg[:, 8 * q:8 * q + 8, :], F.Relu, bn + " bias1", "EQ1%d" % a, bn, bias=cf(20), scale=512.0)
+            bn = "bC%d" % h
+            for j in range(8):
+                mm(T[bn][:, j::8], T.NID[:], kr(a, b, 4 * j + 2 * h), "IDN NID %s %s" % (kn, zn(a, b)), bn, bn, True, False)
+                mm(T[bn][:, j::8], T.IDN[:], Z[:, sl(a, b)], "IDN " + zn(a, b), bn, bn, False, True)
+            act(out, T[bn][:], F.Sign, bn + " half", name, bn, bias=cf(21))
 
-        def ok(h):
-            s0, s1 = HALF[h]
-            ts(T.OK[:, s0:s1], T.bM[:, s0:s1], thdc, None, A.is_ge, None, "met%d %s" % (h, thd), "OK%d" % h, "bM")
+        def met(a, b):
+            for i, k in enumerate(list(range(1, 16, 2)) + list(range(0, 16, 2))):
+                c0 = 8 * B * (k & 1) + 8 * QS_ * a
+                mm(T.bM[:, sl(a, b)], slot(T.E0 if CMPV[a] == "S" else T.EH, k), T.CMP[:, c0 + k // 2:c0 + 8 * QS_:8], "E0 EH cmp%d%d" % (a, k & 1), N("met", a, b), "bM",
+                   i == 0, i == 15)
 
-        def oh(h):
-            s0, s1 = HALF[h]
-            mm(T.bF[:, s0:s1], T.UP[:], T.OK[:, s0:s1], "UP OK%d C16" % h, "first%d" % h, "bF", True, False)
-            mm(T.bF[:, s0:s1], T.NEG[:], T.GREP[:, s0:s1], "NEG GREP", "first%d" % h, "bF", False, True)
-            ts(T.OH[:, s0:s1], T.bF[:, s0:s1], 1.0, None, A.is_ge, None, "first%d" % h, "OH%d" % h, "bF")
+        def use(a, b):
+            o, w = T.bU[:, sl(a, b)], N("use", a, b)
+            for k in range(15, -1, -1):
+                up = kr(a, b, 2 * k + 2) if k < 15 else T.GB[:, sl(a, b)]
+                mm(o, slot(T.EK, k), up, "EK ER %s %s" % (N("GB", a, b), N("KR", a, b)), w, "bU", k == 15, False)
+                mm(o, slot(T.ER, k), kr(a, b, 2 * k + 1), "ER " + N("KR", a, b), w, "bU", False, False)
+            mm(o, T.ONE[:], T.HB[:], "ONE HB0 HB1", w, "bU", False, False)
+            mm(o, T.I16[:], T.OF[:, sl(a, b)], "I16 " + N("OF", a, b), w, "bU", False, True)
 
-        def vl(h):
-            s0, s1 = HALF[h]
-            o = T.bL[:, 64 + 8 * h:72 + 8 * h]
-            mm(o, T.IDN[:], T.B32[:], "IDN B32", "vl%d" % h, "bL", True, False)
+        def ok(a, b):
+            ts(T.OK[:, sl(a, b)], T.bM[:, sl(a, b)], T.NB[:, t:t + 1], 0.5 if CMPV[a] == "S" else 16.5, A.add, A.is_ge, N("met", a, b) + " " + nb, N("OK", a, b), "bM")
+
+        def first(a, b):
+            mm(T.bM[:, sl(a, b, B)], T.NEG[:], T.GREP[:, sl(a, b)], "NEG GREP UP " + N("OK", a, b), N("first", a, b), "bM", True, False)
+            mm(T.bM[:, sl(a, b, B)], T.UP[:], T.OK[:, sl(a, b)], "UP " + N("OK", a, b), N("first", a, b), "bM", False, True)
+
+        def oh(a, b):
+            ts(T.OH[:, sl(a, b)], T.bM[:, sl(a, b, B)], 1.0, None, A.is_ge, None, N("first", a, b), N("OH", a, b), "bM")
+
+        def any_(a, b):
             for r in range(16):
-                mm(o, slot(T.WJ, r), T.OH[:, s0 + r:s1:16], "WJ OH%d" % h, "vl%d" % h, "bL", False, r == 15)
-            mm(T.bF[:, B + s0:B + s1], T.DT[:, 128 * t:128 * t + 128], T.OH[:, s0:s1], "DT OH%d GREP" % h, "de%d" % h, "bF")
+                mm(T.bL[:, 33 + 8 * a:32 + 8 * b:2], slot(T.E0, r), T.OH[:, QS_ * a + r:QS_ * b:16], "E0 " + N("OH", a, b), N("any", a, b), "bL", r == 0, r == 15)
 
-        def dl(h):
-            o = T.bL[:, 64 + 8 * h:72 + 8 * h]
-            tt(lh(1, h), o, T.SL[:, 0:8], A.not_equal, "vl%d b32f" % h, "any%d" % h, "bL")
-            ts(T.AOFF[:, 8 * h:8 * h + 8], o, 2.0, None, A.add, None, "vl%d" % h, "AOFF%d" % h, "bL")
-            tt(lh(2, h), lh(1, h), lh(0, h), A.mult, "any%d dm" % h, "mmx%d" % h)
-            tt(lh(3, h), lh(2, h), T.LI[:, 48 + 8 * h:56 + 8 * h], A.add, "mmx%d to" % h, "mn%d" % h)
+        def ms_(a, b):
+            sc(T.MN[:, lc(a, b, 0, 2)], T.bL[:, lc(a, b, 32, 2)], T.DM[:, lc(a, b, 0, 2)], 0.0, A.mult, A.add, "dm tof " + N("any", a, b), N("MN", a, b), "bL")
 
-        def sm(h):
+        MO = T.LF if last else T["MO%d" % (t + 1)]
+
+        def mo(a, b):
+            tc(MO[:, lc(a, b)], T.MN[:, 8 * a + 1:8 * b:2], N("MN", a, b), N("MO", a, b))
+
+        def sm(a, b):
             if not last:
-                c0, c1 = 8 * h, 8 * h + 8
-                tc(T["MO%d" % (t + 1)][:, c0:c1], lh(3, h), "mn%d" % h, "MO%d" % h)
-                send("ML", t + 1, h, c0, c1, T["MO%d" % (t + 1)], "MO%d" % h)
-            elif h:
-                dma("Y", T.ym[:], lf(3), "o_ym", "mn0 mn1", "")
+                send("ML", t + 1, a, b, 4 * a, 4 * b, MO, N("MO", a, b))
+            elif b == 4:
+                dma("Y", T.ym[:], MO[:, 0:16], "o_ym", N("MO", 0, 4), "")
 
-        def t1(h):
-            s0, s1 = HALF[h]
-            tt(T.T1[:, s0:s1], T.D0[:, 32 * s0:32 * s1].indirect(T.AOFF[:, 8 * h:8 * h + 8]), Z[:, s0:s1], A.subtract,
-               "AOFF%d d0a%d d0z%d %s" % (h, h, h, zh[h]), "T1%d" % h)
+        def vl(a, b):
+            o = T.bL[:, lc(a, b, 16)]
+            mm(o, T.IDN[:], T.B32[:, 0:4 * (b - a)], "IDN B32 WJ " + N("OH", a, b), N("vl", a, b), "bL", True, False)
+            for r in range(16):
+                mm(o, slot(T.WJ, r), T.OH[:, QS_ * a + r:QS_ * b:16], "WJ " + N("OH", a, b), N("vl", a, b), "bL", False, r == 15)
 
-        def t2(h):
-            s0, s1 = HALF[h]
-            act(T.T2[:, s0:s1], T.T1[:, s0:s1], F.Relu, "T1%d c255" % h, "T2%d" % h, bias=cf(22))
+        def ao(a, b):
+            ts(T.AOFF[:, lc(a, b)], T.bL[:, lc(a, b, 16)], 2.0, None, A.add, None, N("vl", a, b), N("AOFF", a, b), "bL")
 
-        def t3(h):
-            s0, s1 = HALF[h]
-            tt(T.T3[:, s0:s1], T.T2[:, s0:s1], T.bF[:, B + s0:B + s1], A.add, "T2%d de%d" % (h, h), "T3%d" % h, "bF")
+        def t1(a, b):
+            tt(T.T1[:, sl(a, b)], T.D0[:, span(a, b, 0, 1)].indirect(T.AOFF[:, lc(a, b)]), T.ZM[:, sl(a, b)], A.max,
+               " ".join(N(x, a, b) for x in ("AOFF", "d0a", "d0z")) + " ZM", N("T1", a, b))
 
-        def sz(h):
-            s0, s1 = HALF[h]
+        def zz(a, b):
+            o, w = T.bF[:, sl(a, b)], N("zz", a, b)
+            mm(o, T.DT[:, 128 * t:128 * t + 128], T.OH[:, sl(a, b)], "DT NID IDN %s %s %s" % (N("OH", a, b), zn(a, b), N("T1", a, b)), w, "bF", True, False)
+            mm(o, T.NID[:], Z[:, sl(a, b)], "NID " + zn(a, b), w, "bF", False, False)
+            mm(o, T.IDN[:], T.T1[:, sl(a, b)], "IDN " + N("T1", a, b), w, "bF", False, True)
+
+        def ab(a, b):
             out = T.ZF if last else T["ZO%d" % (t + 1)]
-            act(out[:, s0:s1], T.T3[:, s0:s1], F.Abs, "T3%d cm255" % h, "ZO%d" % h, bias=cf(23))
+            act(out[:, sl(a, b)], T.bF[:, sl(a, b)], F.Abs, N("zz", a, b), N("ZO", a, b), "bF")
+
+        def sz(a, b):
             if last:
-                dma("Y", T.yz[:, s0:s1], out[:, s0:s1], "o_yz%d" % h, "ZO%d" % h, "")
+                dma("Y", T.yz[:, sl(a, b)], T.ZF[:, sl(a, b)], "o_yz%d" % (a // 2), N("ZO", a, b), "")
             else:
-                send("Z", t + 1, h, s0, s1, out, "ZO%d" % h)
+                send("Z", t + 1, a, b, QS_ * a, QS_ * b, T["ZO%d" % (t + 1)], N("ZO", a, b))
 
-        def conf():
-            e0 = " ".join("EQ0%d" % a for a in range(4))
-            e1 = " ".join("EQ1%d" % a for a in range(4))
-            for c in range(16):
-                o = T.bL[:, 128 + 8 * c:136 + 8 * c]
-                mm(o, T.EQ0[:, c, :], T.GLT[:, 16:24], "GLT " + e0, "CT", "bL", True, c < 8)
-                if c >= 8:
-                    mm(o, T.EQ1[:, c - 8, :], T.GLT[:, 24:32], "GLT " + e1, "CT", "bL", False, True)
+        def n0(a, b):
+            tt(T.N0[:, sl(a, b)], T.bU[:, sl(a, b)], T.GM[:, sl(a, b)], A.min, "GM " + N("use", a, b), N("N0", a, b), "bU")
 
-        def asum():
-            if not last:
-                for j in range(16):
-                    mm(T.bL[:, 80:81], T.ONE[:], T.GLT[:, j:j + 1], "ONE GLT", "as0", "bL", j == 0, j == 15)
+        def nn(a, b):
+            ts(Wc[:, sl(a, b)], T.N0[:, sl(a, b)], W - 1, None, A.bitwise_and, None, N("N0", a, b), N(nw, a, b))
 
-        def par():
-            if not last:
-                tc(T.AI[:, 0:1], T.bL[:, 80:81], "as0", "as2", "bL")
-                ts(T.AI[:, 1:2], T.AI[:, 0:1], 1, None, A.bitwise_and, None, "as2", "as3")
-                ts(T.THR[:, t + 1:t + 2], T.AI[:, 1:2], 2.0, float(2 * QU - 16), A.mult, A.add, "as3", "thd%d" % (t + 1))
-                ts(T.THR[:, t + 5:t + 6], T.AI[:, 1:2], -2.0, 17.0 - 2 * QU, A.mult, A.add, "as3", "thb%d" % (t + 1))
+        def of(a, b):
+            tc(T.OF[:, sl(a, b)], T.O16[:, sl(a, b)], N("O16", a, b), N("OF", a, b))
 
-        def cx():
-            op("V", lambda: V.tensor_tensor_scan(T.CX[:], T.DX[:], T.bL[:, 128:256], 0.0, A.add, A.max), "DX CT", "CX", "bL")
-            ts(lf(6), T.CX[:, 7::8], cf(18), None, A.is_le, None, "CX nb", "free")
-            tt(lf(7), lf(6), lf(5), A.mult, "free gd", "w2")
-            tt(lf(8), lf(7), T.SL[:, 16:32], A.add, "w2 b512", "off")
-            tc(T.OFF[:], lf(8), "off", "OFF")
+        def xl(h):
+            s = " ".join("RL%d" % j for j in range(8))
+            mm(T.bF[:, B:B + 128], T.CD[:, 128 * h:128 * h + 128], T.RL[:], "CD GREP RG " + s, "xl", "bF", True, False)
+            mm(T.bF[:, B:B + 128], T.GREP[:, 128 * h:128 * h + 128], T.RG[:], "GREP RG", "xl", "bF", False, True)
 
-        def ml():
-            tc(li(0), ML[:], mr, "mI")
-            ts(li(1), li(0), 37.0, None, A.mult, None, "mI", "m37")
-            if t == 0:
-                later_const()
+        def xh(h):
+            mm(T.bX[:, 8 * h:8 * h + 8, :], T.CD[:, 128 * h:128 * h + 128], T.RH[:], "CD " + " ".join("RH%d" % j for j in range(8)), "xh%d" % h, "bX")
 
-        def toL():
-            tt(li(2), L(0), li(1), A.add, "uL m37", "to0", "bL")
-            ts(li(3), li(2), M - 1, None, A.bitwise_and, None, "to0", "to")
-            tt(lf(0), li(0), li(3), A.subtract, "mI to", "dm")
+        def lw(h):
+            act(T.LP[:, LPC:LPC + 128], T.bF[:, B:B + 128], F.Relu, "xl wcol wbias", "LP", "bF", bias=cf(12), scale=cf(10))
 
-        def td():
-            tt(lf(4), li(3), T.SL[:, 16:32], A.subtract, "to b512", "td")
-            tt(lf(5), lf(4), T.GLT[:, 0:16], A.mult, "td GLT", "gd")
+        def hh(h):
+            act(T.HH[:, :, 0:32], T.bX[:, 8 * h:8 * h + 8, :], F.Relu, "xh%d m11" % h, "HH", "bX", bias=cf(22))
 
-        def oP():
-            act(T.bO[:, 0:B], T.OF[:], F.Copy, "OF UI", "oP", "bO")
-            act(T.bO[:, B:2 * B], T.OF[:], F.Identity, "OF XQ c1184", "oK", "bO", bias=cf(16), scale=32.0)
+        def hs(h):
+            ts(T.HH[:, :, 32:64], T.HH[:, :, 0:32], cf(4 if h else 3), None, A.mult, None, "HH pf pf1", "HS")
+
+        def tm(h):
+            o = T.bL[:, 128 + h:256:2]
+            mm(o, T.EI[:], T.SR1[:], "EI SR1a SR1b SR2a SR2b LP HH HS", "tm%d" % h, "bL", True, False)
+            mm(o, T.EI[:], T.SR2[:], "SR2a SR2b", "tm%d" % h, "bL", False, False)
+            for j in range(8):
+                mm(o, T.LP[:, LPC - 127 * j:LPC - 127 * j + 1017:8], T.HH[:, j, :], "LP HH HS", "tm%d" % h, "bL", False, j == 7)
+
+        def ul():
+            for r in range(16):
+                mm(T.bL[:, 0:16], slot(T.WE, r), Z[:, r::16], "WE " + zn(0, 4), "uL", "bL", r == 0, r == 15)
+
+        def d16():
+            mm(T.bG[:, 0:B], T.IDN[:], Z[:], "IDN NID %s %s" % (zn(0, 4), N("GB", 0, 4)), "d16", "bG", True, False)
+            mm(T.bG[:, 0:B], T.NID[:], T.GB[:], "NID " + N("GB", 0, 4), "d16", "bG", False, True)
+
+        def mc_():
+            if last:
+                tc(T.YM[:], Wc[:].indirect(T.OFF[:]), "OFF %s %s" % (mc, N(nw, 0, 4)), "YM")
+                dma("Y", T.ymc[:], T.YM[:], "o_ymc", "YM", "")
+            else:
+                tc(Wn[:, B:B + M], Wc[:].indirect(T.OFF[:]), "OFF %s %s" % (mc, N(nw, 0, 4)), "MC%d" % (1 - (t & 1)))
 
         one = {
-            "of": lambda: tc(T.OF[:], T.O16[:], "O160 O161", "OF"),
-            "ui": lambda: tc(T.UI[:], T.bO[:, 0:B], "uR", "UI", "bO"),
-            "uu": lambda: ts(T.UU[:], T.UI[:], W - 1, None, A.bitwise_and, None, "UI", "UU"),
-            "xq": lambda: ts(T.XQ[:], T.bO[:, B:2 * B], cf(15), cf(5), A.mult, A.add, "xR cb cb2", "XQ", "bO"),
-            "bit": lambda: ts(T.BIT[:], T.XQ[:], 1, None, A.bitwise_and, None, "XQ", "BIT"),
-            "br": lambda: tt(T.BR[:], T.BIT[:], T.bM[:, B:2 * B], A.add, "BIT CONST", "BR", "bM"),
-            "ble": lambda: ts(T.BLE[:], T.BIT[:], cf(8), cf(9), A.mult, A.add, "BIT e1 e2", "BLE"),
-            "blo": lambda: ts(T.BLO[:], T.BIT[:], cf(10), cf(11), A.mult, A.add, "BIT o1 o2", "BLO"),
-            "glt": lambda: ts(T.GLT[:], T.bL[:, 16:48], thdc, None, A.is_ge, None, "gL gT0 gT1 " + thd, "GLT", "bL"),
-            "grep": lambda: act(T.GREP[:], T.bF[:, B:2 * B], F.Sign, "gR thb%d" % t, "GREP", "bF", bias=T.THR[:, 4 + t:5 + t]),
-            "fq": lambda: tt(T.FQ[:], T.bO[:, 0:B], T.UU[:], A.mult, "oP UU", "FQ", "bO"),
-            "ft": lambda: tt(T.FT[:], T.FQ[:], T.bO[:, B:2 * B], A.add, "FQ oK", "FT", "bO"),
-            "fr": lambda: ts(T.FR[:], T.FT[:], 5, W - 1, A.arith_shift_right, A.bitwise_and, "FT", "FR"),
-            "df": lambda: tt(T.DF[:], T.FR[:], T.bO[:, 0:B], A.subtract, "FR oP", "DF", "bO"),
-            "low": lambda: ts(T.bO[:, B:2 * B], T.bL[:, B:2 * B], float(TH), None, A.is_lt, None, "use0 use1", "oK", "bL bO"),
-            "ldf": lambda: tt(T.LDF[:], T.bO[:, B:2 * B], T.DF[:], A.mult, "oK DF", "LDF", "bO"),
-            "wr": lambda: tt(T.MC[:, 0:M + B].indirect(T.OFF[:]), T.LDF[:], T.OF[:], A.add, "LDF OF OFF", "MC"),
-            "ml": ml, "zs": zs, "c16": c16, "toL": toL, "oP": oP, "conf": conf, "td": td, "cx": cx, "as": asum, "par": par, "fl": flush}
-        per = {"o16": o16, "GB": GB, "ad": ad, "prs": prs, "prv": prv_, "gw": gw, "scan": scan, "use": use, "ok": ok, "oh": oh, "vl": vl, "dl": dl,
-               "sm": sm, "t1": t1, "t2": t2, "t3": t3, "sz": sz}
+            "m37": lambda: ts(T.LF[:, 16:32], ML[:], 37.0, None, A.mult, None, mn(0, 4), "m37"),
+            "mi": lambda: tc(T.LI[:, 0:16], ML[:], mn(0, 4), "mI"),
+            "to0": lambda: tt(T.LI[:, 16:32], T.bL[:, 0:16], T.LF[:, 16:32], A.add, "uL m37", "to0", "bL"),
+            "ui": lambda: tc(T.LI[:, 32:48], T.bL[:, 0:16], "uL", "ui", "bL"),
+            "to": lambda: ts(T.XI[:, 16:32], T.LI[:, 16:32], M - 1, None, A.bitwise_and, None, "to0", "to"),
+            "u": lambda: ts(T.XI[:, 0:16], T.LI[:, 32:48], W - 1, None, A.bitwise_and, None, "ui", "u"),
+            "tof": lambda: tc(T.DM[:, 1::2], T.XI[:, 16:32], "to", "tof"),
+            "xu": lambda: tc(T.XU[:], T.XI[:], "to u", "XU"),
+            "dm": lambda: tt(T.DM[:, 0::2], T.LI[:, 0:16], T.XI[:, 16:32], A.subtract, "mI to", "dm"),
+            "c16": lambda: act(T.C16[:], T.bG[:, 0:B], F.Sign, "d16 half", "C16", "bG", bias=cf(21)),
+            "gr": lambda: mm(T.bG[:, B:2 * B], T.BO[:], T.C16[:], "BO C16", "gR", "bG"),
+            "grep": lambda: act(T.GREP[:], T.bG[:, B:2 * B], F.Sign, "gR " + nb, "GREP AC", "bG", bias=T.NB[:, t:t + 1], accum_out=T.AC[:, t:t + 1]),
+            "code": lambda: act(T.CD[:], T.CT[:].indirect(T.XU[:, 16:32]), F.Copy, "CT XU", "CD"),
+            "zm": lambda: ts(T.ZM[:], Z[:], -255.0, None, A.add, None, zn(0, 4), "ZM"),
+            "fq": lambda: tt(T.FQ[:], T.UT[:].indirect(T.XU[:, 0:16]), T.OF[:], A.mult, "UT XU " + N("OF", 0, 4), "FQ"),
+            "g": lambda: ts(T.GI[:], T.FQ[:], 0.03125, cf(16), A.mult, A.add, "FQ ck", "GI"),
+            "gm": lambda: ts(T.GM[:], T.GI[:], W - 1, None, A.bitwise_and, None, "GI", "GM"),
+            "rec": lambda: op("V", lambda: V.reciprocal(T.RC[:], T.bL[:, 128:192]), "tm0 tm1", "RC", "bL"),
+            "rt": lambda: tt(T.RT[:], T.bL[:, 192:256], T.RC[:], A.mult, "tm0 tm1 RC", "RT", "bL"),
+            "rm": lambda: tt(T.LI[:, 48:80], T.RT[:, 0::2], T.RT[:, 1::2], A.min, "RT", "rm"),
+            "off": lambda: tc(T.OFF[:], T.LI[:, 48:80], "rm", "OFF"),
+            "ul": ul, "d16": d16, "mc": mc_}
+        ahead = {
+            "as": lambda: mm(T.bG[:, 0:1], T.O32[:], T.AC[:, t:t + 1], "O32 AC", "d16", "bG"),
+            "ai": lambda: tc(T.AI[:, 0:1], T.bG[:, 0:1], "d16", "as2", "bG"),
+            "ap": lambda: ts(T.AI[:, 1:2], T.AI[:, 0:1], 1, None, A.bitwise_and, None, "as2", "as3"),
+            "nb": lambda: ts(T.NB[:, t + 1:t + 2], T.AI[:, 1:2], -2.0, 17.0 - 2 * QU, A.mult, A.add, "as3", "nb%d" % (t + 1))}
+        per = {"o16": o16, "gb": gb, "ad": ad, "pr": pr, "pv": pv, "p0": p0_, "gw": gw, "scan": scan, "k0": k0, "zp": zp, "met": met, "use": use, "ok": ok,
+               "ch": lambda a, b: cmp_(a, b, 1), "cl": lambda a, b: cmp_(a, b, 0), "mo": mo,
+               "first": first, "oh": oh, "any": any_, "ms": ms_, "sm": sm, "vl": vl, "ao": ao, "t1": t1, "zz": zz, "ab": ab, "sz": sz, "n0": n0, "nn": nn, "of": of}
+        half = {"xl": xl, "xh": xh, "lw": lw, "hh": hh, "hs": hs, "tm": tm}
 
         def run(x):
             a, _, b = x.partition(":")
             if a in per:
-                per[a](int(b))
-            elif b:
-                diff(int(a[1:]), int(b))
+                per[a](int(b[0]), int(b[1]))
+            elif a in half:
+                half[a](int(b))
             elif a in one:
                 one[a]()
-            else:
-                pairs(int(a[1:]))
-            if t == 0 and x == "grep":
-                passes()
+            elif a in ahead:
+                if not last:
+                    ahead[a]()
+            elif t == 0:
+                const(int(a[1:]))
         return run
 
     runs = [step(t) for t in range(T_STEPS)]
@@ -501,10 +489,9 @@ def rank_program(g, core, T, topo):
                 runs[t](x)
             elif t + 1 < T_STEPS:
                 runs[t + 1](x[1:])
-    dma("Y", T.ymc[:], T.MC[:, 0:M], "o_ymc", "MC", "")
     need("G", [(s, cnt[s]) for s in ("V", "S", "T", "G")])
     need("G", [("l_" + x, 16) for x in LOADS] + [("o_" + x, 16) for x in OUTS])
     for t in range(1, T_STEPS):
-        for h in range(2):
+        for q in SENDS:
             for b in "mz":
-                need("G", [("r%s%d%d" % (b, t, h), len(eng(prv, core))), ("s%s%d%d" % (b, t, h), len(eng(core, nxt)))])
+                need("G", [("r%s%d%d" % (b, t, q[0]), len(eng(prv, core))), ("s%s%d%d" % (b, t, q[0]), len(eng(core, nxt)))])

@@ -4,31 +4,36 @@ F = ActivationFunctionType
 
 T_STEPS, W, M, B, QU, TH = 4, 2048, 512, 256, 12, 254
 QS_ = 64
-CMPV = "VVVS"
 RATIO = 3.2
-LPC = 896
-P0B = "bL"
-ORDER = ("k0:12 use:12 ad:23 to0 to gr p0:23 grep cl:12 pr:34 ui dm ad:34 met:01 of:24 u xu met:12 #8 fq ok:02 tof use:01 gw:23 g first:02 oh:02 scan:23 zp:23 as +#1 p0:34 gw:34 vl:02 any:02 use:23 gm code ai ms:02 k0:23 mo:02 xh:1 xh:0 scan:34 cl:23 xl:0 use:34 hh:0 k0:34 zm sm:02 hs:0 ch:23 lw:0 tm:0 n0:34 xl:1 hh:1 ao:02 lw:1 n0:03 hs:1 ch:34 tm:1 nn:03 cl:34 t1:02 met:23 nn:34 +gb:02 rec ap rt rm ok:23 off nb mc zz:02 ab:02 met:34 ok:34 +o16:02 +#3 first:24 oh:24 vl:24 sz:02 ao:24 +ad:01 +#5 +pr:01 any:24 t1:24 +#7 ms:24 zz:24 ab:24 +#2 +#4 +#9 +zp:01 +pr:12 +of:02 +ad:12 +p0:01 +zp:12 +#6 mo:24 +p0:12 sm:24 +gw:01 +scan:01 +k0:01 +ch:01 +gw:12 +o16:24 sz:24 +mi +scan:12 +cl:01 +gb:24 +m37 +pr:23 +d16 +ul +ch:12 +c16").split()
-SENDS = [(0, 2), (2, 4)]
+LPC = 1792
+CMPV = ["VV", "VV", "SS", "SS"]
+CMPL = ["VV", "VV", "SS", "SS"]
+CB = [["bC0", "bC0"], ["bC1", "bC1"], ["bC0", "bC1"], ["bG", "bX"]]
+UB, UC, UN = "bU", 256, "d16_0 d16_1"
+ORDER = ("hh p0:34 vl:02 ad:68 zh:34 tof scan:23 dm gg:34 lw an:02 k0:23 mt:02 ai mo:02 of:24 hs:0 ao:02 hc:1 scan:34 zl:34 ch:23 zs:04 cl:23 tm:0 tm:1 ut:24 sm:02 fq rec k0:34 met:23 lo:24 g rt uh:24 t1:02 ok:23 rm ch:34 first:23 n0:24 n0:02 oh:23 cl:34 zz:02 off ab:02 ap vl:23 mc +gb:02 an:23 +o16:12 mt:23 +o16:01 sz:02 met:34 mo:23 ok:34 +pv:01 +pr:24 first:34 oh:34 vl:34 +pv:12 +ad:02 ao:24 an:34 t1:24 mt:34 +p0:02 sm:23 mo:34 +gw:01 +of:02 sm:34 zz:24 +zh:12 ab:24 +scan:01 +zh:01 sz:24 +o16:23 +gg:12 +ad:24 +scan:12 +ch:01 +ut:02 +pr:46 +k0:02 nb +cl:01 +met:01 +cl:12 +m37 +mi +ch:12 +gb:24 +lo:02 +ad:46 +ul +to0 +d16 +ui +met:12 +to +u +c16 +xu +gr +o16:34 +p0:23 +gg:23 +zl:23 +code +ok:02 +grep +xh:1 +xh:0 +pv:67 +first:02 +xl:0 +oh:02 +pr:78 +as +xl:1 +uh:02 +zh:23").split()
+LAST = "scan:23 zl:34 hh p0:34 vl:02 ad:68 zh:34 lw hc:1 tof hs:0 an:02 k0:23 of:24 gg:34 ch:23 cl:23 ao:02 scan:34 dm tm:0 zs tm:1 fq ut:24 met:23 lo:24 k0:34 rec g rt ch:34 ok:23 uh:24 first:23 t1:02 cl:34 mt:02 oh:23 vl:23 rm n0:02 off n0:24 met:34 ao:23 ok:34 t1:23 mc zz:02 first:34 os:34 ab:02 vl:34 ao:34 t1:34 an:24 mo:02 mt:24 zz:23 ab:23 mo:24 zz:34 sz:02 sz:23 ab:34 sm:34 sz:34".split()
+FIRST = "#1 m37 zh:01 o16:04 #3 ad:02 pr:24 #5 gb:04 #2 #7 p0:12 #9 pv:02 #4 p0:01 ad:24 mi d16 c16 pr:46 ul gr zh:12 gw:01 gw:12 grep #8 #6 ad:46 to0 ui p0:23 scan:01 scan:12 ch:01 to k0:02 u gg:23 ch:12 cl:12 xu ut:02 lo:02 code as cl:01 pv:67 met:12 met:01 zl:23 ok:02 xh:0 xh:1 of:02 first:02 xl:0 oh:02 #0 pr:78 xl:1 zh:23 uh:02".split()
+SENDS = [x.lstrip("+")[1] + x[-2] for x in ORDER if x.lstrip("+")[:3] in ("sm:", "sz:")]
 SB, PS = "sbuf", "psum"
 BF, F4, I4, U2, H2 = "bfloat16", "float32", "int32", "uint16", "float16"
-SCRATCH = {"CMP": (SB, [128, 16 * B], BF), "HH": (SB, [128, 8, 64], BF), "bC0": (PS, [128, 512], F4), "bC1": (PS, [128, 512], F4),
-           "bX": (PS, [128, 16, 32], F4), "KR": (SB, [128, 32 * B], BF)}
-for _n, _w, _d in ([(x, 512, F4) for x in ("bM", "bL", "bF", "bU", "bG")]
+BANKS = ("bM", "bL", "bF", "bU", "bG", "bX", "bC0", "bC1")
+SCRATCH = {}
+for _n, _w, _d in ([(x, 512, F4) for x in BANKS]
                    + [("PRW", W, BF), ("ADW", W, BF), ("GLW", M, BF), ("W0", M + B, I4), ("W1", M + B, I4), ("YM", M, F4), ("UT", W, F4),
-                      ("WI", M, I4), ("XQ", M, I4), ("BIT", M, I4), ("CT", M, BF), ("LP", 2048, BF), ("RH", B, BF),
-                      ("M0", 16, I4), ("DV", 4, BF), ("WT", 1, BF), ("O16", B, U2), ("OF", B, H2), ("I16", 128, H2), ("D0", 32 * B, BF), ("D1", 32 * B, BF),
-                      ("AOFF", 16, U2), ("OFF", 32, U2), ("XU", 32, U2), ("XI", 32, I4), ("LI", 80, I4), ("LF", 48, F4), ("DM", 32, F4), ("MN", 32, F4),
+                      ("CT", M, BF), ("LP", 3840, BF), ("RH", B, BF), ("HH", 1024, BF), ("CMP", 16 * B, BF),
+                      ("M0", 16, I4), ("DV", 4, BF), ("WT", 1, BF), ("O16", B, U2), ("OF", B, H2), ("I16", 128, H2),
+                      ("D0", 32 * B, BF), ("D1", 32 * B, BF), ("KR", 32 * B, BF),
+                      ("AOFF", 16, U2), ("OFF", 32, U2), ("XU", 32, U2), ("XI", 32, I4), ("LI", 80, I4), ("LF", 48, F4), ("DM", 32, F4), ("MN", 32, F4), ("AN", 32, F4),
                       ("RC", 64, F4), ("RT", 64, F4), ("CI", 4, I4), ("CF", 32, F4), ("NB", 4, F4), ("AC", 4, F4), ("AI", 2, I4), ("DG", 512, BF), ("DT", 512, BF),
-                      ("IOT", 8, F4), ("WS", 512, BF), ("B32", 8, BF), ("CB", 2, BF), ("SR1", 64, BF), ("SR2", 64, BF), ("HB", QS_, BF), ("O32", 128, F4)]
+                      ("IOT", 16, F4), ("SG", 32, F4), ("WS", 512, BF), ("B32", 8, BF), ("EN", 8, BF), ("LOW", 128, BF), ("I2K", 128, BF), ("CB", 2, BF), ("SR1", 64, BF), ("SR2", 64, BF), ("HB", QS_, BF), ("O32", 128, F4)]
                    + [(x, 144, BF) for x in ("E1", "E2", "E0", "EH", "EK", "ER", "WE", "WJ")]
                    + [(x, B, BF) for x in ("GB", "C16", "CD", "GREP", "OK", "OH", "ZM", "T1")]
-                   + [(x, B, I4) for x in ("GI", "GM", "N0")]
+                   + [(x, B, I4) for x in ("GI", "GM")]
                    + [(x, B, F4) for x in ("FQ", "ZF")]
                    + [(x, 128, BF) for x in ("ONE", "BO1", "BO", "IDN", "NID", "NBO", "U1", "UP", "NEG", "EI", "RL", "RG", "RG1", "S16")]):
-    SCRATCH[_n] = (PS if _n in ("bM", "bL", "bF", "bU", "bG") else SB, [128, _w], _d)
+    SCRATCH[_n] = (PS if _n in BANKS else SB, [128, _w], _d)
 LOADS = ["m0", "mc", "z0", "gl", "wt", "dv", "pr", "ad"]
-OUTS = ["ymc", "yz0", "yz1", "ym"]
+OUTS = ["ymc0", "ymc1", "ym"] + ["yz" + x[-2] for x in LAST + [y for y in ORDER if y[0] == "+"] if x.lstrip("+")[:3] == "sz:"]
 SEMAPHORES = ["V", "S", "T", "G"] + ["l_" + n for n in LOADS] + ["o_" + n for n in OUTS]
 for _t in range(T_STEPS):
     SCRATCH["Z%d" % _t] = (SB, [128, B], BF)
@@ -36,7 +41,7 @@ for _t in range(T_STEPS):
     if _t:
         SCRATCH["ZO%d" % _t] = (SB, [128, B], BF)
         SCRATCH["MO%d" % _t] = (SB, [128, 16], U2)
-        SEMAPHORES += ["%s%s%d%d" % (a, b, _t, q[0]) for a in "rs" for b in "mz" for q in SENDS]
+        SEMAPHORES += ["%s%s%d%s" % (a, q[0], _t, q[1]) for a in "rs" for q in SENDS]
 
 
 def rank_program(g, core, T, topo):
@@ -97,7 +102,7 @@ def rank_program(g, core, T, topo):
         mark((sem, 16), r, w, [])
 
     eng = lambda a, b: topo.engines(a, b)[:8]
-    N = lambda x, a, b: " ".join("%s_%d" % (x, q) for q in range(a, b))
+    N = lambda x, a, b: " ".join("%s_%d" % (y, q) for y in x.split() for q in range(a, b))
 
     def send(buf, t, a, b, c0, c1, src, r):
         rid, pid = topo.addr(nxt, core)
@@ -133,7 +138,7 @@ def rank_program(g, core, T, topo):
         op("S", lambda: S.activation(out, a, f, **kw), r, w, b)
 
     def aff(o, i, pat, cmp, fill, base, cm, r, w):
-        op("G", lambda: g.affine_select(o[:], i[:], pat, cmp, fill, base, cm), r, w)
+        op("G", lambda: g.affine_select(o, i, pat, cmp, fill, base, cm), r, w)
 
     def iota(o, pat, base, cm, w):
         op("G", lambda: g.iota(o, pat, base, cm, allow_small_or_imprecise_dtypes=True), "", w)
@@ -148,89 +153,98 @@ def rank_program(g, core, T, topo):
     dma("Y", T.M0[:], T.m0[:], "l_m0", "", "M0")
     dma("Y", T.W0[:, B:B + M], T.mc[:], "l_mc", "", "MC0")
     dma("S", T.ADW[:], T.ad[:], "l_ad", "", "ADW")
-    dma("S", T.GLW[:], T.gl[:], "l_gl", "", "GLW")
     dma("Y", T.PRW[:], T.pr[:], "l_pr", "", "PRW")
+    dma("Y", T.GLW[:], T.gl[:], "l_gl", "", "GLW")
     dma("Y", T.Z0[:], T.z0[:], "l_z0", "", N("Z0", 0, 4))
     dma("Y", T.WT[:], T.wt[:], "l_wt", "", "WT")
     dma("Y", T.DV[:], T.dv[:], "l_dv", "", "DV")
 
-    ms(T.LP[:], 0.0, "LP")
+    ms(T.LP[:, 0:2048], 0.0, "LP")
     ms(T.ONE[:], 1.0, "ONE")
     ms(T.E1[:], 0.0, "E1")
     ms(T.S16[:], 0.0625, "S16")
     ms(T.E1[:, 15::16], 1.0, "E1")
-    op("G", lambda: g.iota(T.WI[:], [[1, M]], 0, 0), "", "WI")
     op("G", lambda: g.iota(T.CI[:, 0:1], [[0, 1]], 0, 1), "", "pc")
-    aff(T.IDN, T.ONE, [[-1, 128]], A.is_equal, 0.0, 0, 1, "ONE", "IDN")
-    aff(T.E2, T.E1, [[-16, 9], [0, 16]], A.is_ge, 0.0, 0, 1, "E1", "E2")
-    aff(T.BO1, T.ONE, [[-16, 8], [0, 16]], A.is_ge, 0.0, 0, 1, "ONE", "BO1")
-    aff(T.E0, T.E2, [[16, 9], [0, 16]], A.is_ge, 0.0, 15, -1, "E2", "E0")
-    aff(T.BO, T.BO1, [[16, 8], [0, 16]], A.is_ge, 0.0, 15, -1, "BO1", "BO")
-    iota(T.IOT[:], [[16, 8]], 0, 0, "IOT")
-    act(T.D1[:, span(0, 2, 1, 2)], T.LP[:], F.Copy, "LP", N("d1z", 0, 2))
-    act(T.D1[:, span(2, 4, 1, 2)], T.LP[:], F.Copy, "LP", N("d1z", 2, 4))
+    iota(T.IOT[:], [[1, 16]], 0, 0, "IOT")
+    aff(T.IDN[:], T.ONE[:], [[-1, 128]], A.is_equal, 0.0, 0, 1, "ONE", "IDN")
+    aff(T.E2[:], T.E1[:], [[-16, 9], [0, 16]], A.is_ge, 0.0, 0, 1, "E1", "E2")
+    aff(T.BO1[:], T.ONE[:], [[-16, 8], [0, 16]], A.is_ge, 0.0, 0, 1, "ONE", "BO1")
+    aff(T.E0[:], T.E2[:], [[16, 9], [0, 16]], A.is_ge, 0.0, 15, -1, "E2", "E0")
+    aff(T.BO[:], T.BO1[:], [[16, 8], [0, 16]], A.is_ge, 0.0, 15, -1, "BO1", "BO")
+    act(T.D1[:, span(0, 2, 1, 2)], T.LP[:, 0:2048], F.Copy, "LP", N("d1z", 0, 2))
+    act(T.D1[:, span(2, 4, 1, 2)], T.LP[:, 0:2048], F.Copy, "LP", N("d1z", 2, 4))
     ms(T.D0[:, span(0, 2, 0, 2)], 0.0, N("d0z", 0, 2))
     ms(T.WS[:, 0:128], 1.0 / RATIO, "wsa")
     ms(cf(25), 2.0 ** 57, "big")
     ms(cf(26), 2.0 ** -57, "tiny")
     ms(T.D0[:, span(0, 2, 0, 32)], -512.0, N("d0z", 0, 2))
-    ts(T.WS[:, 128:256], T.E1[:, 15:143], -0.5, 0.5, A.mult, A.add, "E1", "wsb")
     ts(cf(23), cf(25), RATIO * 2.0 ** 56, None, A.mult, None, "big", "top")
     tc(T.ML0[:], T.M0[:], "M0", N("ML0", 0, 4))
 
     def const(i):
+        if i == 0:
+            iota(T.LP[:, 2048:3840], [[0, 1792]], 0, 0, "LP2")
         if i == 1:
             sc(T.WS[:, 256:384], T.WS[:, 0:128], T.LP[:, 0:128], cf(23), A.mult, A.add, "wsa LP top", "wsc")
-            sc(T.WS[:, 384:512], T.WS[:, 128:256], T.E1[:, 15:143], 0.0, A.mult, A.add, "wsb E1", "wsd")
             ts(T.CI[:, 1:2], T.CI[:, 0:1], 15, None, A.bitwise_and, None, "pc", "kc")
             tc(cf(3), T.CI[:, 0:1], "pc", "pf")
-            mm(T.bG[:, 0:1], T.WS[:, 256:384], T.IDN[:, 0:1], "wsc IDN", "d16", "bG")
-            mm(T.bG[:, 1:2], T.WS[:, 384:512], T.IDN[:, 0:1], "wsd IDN", "d16", "bG")
+            mm(T.bL[:, 64:65], T.WS[:, 256:384], T.IDN[:, 0:1], "wsc IDN", "as1", "bL")
             tc(cf(0), T.CI[:, 1:2], "kc", "kf")
-            tc(T.CF[:, 10:12], T.bG[:, 0:2], "d16", "wcol cb", "bG")
+            tc(cf(10), T.bL[:, 64:65], "as1", "wcol", "bL")
             for q in (2, 3):
                 iota(T.D0[:, span(q, q + 1, 0, 2)], [[0, 16 * QS_]], 0, 0, N("d0z", q, q + 1))
                 iota(T.D0[:, span(q, q + 1, 0, 32)], [[0, QS_]], -512, 0, N("d0z", q, q + 1))
                 if q == 2:
                     ts(T.NBO[:], T.BO[:], -1.0, None, A.mult, None, "BO", "NBO")
-                    aff(T.RG1, T.S16, [[0, 16], [-16, 8]], A.is_ge, 0.0, 0, 1, "S16", "RG1")
-                    aff(T.U1, T.NBO, [[-1, 128]], A.not_equal, 1.0, 0, 1, "NBO", "U1")
-                    aff(T.RG, T.RG1, [[0, 16], [16, 8]], A.is_ge, 0.0, 15, -1, "RG1", "RG")
-                    aff(T.UP, T.U1, [[-1, 128]], A.is_ge, 0.0, 0, 1, "U1", "UP")
-                    iota(T.SR1[:, 32:64], [[16, 32]], B, 0, "SR1b")
+                    aff(T.RG1[:], T.S16[:], [[0, 16], [-16, 8]], A.is_ge, 0.0, 0, 1, "S16", "RG1")
+                    aff(T.U1[:], T.NBO[:], [[-1, 128]], A.not_equal, 1.0, 0, 1, "NBO", "U1")
+                    aff(T.RG[:], T.RG1[:], [[0, 16], [16, 8]], A.is_ge, 0.0, 15, -1, "RG1", "RG")
+                    aff(T.UP[:], T.U1[:], [[-1, 128]], A.is_ge, 0.0, 0, 1, "U1", "UP")
+                    iota(T.SR1[:, 1::2], [[16, 32]], B, 0, "SR1b")
             iota(T.UT[:], [[1, W]], 32, 0, "UT")
         if i == 2:
             ts(T.EH[:], T.E0[:], 2.0, None, A.mult, None, "E0", "EH")
-            ts(T.EK[:], T.E0[:], -4096.0, None, A.mult, None, "E0", "EK")
-            ts(T.ER[:], T.E0[:], 4096.0, None, A.mult, None, "E0", "ER")
             tc(T.I16[:], T.IDN[:], "IDN", "I16")
-            ms(T.HB[0:64, :], 8192.0, "HB0")
-            ms(T.HB[64:128, :], (TH - 0.5) * 64.0 - 8192.0, "HB1")
+            ts(T.I2K[:], T.IDN[:], 2.0 ** 18, None, A.mult, None, "IDN", "I2K")
+            ts(T.EN[:], T.E0[:, 15:128:16], -1.0, None, A.mult, None, "E0", "EN")
+            ms(cf(20), TH - 0.5, "th")
         if i == 3:
-            ts(cf(15), cf(11), 0.5, -0.5, A.mult, A.add, "cb", "cb2")
-            ts(T.CB[:, 0:1], cf(0), 3.5, None, A.is_le, None, "kf", "le3")
-            ts(T.XQ[:], T.WI[:], cf(11), cf(15), A.mult, A.add, "WI cb cb2", "XQ")
-            ts(T.CB[:, 1:2], cf(0), 3.5, None, A.is_ge, None, "kf", "ge4")
-            ts(T.BIT[:], T.XQ[:], 1, None, A.bitwise_and, None, "XQ", "BIT")
-            ts(cf(12), cf(10), -4.0, None, A.mult, None, "wcol", "wbias")
-            ts(T.CT[:], T.BIT[:], 2.0, -1.0, A.mult, A.add, "BIT", "CT")
+            ts(T.SG[:, 0:16], T.IOT[:], cf(0), None, A.not_equal, None, "IOT kf", "sg0")
+            ms(T.CT[:, 0:1], -1.0, "CT")
+            ts(T.SG[:, 16:32], T.SG[:, 0:16], 2.0, -1.0, A.mult, A.add, "sg0", "sg")
+            fill = [lambda: ts(T.CB[:, 0:1], cf(0), 3.5, None, A.is_le, None, "kf", "le3"),
+                    lambda: ts(T.CB[:, 1:2], cf(0), 3.5, None, A.is_ge, None, "kf", "ge4"),
+                    lambda: ts(cf(12), cf(10), -4.0, None, A.mult, None, "wcol", "wbias"),
+                    lambda: ts(cf(24), cf(26), 2.0 ** -56, None, A.mult, None, "tiny", "eps"),
+                    lambda: ts(cf(16), cf(0), 37.0, -15.5 / 32, A.mult, A.add, "kf", "ck"),
+                    lambda: ts(cf(4), cf(3), 128.0, None, A.add, None, "pf", "pf1"),
+                    lambda: ts(cf(17), cf(0), 2.0, -1.0, A.mult, A.add, "kf", "cj"),
+                    lambda: ts(T.LF[:, 32:40], T.IOT[:, 0:8], 16.0, cf(0), A.mult, A.add, "IOT kf", "sl"),
+                    lambda: ts(T.SR2[:, 1::2], T.ONE[:, 0:32], cf(0), None, A.mult, None, "ONE kf", "SR2b")]
+            for j in range(9):
+                fill[j]()
+                ts(T.CT[:, 1 << j:2 << j], T.CT[:, 0:1 << j], T.SG[:, 16 + j:17 + j], None, A.mult, None, "CT sg", "CT")
         if i == 4:
             ts(T.NID[:], T.IDN[:], -1.0, None, A.mult, None, "IDN", "NID")
             ts(T.WE[:], T.E0[:], T.WT[:, 0:1], None, A.mult, None, "E0 WT", "WE")
             ms(cf(21), 0.5, "half")
             ms(T.NB[:, 0:1], 17.0 - 2 * QU, "nb0")
         if i == 5:
-            ts(cf(17), cf(0), 2.0, -1.0, A.mult, A.add, "kf", "cj")
-            ts(T.LF[:, 32:40], T.IOT[:], cf(0), None, A.add, None, "IOT kf", "sl")
             ts(T.NEG[:], T.BO[:], -0.03125, None, A.mult, None, "BO", "NEG")
             ts(T.WJ[:], T.E0[:], cf(17), None, A.mult, None, "E0 cj", "WJ")
             ts(T.B32[:], T.LF[:, 32:40], 32.0, None, A.mult, None, "sl", "B32")
-            ms(T.bL[:, 32:64], 0.0, N("any", 0, 4), "bL")
+            ts(T.LF[:, 40:48], T.LF[:, 32:40], 32.0, None, A.mult, None, "sl", "b32")
+            ms(T.AN[:], 0.0, N("any", 0, 4))
+            ms(cf(18), -2.0, "m2")
+            if [x for x in CMPV + CMPL if x[0] != x[1]]:
+                ts(T.CI[:, 2:3], T.CI[:, 0:1], 1, None, A.bitwise_and, None, "pc", "oc")
+                ts(cf(27), T.CI[:, 2:3], 16.0, 0.5, A.mult, A.add, "oc", "SV")
+                ts(cf(28), T.CI[:, 2:3], -16.0, 16.5, A.mult, A.add, "oc", "VS")
         if i == 6:
             for t in range(T_STEPS):
                 ts(T.DG[:, 128 * t:128 * t + 128], T.IDN[:], T.DV[:, t:t + 1], None, A.mult, None, "IDN DV", "DG%d" % t)
-            mm(T.bF[:], T.BO[:], T.DG[:], "BO DG0 DG1 DG2 DG3", "xl " + N("zz", 0, 4), "bF")
-            act(T.DT[:], T.bF[:], F.Copy, "xl", "DT", "bF")
+            mm(T.bF[:], T.BO[:], T.DG[:], "BO DG0 DG1 DG2 DG3", "xl0 xl1 " + N("zz", 0, 4), "bF")
+            act(T.DT[:], T.bF[:], F.Copy, "xl0", "DT", "bF")
         if i == 7:
             for j in range(8):
                 ts(T.RL[:, j::8], T.CT[:, 0:16], own(j), T.CB[:, 0:1], A.mult, A.mult, "CT E0 le3", "RL%d" % j)
@@ -238,115 +252,113 @@ def rank_program(g, core, T, topo):
             for j in range(8):
                 ts(T.RH[:, 32 * j:32 * j + 32], T.CT[:, 0::16], own(j), T.CB[:, 1:2], A.mult, A.mult, "CT E0 ge4", "RH%d" % j)
         if i == 9:
-            ts(cf(24), cf(26), 2.0 ** -56, None, A.mult, None, "tiny", "eps")
-            ts(cf(16), cf(0), 37.0, -15.5 / 32, A.mult, A.add, "kf", "ck")
-            ts(cf(4), cf(3), 128.0, None, A.add, None, "pf", "pf1")
             ms(cf(22), -11.0, "m11")
+            ms(cf(19), -255.0, "m255")
             ts(T.EI[:], T.IDN[:], cf(24), None, A.mult, None, "IDN eps", "EI")
-            ms(T.SR1[:, 0:32], 1.0, "SR1a")
-            ms(T.SR2[:, 0:32], 0.0, "SR2a")
-            ts(T.SR2[:, 32:64], T.ONE[:, 0:32], cf(0), None, A.mult, None, "ONE kf", "SR2b")
+            ms(T.SR1[:, 0::2], 1.0, "SR1a")
+            ms(T.SR2[:, 0::2], 0.0, "SR2a")
             ms(T.O32[:], 0.03125, "O32")
 
     def step(t):
         last = t == T_STEPS - 1
+        who = CMPL if last else CMPV
         Z, ML = T["Z%d" % t], T["ML%d" % t]
         Wc, Wn = T["W%d" % (t & 1)], T["W%d" % (1 - (t & 1))]
-        mc, nw, nb = "MC%d" % (t & 1), "NW%d" % (t & 1), "nb%d" % t
-        zn = lambda a, b: N("Z%d" % t, a, b)
-        mn = lambda a, b: N("ML%d" % t, a, b)
+        MO = T.LF if last else T["MO%d" % (t + 1)]
+        ZO = T.ZF if last else T["ZO%d" % (t + 1)]
+        mc, nw, nb, zn, mn = "MC%d" % (t & 1), "NW%d" % (t & 1), "nb%d" % t, "Z%d" % t, "ML%d" % t
         sl = lambda a, b, o=0: slice(o + QS_ * a, o + QS_ * b)
         lc = lambda a, b, o=0, k=1: slice(o + 4 * k * a, o + 4 * k * b)
-        p0 = lambda a, b: T[P0B][:, sl(a, b, B)]
+        xu = lambda a, b: slice(8 * a, 4 * (a + b))
+        xt = lambda a, b: slice(4 * (a + b), 8 * b)
+        kr = lambda a, b, i: T.KR[:, span(a, b, i, 32)]
+        bk = lambda a, h: CB[a][1 if who[a] == "VV" else h]
+        loaded, signed, sums = set(), set(), []
 
-        def kr(a, b, i):
-            return T.KR[:, span(a, b, i, 32)]
-
-        def o16(a, b):
-            tc(T.O16[:, sl(a, b)], Wc[:, B:B + M].indirect(ML[:, lc(a, b)]), mc + " " + mn(a, b), N("O16", a, b))
-
-        def gb(a, b):
-            act(T.GB[:, sl(a, b)], T.GLW[:].indirect(ML[:, lc(a, b)]), F.Copy, "GLW " + mn(a, b), N("GB", a, b))
-
-        def ad(a, b):
-            act(T.D0[:, span(a, b, 1, 2)], T.ADW[:].indirect(T.O16[:, sl(a, b)]), F.Copy, "ADW " + N("O16", a, b), N("d0a", a, b), scale=-1.0)
-
-        def pr(a, b):
-            act(T.D1[:, span(a, b, 0, 2)], T.PRW[:].indirect(T.O16[:, sl(a, b)]), F.Copy, "PRW " + N("O16", a, b), N("d1p", a, b))
-
-        def pv(a, b):
-            tc(T.D1[:, span(a, b, 0, 2)], T.PRW[:].indirect(T.O16[:, sl(a, b)]), "PRW " + N("O16", a, b), N("d1p", a, b))
-
-        def p0_(a, b):
-            mm(p0(a, b), T.IDN[:], T.D1[:, span(a, b, 0, 32)], "IDN " + N("d1p", a, b), N("P0", a, b), P0B)
-
-        def gw(a, b):
-            tc(T.D1[:, span(a, b, 32, 32)], T.GB[:, QS_ * a:QS_ * b - 1], N("GB", a, b), N("d1p", a, b))
+        def gather(kind, a, b):
+            lst, src = T.O16[:, 32 * a:32 * b], N("O16", a // 2, (b + 1) // 2)
+            if kind[0] == "a":
+                out, win, r, w = T.D0[:, 1024 * a + 1:1024 * b:2], T.ADW[:].indirect(lst), "ADW " + src, N("d0a", a, b)
+            else:
+                out, win, r, w = T.D1[:, 1024 * a:1024 * b:2], T.PRW[:].indirect(lst), "PRW " + src, N("d1p", a, b)
+            if kind == "ad":
+                act(out, win, F.Copy, r, w, scale=-1.0)
+            elif kind == "pr":
+                act(out, win, F.Copy, r, w)
+            elif kind == "av":
+                ts(out, win, -1.0, None, A.mult, None, r, w)
+            else:
+                tc(out, win, r, w)
 
         def scan(a, b):
             hi, lo = 32 * QS_ * b - 1, 32 * QS_ * a - 1 if a else None
             sc(T.KR[:, hi:lo:-1], T.D0[:, hi:lo:-1], T.D1[:, hi:lo:-1], T.GB[:, QS_ * b - 1:QS_ * b], A.add, A.max,
-               " ".join(N(x, a, b) for x in ("GB", "d0a", "d0z", "d1p", "d1z")), N("KR", a, b) + " " + N("K0", a, b))
+               N("GB d0z d1z", a, b) + " " + N("d0a d1p", 2 * a, 2 * b), N("KR K0", a, b))
 
-        def k0(a, b):
-            tt(kr(a, b, 0), p0(a, b), kr(a, b, 1), A.max, N("P0", a, b) + " " + N("KR", a, b), N("K0", a, b), P0B)
-
-        def zp(a, b):
-            bn = "bC%d" % (a & 1)
-            if CMPV[a] == "V":
-                for j in range(8):
-                    mm(T[bn][:, j::8], T.IDN[:], Z[:, sl(a, b)], "IDN " + zn(a, b), bn, bn)
+        def zp(a, b, h):
+            bn = bk(a, h)
+            for j in range(8):
+                if who[a][h] == "V":
+                    mm(T[bn][:, j::8], T.IDN[:], Z[:, sl(a, b)], "IDN " + N(zn, a, b), bn, bn)
+                else:
+                    mm(T[bn][:, j::8], T.IDN[:], Z[:, sl(a, b)], "IDN " + N(zn, a, b), bn, bn, j == 0, False)
+            loaded.add((a, h))
 
         def cmp_(a, b, h):
-            kn = N("KR", a, b) + ("" if h else " " + N("K0", a, b))
+            kn = N("KR" if h else "KR K0", a, b)
             c0 = 8 * B * h + 8 * QS_ * a
-            out, name = T.CMP[:, c0:c0 + 8 * QS_], "cmp%d%d" % (a, h)
-            if CMPV[a] == "V":
-                bn = "bC%d" % (a & 1)
+            out, name, bn = T.CMP[:, c0:c0 + 8 * QS_], "cmp%d%d" % (a, h), bk(a, h)
+            if who[a][h] == "V":
                 tt(out, T.KR[:, span(a, b, 2 * h, 4)], T[bn][:], A.is_le, kn + " " + bn, name, bn)
                 return
-            bn = "bC%d" % h
             for j in range(8):
-                mm(T[bn][:, j::8], T.NID[:], kr(a, b, 4 * j + 2 * h), "IDN NID %s %s" % (kn, zn(a, b)), bn, bn, True, False)
-                mm(T[bn][:, j::8], T.IDN[:], Z[:, sl(a, b)], "IDN " + zn(a, b), bn, bn, False, True)
+                if (a, h) in loaded:
+                    mm(T[bn][:, j::8], T.NID[:], kr(a, b, 4 * j + 2 * h), "NID %s %s" % (kn, "" if j else bn), bn, bn, False, j == 7)
+                else:
+                    mm(T[bn][:, j::8], T.NID[:], kr(a, b, 4 * j + 2 * h), "IDN NID %s %s" % (kn, N(zn, a, b)), bn, bn, True, False)
+                    mm(T[bn][:, j::8], T.IDN[:], Z[:, sl(a, b)], "IDN " + N(zn, a, b), bn, bn, False, True)
             act(out, T[bn][:], F.Sign, bn + " half", name, bn, bias=cf(21))
 
         def met(a, b):
             for i, k in enumerate(list(range(1, 16, 2)) + list(range(0, 16, 2))):
                 c0 = 8 * B * (k & 1) + 8 * QS_ * a
-                mm(T.bM[:, sl(a, b)], slot(T.E0 if CMPV[a] == "S" else T.EH, k), T.CMP[:, c0 + k // 2:c0 + 8 * QS_:8], "E0 EH cmp%d%d" % (a, k & 1), N("met", a, b), "bM",
-                   i == 0, i == 15)
+                mm(T.bM[:, sl(a, b)], slot(T.E0 if who[a][k & 1] == "S" else T.EH, k), T.CMP[:, c0 + k // 2:c0 + 8 * QS_:8], "E0 EH cmp%d%d" % (a, k & 1),
+                   N("met", a, b), "bM", i == 0, i == 15)
 
         def use(a, b):
             o, w = T.bU[:, sl(a, b)], N("use", a, b)
             for k in range(15, -1, -1):
                 up = kr(a, b, 2 * k + 2) if k < 15 else T.GB[:, sl(a, b)]
-                mm(o, slot(T.EK, k), up, "EK ER %s %s" % (N("GB", a, b), N("KR", a, b)), w, "bU", k == 15, False)
+                mm(o, slot(T.EK, k), up, "EK ER " + N("GB KR", a, b), w, "bU", k == 15, False)
                 mm(o, slot(T.ER, k), kr(a, b, 2 * k + 1), "ER " + N("KR", a, b), w, "bU", False, False)
             mm(o, T.ONE[:], T.HB[:], "ONE HB0 HB1", w, "bU", False, False)
             mm(o, T.I16[:], T.OF[:, sl(a, b)], "I16 " + N("OF", a, b), w, "bU", False, True)
 
+        def ut(a, b):
+            for k in range(15, -1, -1):
+                up = kr(a, b, 2 * k + 2) if k < 15 else T.GB[:, sl(a, b)]
+                o = T[UB][0:QS_ * (b - a), UC + k:UC + 128:16]
+                mm(o, up, T.E0[:, 15:128:16], "E0 EN " + N("GB KR", a, b), UN, UB, True, False)
+                mm(o, kr(a, b, 2 * k + 1), T.EN[:], "EN " + N("KR", a, b), UN, UB, False, True)
+
+        def uh(a, b):
+            o, w, k = T.bU[:, sl(a, b)], N("use", a, b), QS_ * (b - a)
+            mm(o, T.I16[:], T.OF[:, sl(a, b)], "LOW I2K I16 " + N("OF", a, b), w, "bU", True, False)
+            mm(o, T.LOW[0:k, :], T.I2K[0:k, 0:k], "LOW I2K", w, "bU", False, True)
+            signed.update(range(a, b))
+
         def ok(a, b):
-            ts(T.OK[:, sl(a, b)], T.bM[:, sl(a, b)], T.NB[:, t:t + 1], 0.5 if CMPV[a] == "S" else 16.5, A.add, A.is_ge, N("met", a, b) + " " + nb, N("OK", a, b), "bM")
+            c = {"SS": 0.5, "VV": 16.5, "SV": cf(27), "VS": cf(28)}[who[a]]
+            ts(T.OK[:, sl(a, b)], T.bM[:, sl(a, b)], T.NB[:, t:t + 1], c, A.add, A.is_ge,
+               "%s %s %s" % (N("met", a, b), nb, who[a] if who[a] in "SVS" else ""), N("OK", a, b), "bM")
 
         def first(a, b):
-            mm(T.bM[:, sl(a, b, B)], T.NEG[:], T.GREP[:, sl(a, b)], "NEG GREP UP " + N("OK", a, b), N("first", a, b), "bM", True, False)
+            mm(T.bM[:, sl(a, b, B)], T.NEG[:], T.GREP[:, sl(a, b)], "NEG UP " + N("OK GREP", a, b), N("first", a, b), "bM", True, False)
             mm(T.bM[:, sl(a, b, B)], T.UP[:], T.OK[:, sl(a, b)], "UP " + N("OK", a, b), N("first", a, b), "bM", False, True)
-
-        def oh(a, b):
-            ts(T.OH[:, sl(a, b)], T.bM[:, sl(a, b, B)], 1.0, None, A.is_ge, None, N("first", a, b), N("OH", a, b), "bM")
 
         def any_(a, b):
             for r in range(16):
                 mm(T.bL[:, 33 + 8 * a:32 + 8 * b:2], slot(T.E0, r), T.OH[:, QS_ * a + r:QS_ * b:16], "E0 " + N("OH", a, b), N("any", a, b), "bL", r == 0, r == 15)
-
-        def ms_(a, b):
-            sc(T.MN[:, lc(a, b, 0, 2)], T.bL[:, lc(a, b, 32, 2)], T.DM[:, lc(a, b, 0, 2)], 0.0, A.mult, A.add, "dm tof " + N("any", a, b), N("MN", a, b), "bL")
-
-        MO = T.LF if last else T["MO%d" % (t + 1)]
-
-        def mo(a, b):
-            tc(MO[:, lc(a, b)], T.MN[:, 8 * a + 1:8 * b:2], N("MN", a, b), N("MO", a, b))
 
         def sm(a, b):
             if not last:
@@ -356,118 +368,147 @@ def rank_program(g, core, T, topo):
 
         def vl(a, b):
             o = T.bL[:, lc(a, b, 16)]
-            mm(o, T.IDN[:], T.B32[:, 0:4 * (b - a)], "IDN B32 WJ " + N("OH", a, b), N("vl", a, b), "bL", True, False)
+            mm(o, T.IDN[:], T.B32[:, lc(a & 1, b - (a & 2))], "IDN B32 WJ " + N("OH", a, b), N("vl", a, b), "bL", True, False)
             for r in range(16):
                 mm(o, slot(T.WJ, r), T.OH[:, QS_ * a + r:QS_ * b:16], "WJ " + N("OH", a, b), N("vl", a, b), "bL", False, r == 15)
 
-        def ao(a, b):
-            ts(T.AOFF[:, lc(a, b)], T.bL[:, lc(a, b, 16)], 2.0, None, A.add, None, N("vl", a, b), N("AOFF", a, b), "bL")
-
-        def t1(a, b):
-            tt(T.T1[:, sl(a, b)], T.D0[:, span(a, b, 0, 1)].indirect(T.AOFF[:, lc(a, b)]), T.ZM[:, sl(a, b)], A.max,
-               " ".join(N(x, a, b) for x in ("AOFF", "d0a", "d0z")) + " ZM", N("T1", a, b))
-
         def zz(a, b):
             o, w = T.bF[:, sl(a, b)], N("zz", a, b)
-            mm(o, T.DT[:, 128 * t:128 * t + 128], T.OH[:, sl(a, b)], "DT NID IDN %s %s %s" % (N("OH", a, b), zn(a, b), N("T1", a, b)), w, "bF", True, False)
-            mm(o, T.NID[:], Z[:, sl(a, b)], "NID " + zn(a, b), w, "bF", False, False)
+            mm(o, T.DT[:, 128 * t:128 * t + 128], T.OH[:, sl(a, b)], "DT NID IDN " + N("OH T1 " + zn, a, b), w, "bF", True, False)
+            mm(o, T.NID[:], Z[:, sl(a, b)], "NID " + N(zn, a, b), w, "bF", False, False)
             mm(o, T.IDN[:], T.T1[:, sl(a, b)], "IDN " + N("T1", a, b), w, "bF", False, True)
-
-        def ab(a, b):
-            out = T.ZF if last else T["ZO%d" % (t + 1)]
-            act(out[:, sl(a, b)], T.bF[:, sl(a, b)], F.Abs, N("zz", a, b), N("ZO", a, b), "bF")
 
         def sz(a, b):
             if last:
-                dma("Y", T.yz[:, sl(a, b)], T.ZF[:, sl(a, b)], "o_yz%d" % (a // 2), N("ZO", a, b), "")
+                dma("Y", T.yz[:, sl(a, b)], ZO[:, sl(a, b)], "o_yz%d" % a, N("ZO", a, b), "")
             else:
-                send("Z", t + 1, a, b, QS_ * a, QS_ * b, T["ZO%d" % (t + 1)], N("ZO", a, b))
+                send("Z", t + 1, a, b, QS_ * a, QS_ * b, ZO, N("ZO", a, b))
 
         def n0(a, b):
-            tt(T.N0[:, sl(a, b)], T.bU[:, sl(a, b)], T.GM[:, sl(a, b)], A.min, "GM " + N("use", a, b), N("N0", a, b), "bU")
-
-        def nn(a, b):
-            ts(Wc[:, sl(a, b)], T.N0[:, sl(a, b)], W - 1, None, A.bitwise_and, None, N("N0", a, b), N(nw, a, b))
-
-        def of(a, b):
-            tc(T.OF[:, sl(a, b)], T.O16[:, sl(a, b)], N("O16", a, b), N("OF", a, b))
+            gn = "GI" if a in signed else "GM"
+            tt(Wc[:, sl(a, b)], T.bU[:, sl(a, b)], T[gn][:, sl(a, b)], A.min, N(gn + " use", a, b), N(nw, a, b), "bU")
+            if last:
+                ts(Wc[:, sl(a, b)], Wc[:, sl(a, b)], W - 1, None, A.bitwise_and, None, N(nw, a, b), N(nw, a, b))
 
         def xl(h):
-            s = " ".join("RL%d" % j for j in range(8))
-            mm(T.bF[:, B:B + 128], T.CD[:, 128 * h:128 * h + 128], T.RL[:], "CD GREP RG " + s, "xl", "bF", True, False)
-            mm(T.bF[:, B:B + 128], T.GREP[:, 128 * h:128 * h + 128], T.RG[:], "GREP RG", "xl", "bF", False, True)
+            s = " ".join("RL%d" % j for j in range(8)) + " RG " + N("CD GREP", 2 * h, 2 * h + 2)
+            mm(T.bF[:, B + h:2 * B:2], T.CD[:, 128 * h:128 * h + 128], T.RL[:], s, "xl%d" % h, "bF", True, False)
+            mm(T.bF[:, B + h:2 * B:2], T.GREP[:, 128 * h:128 * h + 128], T.RG[:], "RG", "xl%d" % h, "bF", False, True)
 
         def xh(h):
-            mm(T.bX[:, 8 * h:8 * h + 8, :], T.CD[:, 128 * h:128 * h + 128], T.RH[:], "CD " + " ".join("RH%d" % j for j in range(8)), "xh%d" % h, "bX")
+            s = " ".join("RH%d" % j for j in range(8)) + " " + N("CD", 2 * h, 2 * h + 2)
+            mm(T.bX[:, B * h:B * h + B], T.CD[:, 128 * h:128 * h + 128], T.RH[:], s, "bX" if h else "bX0", "bX")
 
-        def lw(h):
-            act(T.LP[:, LPC:LPC + 128], T.bF[:, B:B + 128], F.Relu, "xl wcol wbias", "LP", "bF", bias=cf(12), scale=cf(10))
+        def lw(a, b):
+            st = 1 if b - a == 4 else 2
+            hv = range(a // 2, b // 2)
+            act(T.LP[:, LPC + a // 2:LPC + B:st], T.bF[:, B + a // 2:2 * B:st], F.Relu, "wcol wbias " + " ".join("xl%d" % h for h in hv),
+                " ".join("LW%d" % h for h in hv) + ("" if t else " LP"), "bF", bias=cf(12), scale=cf(10))
 
-        def hh(h):
-            act(T.HH[:, :, 0:32], T.bX[:, 8 * h:8 * h + 8, :], F.Relu, "xh%d m11" % h, "HH", "bX", bias=cf(22))
+        def hh(a, b):
+            hv = range(a // 2, b // 2)
+            act(T.HH[:, B * a:B * b:2], T.bX[:, 128 * a:128 * b], F.Relu, "m11 " + " ".join("bX" if h else "bX0" for h in hv), " ".join("HH%d" % h for h in hv), "bX", bias=cf(22))
 
         def hs(h):
-            ts(T.HH[:, :, 32:64], T.HH[:, :, 0:32], cf(4 if h else 3), None, A.mult, None, "HH pf pf1", "HS")
+            ts(T.HH[:, 512 * h + 1:512 * h + 512:2], T.HH[:, 512 * h:512 * h + 512:2], cf(4 if h else 3), None, A.mult, None, "HH%d pf pf1" % h, "HS%d" % h)
+
+        def hc(h):
+            act(T.HH[:, 512 * h + 1:512 * h + 512:2], T.HH[:, 512 * h:512 * h + 512:2], F.Copy, "HH%d pf pf1" % h, "HS%d" % h, scale=cf(4 if h else 3))
 
         def tm(h):
-            o = T.bL[:, 128 + h:256:2]
-            mm(o, T.EI[:], T.SR1[:], "EI SR1a SR1b SR2a SR2b LP HH HS", "tm%d" % h, "bL", True, False)
+            o = T.bL[:, 128 + 64 * h:192 + 64 * h]
+            mm(o, T.EI[:], T.SR1[:], "EI SR1a SR1b SR2a SR2b LP2 LW{0} HH{0} HS{0}".format(h), "tm%d" % h, "bL", True, False)
             mm(o, T.EI[:], T.SR2[:], "SR2a SR2b", "tm%d" % h, "bL", False, False)
             for j in range(8):
-                mm(o, T.LP[:, LPC - 127 * j:LPC - 127 * j + 1017:8], T.HH[:, j, :], "LP HH HS", "tm%d" % h, "bL", False, j == 7)
+                c0 = LPC - 254 * j + h
+                mm(o, T.LP[:, c0:c0 + 2033:16], T.HH[:, 512 * h + 64 * j:512 * h + 64 * j + 64], "LW{0} HH{0} HS{0}".format(h), "tm%d" % h, "bL", False, j == 7)
 
-        def ul():
+        def ul(a, b):
             for r in range(16):
-                mm(T.bL[:, 0:16], slot(T.WE, r), Z[:, r::16], "WE " + zn(0, 4), "uL", "bL", r == 0, r == 15)
+                mm(T.bL[:, lc(a, b)], slot(T.WE, r), Z[:, QS_ * a + r:QS_ * b:16], "WE " + N(zn, a, b), N("uL", a, b), "bL", r == 0, r == 15)
 
-        def d16():
-            mm(T.bG[:, 0:B], T.IDN[:], Z[:], "IDN NID %s %s" % (zn(0, 4), N("GB", 0, 4)), "d16", "bG", True, False)
-            mm(T.bG[:, 0:B], T.NID[:], T.GB[:], "NID " + N("GB", 0, 4), "d16", "bG", False, True)
+        def d16(a, b):
+            mm(T.bU[:, sl(a, b, B)], T.IDN[:], Z[:, sl(a, b)], "IDN NID " + N("GB " + zn, a, b), N("d16", a, b), "bU", True, False)
+            mm(T.bU[:, sl(a, b, B)], T.NID[:], T.GB[:, sl(a, b)], "NID " + N("GB", a, b), N("d16", a, b), "bU", False, True)
+
+        def grep(a, b):
+            act(T.GREP[:, sl(a, b)], T.bU[:, sl(a, b, B)], F.Sign, N("d16", a, b) + " " + nb, N("GREP AC", a, b), "bU", bias=T.NB[:, t:t + 1], accum_out=T.AC[:, a:a + 1])
+            sums.append(a)
+
+        def asum():
+            for a in sums:
+                mm(T.bL[:, 64:65], T.O32[:], T.AC[:, a:a + 1], "O32 " + N("AC", 0, 4), "as1", "bL", a == sums[0], a == sums[-1])
 
         def mc_():
+            r = "OFF %s %s" % (mc, N(nw, 0, 4))
             if last:
-                tc(T.YM[:], Wc[:].indirect(T.OFF[:]), "OFF %s %s" % (mc, N(nw, 0, 4)), "YM")
-                dma("Y", T.ymc[:], T.YM[:], "o_ymc", "YM", "")
+                for h in range(2):
+                    tc(T.YM[:, B * h:B * h + B], Wc[:].indirect(T.OFF[:, 16 * h:16 * h + 16]), r, "YM%d" % h)
+                    dma("Y", T.ymc[:, B * h:B * h + B], T.YM[:, B * h:B * h + B], "o_ymc%d" % h, "YM%d" % h, "")
             else:
-                tc(Wn[:, B:B + M], Wc[:].indirect(T.OFF[:]), "OFF %s %s" % (mc, N(nw, 0, 4)), "MC%d" % (1 - (t & 1)))
+                ts(Wn[:, B:B + M], Wc[:].indirect(T.OFF[:]), W - 1, None, A.bitwise_and, None, r, "MC%d" % (1 - (t & 1)))
 
+        per = {
+            "o16": lambda a, b: tc(T.O16[:, sl(a, b)], Wc[:, B:B + M].indirect(ML[:, lc(a, b)]), mc + " " + N(mn, a, b), N("O16", a, b)),
+            "of": lambda a, b: tc(T.OF[:, sl(a, b)], T.O16[:, sl(a, b)], N("O16", a, b), N("OF", a, b)),
+            "og": lambda a, b: aff(T.OF[:, sl(a, b)], T.O16[:, sl(a, b)], [[0, QS_ * (b - a)]], A.is_ge, 0.0, 0, 0, N("O16", a, b), N("OF", a, b)),
+            "gb": lambda a, b: act(T.GB[:, sl(a, b)], T.GLW[:].indirect(ML[:, lc(a, b)]), F.Copy, "GLW " + N(mn, a, b), N("GB", a, b)),
+            "p0": lambda a, b: mm(T.bL[:, sl(a, b, B)], T.IDN[:], T.D1[:, span(a, b, 0, 32)], "IDN " + N("d1p", 2 * a, 2 * b), N("P0", a, b), "bL"),
+            "gw": lambda a, b: tc(T.D1[:, span(a, b, 32, 32)], T.GB[:, QS_ * a:QS_ * b - 1], N("GB", a, b), N("d1p", 2 * a, 2 * b)),
+            "gg": lambda a, b: aff(T.D1[:, span(a, b, 32, 32)], T.GB[:, QS_ * a:QS_ * b - 1], [[0, QS_ * (b - a) - 1]], A.is_ge, 0.0, 0, 0,
+                                   N("GB", a, b), N("d1p", 2 * a, 2 * b)),
+            "k0": lambda a, b: tt(kr(a, b, 0), T.bL[:, sl(a, b, B)], kr(a, b, 1), A.max, N("P0 KR", a, b), N("K0", a, b), "bL"),
+            "zh": lambda a, b: zp(a, b, 1), "zl": lambda a, b: zp(a, b, 0), "ch": lambda a, b: cmp_(a, b, 1), "cl": lambda a, b: cmp_(a, b, 0),
+            "oh": lambda a, b: ts(T.OH[:, sl(a, b)], T.bM[:, sl(a, b, B)], 1.0, None, A.is_ge, None, N("first", a, b), N("OH", a, b), "bM"),
+            "os": lambda a, b: act(T.OH[:, sl(a, b)], T.bM[:, sl(a, b, B)], F.Relu, "m2 " + N("first", a, b), N("OH", a, b), "bM", bias=cf(18), scale=2.0),
+            "ms": lambda a, b: sc(T.MN[:, lc(a, b, 0, 2)], T.bL[:, lc(a, b, 32, 2)], T.DM[:, lc(a, b, 0, 2)], 0.0, A.mult, A.add, N("dm tof any", a, b), N("MN", a, b), "bL"),
+            "mo": lambda a, b: tc(MO[:, lc(a, b)], T.MN[:, 8 * a + 1:8 * b:2], N("MN", a, b), N("MO", a, b)),
+            "ao": lambda a, b: ts(T.AOFF[:, lc(a, b)], T.bL[:, lc(a, b, 16)], 2.0, None, A.add, None, N("vl", a, b), N("AOFF", a, b), "bL"),
+            "t1": lambda a, b: tt(T.T1[:, sl(a, b)], T.D0[:, span(a & 2, b, 0, 1)].indirect(T.AOFF[:, lc(a, b)]), T.ZM[:, sl(a, b)], A.max,
+                                  "%s %s %s" % (N("AOFF ZM", a, b), N("d0z", a & 2, b), N("d0a", 2 * (a & 2), 2 * b)), N("T1", a, b)),
+            "an": lambda a, b: tt(T.AN[:, 8 * a + 1:8 * b:2], T.bL[:, lc(a, b, 16)], T.LF[:, lc(a & 1, b - (a & 2), 40)], A.not_equal, "b32 " + N("vl", a, b), N("any", a, b), "bL"),
+            "mt": lambda a, b: sc(T.MN[:, lc(a, b, 0, 2)], T.AN[:, lc(a, b, 0, 2)], T.DM[:, lc(a, b, 0, 2)], 0.0, A.mult, A.add, N("dm tof any", a, b), N("MN", a, b)),
+            "ab": lambda a, b: act(ZO[:, sl(a, b)], T.bF[:, sl(a, b)], F.Abs, N("zz", a, b), N("ZO", a, b), "bF"),
+            "m37": lambda a, b: ts(T.LF[:, lc(a, b, 16)], ML[:, lc(a, b)], 37.0, None, A.mult, None, N(mn, a, b), N("m37", a, b)),
+            "mi": lambda a, b: tc(T.LI[:, lc(a, b)], ML[:, lc(a, b)], N(mn, a, b), N("mI", a, b)),
+            "to0": lambda a, b: tt(T.LI[:, lc(a, b, 16)], T.bL[:, lc(a, b)], T.LF[:, lc(a, b, 16)], A.add, N("uL m37", a, b), N("to0", a, b), "bL"),
+            "ui": lambda a, b: tc(T.LI[:, lc(a, b, 32)], T.bL[:, lc(a, b)], N("uL", a, b), N("ui", a, b), "bL"),
+            "to": lambda a, b: ts(T.XI[:, xt(a, b)], T.LI[:, lc(a, b, 16)], M - 1, None, A.bitwise_and, None, N("to0", a, b), N("to", a, b)),
+            "u": lambda a, b: ts(T.XI[:, xu(a, b)], T.LI[:, lc(a, b, 32)], W - 1, None, A.bitwise_and, None, N("ui", a, b), N("u", a, b)),
+            "tof": lambda a, b: tc(T.DM[:, 8 * a + 1:8 * b:2], T.XI[:, xt(a, b)], N("to", a, b), N("tof", a, b)),
+            "xu": lambda a, b: tc(T.XU[:, 8 * a:8 * b], T.XI[:, 8 * a:8 * b], N("to u", a, b), N("XU", a, b)),
+            "dm": lambda a, b: tt(T.DM[:, 8 * a:8 * b:2], T.LI[:, lc(a, b)], T.XI[:, xt(a, b)], A.subtract, N("mI to", a, b), N("dm", a, b)),
+            "c16": lambda a, b: act(T.C16[:, sl(a, b)], T.bU[:, sl(a, b, B)], F.Sign, "half " + N("d16", a, b), N("C16", a, b), "bU", bias=cf(21)),
+            "gr": lambda a, b: mm(T.bU[:, sl(a, b, B)], T.BO[:], T.C16[:, sl(a, b)], "BO " + N("C16", a, b), N("d16", a, b), "bU"),
+            "code": lambda a, b: act(T.CD[:, sl(a, b)], T.CT[:].indirect(T.XU[:, xt(a, b)]), F.Copy, "CT " + N("XU", a, b), N("CD", a, b)),
+            "zm": lambda a, b: ts(T.ZM[:, sl(a, b)], Z[:, sl(a, b)], -255.0, None, A.add, None, N(zn, a, b), N("ZM", a, b)),
+            "zs": lambda a, b: act(T.ZM[:, sl(a, b)], Z[:, sl(a, b)], F.Identity, "m255 " + N(zn, a, b), N("ZM", a, b), bias=cf(19)),
+            "fq": lambda a, b: tt(T.FQ[:, sl(a, b)], T.UT[:].indirect(T.XU[:, xu(a, b)]), T.OF[:, sl(a, b)], A.mult, "UT " + N("XU OF", a, b), N("FQ", a, b)),
+            "g": lambda a, b: ts(T.GI[:, sl(a, b)], T.FQ[:, sl(a, b)], 0.03125, cf(16), A.mult, A.add, "ck " + N("FQ", a, b), N("GI", a, b)),
+            "gm": lambda a, b: ts(T.GM[:, sl(a, b)], T.GI[:, sl(a, b)], W - 1, None, A.bitwise_and, None, N("GI", a, b), N("GM", a, b)),
+            "lo": lambda a, b: act(T.LOW[0:QS_ * (b - a), :], T[UB][0:QS_ * (b - a), UC:UC + 128], F.Sign, UN + " th", "LOW", UB,
+                                   bias=T.CF[0:QS_ * (b - a), 20:21], scale=-1.0),
+            "ut": ut, "uh": uh, "scan": scan, "met": met, "use": use, "ok": ok, "first": first, "any": any_, "sm": sm, "vl": vl, "zz": zz, "sz": sz, "n0": n0,
+            "ul": ul, "d16": d16, "grep": grep, "lw": lw, "hh": hh}
         one = {
-            "m37": lambda: ts(T.LF[:, 16:32], ML[:], 37.0, None, A.mult, None, mn(0, 4), "m37"),
-            "mi": lambda: tc(T.LI[:, 0:16], ML[:], mn(0, 4), "mI"),
-            "to0": lambda: tt(T.LI[:, 16:32], T.bL[:, 0:16], T.LF[:, 16:32], A.add, "uL m37", "to0", "bL"),
-            "ui": lambda: tc(T.LI[:, 32:48], T.bL[:, 0:16], "uL", "ui", "bL"),
-            "to": lambda: ts(T.XI[:, 16:32], T.LI[:, 16:32], M - 1, None, A.bitwise_and, None, "to0", "to"),
-            "u": lambda: ts(T.XI[:, 0:16], T.LI[:, 32:48], W - 1, None, A.bitwise_and, None, "ui", "u"),
-            "tof": lambda: tc(T.DM[:, 1::2], T.XI[:, 16:32], "to", "tof"),
-            "xu": lambda: tc(T.XU[:], T.XI[:], "to u", "XU"),
-            "dm": lambda: tt(T.DM[:, 0::2], T.LI[:, 0:16], T.XI[:, 16:32], A.subtract, "mI to", "dm"),
-            "c16": lambda: act(T.C16[:], T.bG[:, 0:B], F.Sign, "d16 half", "C16", "bG", bias=cf(21)),
-            "gr": lambda: mm(T.bG[:, B:2 * B], T.BO[:], T.C16[:], "BO C16", "gR", "bG"),
-            "grep": lambda: act(T.GREP[:], T.bG[:, B:2 * B], F.Sign, "gR " + nb, "GREP AC", "bG", bias=T.NB[:, t:t + 1], accum_out=T.AC[:, t:t + 1]),
-            "code": lambda: act(T.CD[:], T.CT[:].indirect(T.XU[:, 16:32]), F.Copy, "CT XU", "CD"),
-            "zm": lambda: ts(T.ZM[:], Z[:], -255.0, None, A.add, None, zn(0, 4), "ZM"),
-            "fq": lambda: tt(T.FQ[:], T.UT[:].indirect(T.XU[:, 0:16]), T.OF[:], A.mult, "UT XU " + N("OF", 0, 4), "FQ"),
-            "g": lambda: ts(T.GI[:], T.FQ[:], 0.03125, cf(16), A.mult, A.add, "FQ ck", "GI"),
-            "gm": lambda: ts(T.GM[:], T.GI[:], W - 1, None, A.bitwise_and, None, "GI", "GM"),
-            "rec": lambda: op("V", lambda: V.reciprocal(T.RC[:], T.bL[:, 128:192]), "tm0 tm1", "RC", "bL"),
-            "rt": lambda: tt(T.RT[:], T.bL[:, 192:256], T.RC[:], A.mult, "tm0 tm1 RC", "RT", "bL"),
-            "rm": lambda: tt(T.LI[:, 48:80], T.RT[:, 0::2], T.RT[:, 1::2], A.min, "RT", "rm"),
+            "rec": lambda: op("V", lambda: V.reciprocal(T.RC[:], T.bL[:, 128:256:2]), "tm0 tm1", "RC", "bL"),
+            "rt": lambda: tt(T.RT[:], T.bL[:, 129:256:2], T.RC[:], A.mult, "tm0 tm1 RC", "RT", "bL"),
+            "rm": lambda: tt(T.LI[:, 48:80], T.RT[:, 0:32], T.RT[:, 32:64], A.min, "RT", "rm"),
             "off": lambda: tc(T.OFF[:], T.LI[:, 48:80], "rm", "OFF"),
-            "ul": ul, "d16": d16, "mc": mc_}
+            "mc": mc_}
         ahead = {
-            "as": lambda: mm(T.bG[:, 0:1], T.O32[:], T.AC[:, t:t + 1], "O32 AC", "d16", "bG"),
-            "ai": lambda: tc(T.AI[:, 0:1], T.bG[:, 0:1], "d16", "as2", "bG"),
+            "as": asum,
+            "ai": lambda: tc(T.AI[:, 0:1], T.bL[:, 64:65], "as1", "as2", "bL"),
             "ap": lambda: ts(T.AI[:, 1:2], T.AI[:, 0:1], 1, None, A.bitwise_and, None, "as2", "as3"),
             "nb": lambda: ts(T.NB[:, t + 1:t + 2], T.AI[:, 1:2], -2.0, 17.0 - 2 * QU, A.mult, A.add, "as3", "nb%d" % (t + 1))}
-        per = {"o16": o16, "gb": gb, "ad": ad, "pr": pr, "pv": pv, "p0": p0_, "gw": gw, "scan": scan, "k0": k0, "zp": zp, "met": met, "use": use, "ok": ok,
-               "ch": lambda a, b: cmp_(a, b, 1), "cl": lambda a, b: cmp_(a, b, 0), "mo": mo,
-               "first": first, "oh": oh, "any": any_, "ms": ms_, "sm": sm, "vl": vl, "ao": ao, "t1": t1, "zz": zz, "ab": ab, "sz": sz, "n0": n0, "nn": nn, "of": of}
-        half = {"xl": xl, "xh": xh, "lw": lw, "hh": hh, "hs": hs, "tm": tm}
+        half = {"xl": xl, "xh": xh, "hs": hs, "hc": hc, "tm": tm}
 
         def run(x):
             a, _, b = x.partition(":")
             if a in per:
-                per[a](int(b[0]), int(b[1]))
+                per[a](int(b[:1] or 0), int(b[1:] or 4))
+            elif a in ("ad", "pr", "av", "pv"):
+                gather(a, int(b[0]), int(b[1]))
             elif a in half:
                 half[a](int(b))
             elif a in one:
@@ -480,18 +521,15 @@ def rank_program(g, core, T, topo):
         return run
 
     runs = [step(t) for t in range(T_STEPS)]
-    for x in ORDER:
-        if x[0] == "+":
-            runs[0](x[1:])
-    for t in range(T_STEPS):
+    for x in FIRST:
+        runs[0](x)
+    for t in range(T_STEPS - 1):
         for x in ORDER:
-            if x[0] != "+":
-                runs[t](x)
-            elif t + 1 < T_STEPS:
-                runs[t + 1](x[1:])
+            runs[t + (x[0] == "+")](x.lstrip("+"))
+    for x in LAST:
+        runs[-1](x)
     need("G", [(s, cnt[s]) for s in ("V", "S", "T", "G")])
     need("G", [("l_" + x, 16) for x in LOADS] + [("o_" + x, 16) for x in OUTS])
     for t in range(1, T_STEPS):
         for q in SENDS:
-            for b in "mz":
-                need("G", [("r%s%d%d" % (b, t, q[0]), len(eng(prv, core))), ("s%s%d%d" % (b, t, q[0]), len(eng(core, nxt)))])
+            need("G", [("r%s%d%s" % (q[0], t, q[1]), len(eng(prv, core))), ("s%s%d%s" % (q[0], t, q[1]), len(eng(core, nxt)))])

from concourse.mybir import dt, AluOpType, AxisListType, ActivationFunctionType
A = AluOpType
F = ActivationFunctionType

T_STEPS, W, M, B, QU, TH = 4, 2048, 512, 256, 12, 254
QS_ = 64
RATIO = 3.2
LPC = 1792
CMPV = ["VV", "VV", "SS", "SS"]
CMPL = ["VV", "VV", "SS", "SS"]
CB = [["bC0", "bC0"], ["bC1", "bC1"], ["bC0", "bC1"], ["bG", "bX"]]
UB, UC, UN = "bU", 256, "d16_0 d16_1"
ORDER = ("hh p0:34 vl:02 ad:68 zh:34 tof scan:23 dm gg:34 lw an:02 k0:23 mt:02 ai mo:02 of:24 hs:0 ao:02 hc:1 scan:34 zl:34 ch:23 zs:04 cl:23 tm:0 tm:1 ut:24 sm:02 fq rec k0:34 met:23 lo:24 g rt uh:24 t1:02 ok:23 rm ch:34 first:23 n0:24 n0:02 oh:23 cl:34 zz:02 off ab:02 ap vl:23 mc +gb:02 an:23 +o16:12 mt:23 +o16:01 sz:02 met:34 mo:23 ok:34 +pv:01 +pr:24 first:34 oh:34 vl:34 +pv:12 +ad:02 ao:24 an:34 t1:24 mt:34 +p0:02 sm:23 mo:34 +gw:01 +of:02 sm:34 zz:24 +zh:12 ab:24 +scan:01 +zh:01 sz:24 +o16:23 +gg:12 +ad:24 +scan:12 +ch:01 +ut:02 +pr:46 +k0:02 nb +cl:01 +met:01 +cl:12 +m37 +mi +ch:12 +gb:24 +lo:02 +ad:46 +ul +to0 +d16 +ui +met:12 +to +u +c16 +xu +gr +o16:34 +p0:23 +gg:23 +zl:23 +code +ok:02 +grep +xh:1 +xh:0 +pv:67 +first:02 +xl:0 +oh:02 +pr:78 +as +xl:1 +uh:02 +zh:23").split()
LAST = "scan:23 zl:34 hh p0:34 vl:02 ad:68 zh:34 lw hc:1 tof hs:0 an:02 k0:23 of:24 gg:34 ch:23 cl:23 ao:02 scan:34 dm tm:0 zs tm:1 fq ut:24 met:23 lo:24 k0:34 rec g rt ch:34 ok:23 uh:24 first:23 t1:02 cl:34 mt:02 oh:23 vl:23 rm n0:02 off n0:24 met:34 ao:23 ok:34 t1:23 mc zz:02 first:34 os:34 ab:02 vl:34 ao:34 t1:34 an:24 mo:02 mt:24 zz:23 ab:23 mo:24 zz:34 sz:02 sz:23 ab:34 sm:34 sz:34".split()
FIRST = "#1 m37 zh:01 o16:04 #3 ad:02 pr:24 #5 gb:04 #2 #7 p0:12 #9 pv:02 #4 p0:01 ad:24 mi d16 c16 pr:46 ul gr zh:12 gw:01 gw:12 grep #8 #6 ad:46 to0 ui p0:23 scan:01 scan:12 ch:01 to k0:02 u gg:23 ch:12 cl:12 xu ut:02 lo:02 code as cl:01 pv:67 met:12 met:01 zl:23 ok:02 xh:0 xh:1 of:02 first:02 xl:0 oh:02 #0 pr:78 xl:1 zh:23 uh:02".split()
SENDS = [x.lstrip("+")[1] + x[-2] for x in ORDER if x.lstrip("+")[:3] in ("sm:", "sz:")]
SB, PS = "sbuf", "psum"
BF, F4, I4, U2, H2 = "bfloat16", "float32", "int32", "uint16", "float16"
BANKS = ("bM", "bL", "bF", "bU", "bG", "bX", "bC0", "bC1")
SCRATCH = {}
for _n, _w, _d in ([(x, 512, F4) for x in BANKS]
                   + [("PRW", W, BF), ("ADW", W, BF), ("GLW", M, BF), ("W0", M + B, I4), ("W1", M + B, I4), ("YM", M, F4), ("UT", W, F4),
                      ("CT", M, BF), ("LP", 3840, BF), ("RH", B, BF), ("HH", 1024, BF), ("CMP", 16 * B, BF),
                      ("M0", 16, I4), ("DV", 4, BF), ("WT", 1, BF), ("O16", B, U2), ("OF", B, H2), ("I16", 128, H2),
                      ("D0", 32 * B, BF), ("D1", 32 * B, BF), ("KR", 32 * B, BF),
                      ("AOFF", 16, U2), ("OFF", 32, U2), ("XU", 32, U2), ("XI", 32, I4), ("LI", 80, I4), ("LF", 48, F4), ("DM", 32, F4), ("MN", 32, F4), ("AN", 32, F4),
                      ("RC", 64, F4), ("RT", 64, F4), ("CI", 4, I4), ("CF", 32, F4), ("NB", 4, F4), ("AC", 4, F4), ("AI", 2, I4), ("DG", 512, BF), ("DT", 512, BF),
                      ("IOT", 16, F4), ("SG", 32, F4), ("WS", 512, BF), ("B32", 8, BF), ("EN", 8, BF), ("LOW", 128, BF), ("I2K", 128, BF), ("CB", 2, BF), ("SR1", 64, BF), ("SR2", 64, BF), ("HB", QS_, BF), ("O32", 128, F4)]
                   + [(x, 144, BF) for x in ("E1", "E2", "E0", "EH", "EK", "ER", "WE", "WJ")]
                   + [(x, B, BF) for x in ("GB", "C16", "CD", "GREP", "OK", "OH", "ZM", "T1")]
                   + [(x, B, I4) for x in ("GI", "GM")]
                   + [(x, B, F4) for x in ("FQ", "ZF")]
                   + [(x, 128, BF) for x in ("ONE", "BO1", "BO", "IDN", "NID", "NBO", "U1", "UP", "NEG", "EI", "RL", "RG", "RG1", "S16")]):
    SCRATCH[_n] = (PS if _n in BANKS else SB, [128, _w], _d)
LOADS = ["m0", "mc", "z0", "gl", "wt", "dv", "pr", "ad"]
OUTS = ["ymc0", "ymc1", "ym"] + ["yz" + x[-2] for x in LAST + [y for y in ORDER if y[0] == "+"] if x.lstrip("+")[:3] == "sz:"]
SEMAPHORES = ["V", "S", "T", "G"] + ["l_" + n for n in LOADS] + ["o_" + n for n in OUTS]
for _t in range(T_STEPS):
    SCRATCH["Z%d" % _t] = (SB, [128, B], BF)
    SCRATCH["ML%d" % _t] = (SB, [128, 16], U2)
    if _t:
        SCRATCH["ZO%d" % _t] = (SB, [128, B], BF)
        SCRATCH["MO%d" % _t] = (SB, [128, 16], U2)
        SEMAPHORES += ["%s%s%d%s" % (a, q[0], _t, q[1]) for a in "rs" for q in SENDS]


def rank_program(g, core, T, topo):
    rank = T.rank_of(core)
    if rank is None:
        return
    n = len(T.cores)
    nxt, prv = T.cores[(rank + 1) % n], T.cores[(rank - 1) % n]
    V, S, P = g.vector, g.scalar, g.tensor
    QS = {"V": V, "S": S, "T": P, "G": g, "Y": g.sync}
    cnt = {e: 0 for e in QS}
    clock = {e: {} for e in QS}
    snap = {}
    wrote, read, bank = {}, {}, {}

    def need(e, pairs):
        want = {}
        for s, v in pairs:
            want[s] = max(want.get(s, 0), v)
        for s, v in want.items():
            if clock[e].get(s, 0) < v:
                QS[e].wait_ge(T.sem[s], v)
                clock[e][s] = v
                for s2, v2 in snap.get((s, v), {}).items():
                    clock[e][s2] = max(clock[e].get(s2, 0), v2)

    def deps(e, r, w, b):
        p = [wrote[x] for x in r]
        for x in w:
            q = ([wrote[x]] if x in wrote else []) + list(read.get(x, {}).items())
            p += [y for y in q if not (e == "T" and y[0] == "T")]
        for x in b:
            p += [q for q in bank.get(x, {}).items() if q[0] != e]
        need(e, p)

    def mark(tag, r, w, b):
        for x in r:
            d = read.setdefault(x, {})
            d[tag[0]] = max(d.get(tag[0], 0), tag[1])
        for x in w:
            wrote[x] = tag
            read[x] = {}
        for x in b:
            bank.setdefault(x, {})[tag[0]] = tag[1]

    def op(e, fn, r="", w="", b=""):
        r, w, b = r.split(), w.split(), b.split()
        deps(e, r, w, b)
        cnt[e] += 1
        fn().then_inc(T.sem[e], 1)
        snap[(e, cnt[e])] = dict(clock[e])
        mark((e, cnt[e]), r, w, b)

    def dma(e, out, in_, sem, r="", w=""):
        r, w = r.split(), w.split()
        deps(e, r, w, [])
        QS[e].dma_start(out, in_).then_inc(T.sem[sem], 16)
        mark((sem, 16), r, w, [])

    eng = lambda a, b: topo.engines(a, b)[:8]
    N = lambda x, a, b: " ".join("%s_%d" % (y, q) for y in x.split() for q in range(a, b))

    def send(buf, t, a, b, c0, c1, src, r):
        rid, pid = topo.addr(nxt, core)
        deps("G", r.split(), [], [])
        k = ("m" if buf == "ML" else "z") + "%d%d" % (t, a)
        g.remote_dma(T[buf + str(t)][:, c0:c1], src[:, c0:c1], T.sem["r" + k], T.sem["s" + k], pid, rid, sum(1 << e for e in eng(core, nxt)))
        mark(("s" + k, len(eng(core, nxt))), r.split(), [], [])
        for x in N("%s%d" % (buf, t), a, b).split():
            wrote[x] = ("r" + k, len(eng(prv, core)))

    def mm(out, l, rr, r, w, b, st=True, sp=True):
        op("T", lambda: P.matmul(out, l, rr, st, sp), r, w, b)

    def tt(out, a, c, o, r, w, b=""):
        op("V", lambda: V.tensor_tensor(out, a, c, o), r, w, b)

    def ts(out, a, s1, s2, o1, o2, r, w, b=""):
        if o2 is None:
            op("V", lambda: V.tensor_scalar(out, a, s1, None, o1), r, w, b)
        else:
            op("V", lambda: V.tensor_scalar(out, a, s1, s2, o1, o2), r, w, b)

    def tc(out, a, r, w, b=""):
        op("V", lambda: V.tensor_copy(out, a), r, w, b)

    def ms(out, c, w, b=""):
        op("V", lambda: V.memset(out, c), "", w, b)

    def sc(out, a, c, init, o0, o1, r, w, b=""):
        op("V", lambda: V.tensor_tensor_scan(out, a, c, init, o0, o1), r, w, b)

    def act(out, a, f, r, w, b="", **kw):
        op("S", lambda: S.activation(out, a, f, **kw), r, w, b)

    def aff(o, i, pat, cmp, fill, base, cm, r, w):
        op("G", lambda: g.affine_select(o, i, pat, cmp, fill, base, cm), r, w)

    def iota(o, pat, base, cm, w):
        op("G", lambda: g.iota(o, pat, base, cm, allow_small_or_imprecise_dtypes=True), "", w)

    def slot(pad, k):
        return pad[:, 15 - k:143 - k]

    cf = lambda i: T.CF[:, i:i + 1]
    own = lambda j: T.E0[:, 15 + 16 * j:16 + 16 * j]
    span = lambda a, b, i, st: slice(32 * QS_ * a + i, 32 * QS_ * b, st)

    dma("Y", T.M0[:], T.m0[:], "l_m0", "", "M0")
    dma("Y", T.W0[:, B:B + M], T.mc[:], "l_mc", "", "MC0")
    dma("S", T.ADW[:], T.ad[:], "l_ad", "", "ADW")
    dma("Y", T.PRW[:], T.pr[:], "l_pr", "", "PRW")
    dma("Y", T.GLW[:], T.gl[:], "l_gl", "", "GLW")
    dma("Y", T.Z0[:], T.z0[:], "l_z0", "", N("Z0", 0, 4))
    dma("Y", T.WT[:], T.wt[:], "l_wt", "", "WT")
    dma("Y", T.DV[:], T.dv[:], "l_dv", "", "DV")

    ms(T.LP[:, 0:2048], 0.0, "LP")
    ms(T.ONE[:], 1.0, "ONE")
    ms(T.E1[:], 0.0, "E1")
    ms(T.S16[:], 0.0625, "S16")
    ms(T.E1[:, 15::16], 1.0, "E1")
    op("G", lambda: g.iota(T.CI[:, 0:1], [[0, 1]], 0, 1), "", "pc")
    iota(T.IOT[:], [[1, 16]], 0, 0, "IOT")
    aff(T.IDN[:], T.ONE[:], [[-1, 128]], A.is_equal, 0.0, 0, 1, "ONE", "IDN")
    aff(T.E2[:], T.E1[:], [[-16, 9], [0, 16]], A.is_ge, 0.0, 0, 1, "E1", "E2")
    aff(T.BO1[:], T.ONE[:], [[-16, 8], [0, 16]], A.is_ge, 0.0, 0, 1, "ONE", "BO1")
    aff(T.E0[:], T.E2[:], [[16, 9], [0, 16]], A.is_ge, 0.0, 15, -1, "E2", "E0")
    aff(T.BO[:], T.BO1[:], [[16, 8], [0, 16]], A.is_ge, 0.0, 15, -1, "BO1", "BO")
    act(T.D1[:, span(0, 2, 1, 2)], T.LP[:, 0:2048], F.Copy, "LP", N("d1z", 0, 2))
    act(T.D1[:, span(2, 4, 1, 2)], T.LP[:, 0:2048], F.Copy, "LP", N("d1z", 2, 4))
    ms(T.D0[:, span(0, 2, 0, 2)], 0.0, N("d0z", 0, 2))
    ms(T.WS[:, 0:128], 1.0 / RATIO, "wsa")
    ms(cf(25), 2.0 ** 57, "big")
    ms(cf(26), 2.0 ** -57, "tiny")
    ms(T.D0[:, span(0, 2, 0, 32)], -512.0, N("d0z", 0, 2))
    ts(cf(23), cf(25), RATIO * 2.0 ** 56, None, A.mult, None, "big", "top")
    tc(T.ML0[:], T.M0[:], "M0", N("ML0", 0, 4))

    def const(i):
        if i == 0:
            iota(T.LP[:, 2048:3840], [[0, 1792]], 0, 0, "LP2")
        if i == 1:
            sc(T.WS[:, 256:384], T.WS[:, 0:128], T.LP[:, 0:128], cf(23), A.mult, A.add, "wsa LP top", "wsc")
            ts(T.CI[:, 1:2], T.CI[:, 0:1], 15, None, A.bitwise_and, None, "pc", "kc")
            tc(cf(3), T.CI[:, 0:1], "pc", "pf")
            mm(T.bL[:, 64:65], T.WS[:, 256:384], T.IDN[:, 0:1], "wsc IDN", "as1", "bL")
            tc(cf(0), T.CI[:, 1:2], "kc", "kf")
            tc(cf(10), T.bL[:, 64:65], "as1", "wcol", "bL")
            for q in (2, 3):
                iota(T.D0[:, span(q, q + 1, 0, 2)], [[0, 16 * QS_]], 0, 0, N("d0z", q, q + 1))
                iota(T.D0[:, span(q, q + 1, 0, 32)], [[0, QS_]], -512, 0, N("d0z", q, q + 1))
                if q == 2:
                    ts(T.NBO[:], T.BO[:], -1.0, None, A.mult, None, "BO", "NBO")
                    aff(T.RG1[:], T.S16[:], [[0, 16], [-16, 8]], A.is_ge, 0.0, 0, 1, "S16", "RG1")
                    aff(T.U1[:], T.NBO[:], [[-1, 128]], A.not_equal, 1.0, 0, 1, "NBO", "U1")
                    aff(T.RG[:], T.RG1[:], [[0, 16], [16, 8]], A.is_ge, 0.0, 15, -1, "RG1", "RG")
                    aff(T.UP[:], T.U1[:], [[-1, 128]], A.is_ge, 0.0, 0, 1, "U1", "UP")
                    iota(T.SR1[:, 1::2], [[16, 32]], B, 0, "SR1b")
            iota(T.UT[:], [[1, W]], 32, 0, "UT")
        if i == 2:
            ts(T.EH[:], T.E0[:], 2.0, None, A.mult, None, "E0", "EH")
            tc(T.I16[:], T.IDN[:], "IDN", "I16")
            ts(T.I2K[:], T.IDN[:], 2.0 ** 18, None, A.mult, None, "IDN", "I2K")
            ts(T.EN[:], T.E0[:, 15:128:16], -1.0, None, A.mult, None, "E0", "EN")
            ms(cf(20), TH - 0.5, "th")
        if i == 3:
            ts(T.SG[:, 0:16], T.IOT[:], cf(0), None, A.not_equal, None, "IOT kf", "sg0")
            ms(T.CT[:, 0:1], -1.0, "CT")
            ts(T.SG[:, 16:32], T.SG[:, 0:16], 2.0, -1.0, A.mult, A.add, "sg0", "sg")
            fill = [lambda: ts(T.CB[:, 0:1], cf(0), 3.5, None, A.is_le, None, "kf", "le3"),
                    lambda: ts(T.CB[:, 1:2], cf(0), 3.5, None, A.is_ge, None, "kf", "ge4"),
                    lambda: ts(cf(12), cf(10), -4.0, None, A.mult, None, "wcol", "wbias"),
                    lambda: ts(cf(24), cf(26), 2.0 ** -56, None, A.mult, None, "tiny", "eps"),
                    lambda: ts(cf(16), cf(0), 37.0, -15.5 / 32, A.mult, A.add, "kf", "ck"),
                    lambda: ts(cf(4), cf(3), 128.0, None, A.add, None, "pf", "pf1"),
                    lambda: ts(cf(17), cf(0), 2.0, -1.0, A.mult, A.add, "kf", "cj"),
                    lambda: ts(T.LF[:, 32:40], T.IOT[:, 0:8], 16.0, cf(0), A.mult, A.add, "IOT kf", "sl"),
                    lambda: ts(T.SR2[:, 1::2], T.ONE[:, 0:32], cf(0), None, A.mult, None, "ONE kf", "SR2b")]
            for j in range(9):
                fill[j]()
                ts(T.CT[:, 1 << j:2 << j], T.CT[:, 0:1 << j], T.SG[:, 16 + j:17 + j], None, A.mult, None, "CT sg", "CT")
        if i == 4:
            ts(T.NID[:], T.IDN[:], -1.0, None, A.mult, None, "IDN", "NID")
            ts(T.WE[:], T.E0[:], T.WT[:, 0:1], None, A.mult, None, "E0 WT", "WE")
            ms(cf(21), 0.5, "half")
            ms(T.NB[:, 0:1], 17.0 - 2 * QU, "nb0")
        if i == 5:
            ts(T.NEG[:], T.BO[:], -0.03125, None, A.mult, None, "BO", "NEG")
            ts(T.WJ[:], T.E0[:], cf(17), None, A.mult, None, "E0 cj", "WJ")
            ts(T.B32[:], T.LF[:, 32:40], 32.0, None, A.mult, None, "sl", "B32")
            ts(T.LF[:, 40:48], T.LF[:, 32:40], 32.0, None, A.mult, None, "sl", "b32")
            ms(T.AN[:], 0.0, N("any", 0, 4))
            ms(cf(18), -2.0, "m2")
            if [x for x in CMPV + CMPL if x[0] != x[1]]:
                ts(T.CI[:, 2:3], T.CI[:, 0:1], 1, None, A.bitwise_and, None, "pc", "oc")
                ts(cf(27), T.CI[:, 2:3], 16.0, 0.5, A.mult, A.add, "oc", "SV")
                ts(cf(28), T.CI[:, 2:3], -16.0, 16.5, A.mult, A.add, "oc", "VS")
        if i == 6:
            for t in range(T_STEPS):
                ts(T.DG[:, 128 * t:128 * t + 128], T.IDN[:], T.DV[:, t:t + 1], None, A.mult, None, "IDN DV", "DG%d" % t)
            mm(T.bF[:], T.BO[:], T.DG[:], "BO DG0 DG1 DG2 DG3", "xl0 xl1 " + N("zz", 0, 4), "bF")
            act(T.DT[:], T.bF[:], F.Copy, "xl0", "DT", "bF")
        if i == 7:
            for j in range(8):
                ts(T.RL[:, j::8], T.CT[:, 0:16], own(j), T.CB[:, 0:1], A.mult, A.mult, "CT E0 le3", "RL%d" % j)
        if i == 8:
            for j in range(8):
                ts(T.RH[:, 32 * j:32 * j + 32], T.CT[:, 0::16], own(j), T.CB[:, 1:2], A.mult, A.mult, "CT E0 ge4", "RH%d" % j)
        if i == 9:
            ms(cf(22), -11.0, "m11")
            ms(cf(19), -255.0, "m255")
            ts(T.EI[:], T.IDN[:], cf(24), None, A.mult, None, "IDN eps", "EI")
            ms(T.SR1[:, 0::2], 1.0, "SR1a")
            ms(T.SR2[:, 0::2], 0.0, "SR2a")
            ms(T.O32[:], 0.03125, "O32")

    def step(t):
        last = t == T_STEPS - 1
        who = CMPL if last else CMPV
        Z, ML = T["Z%d" % t], T["ML%d" % t]
        Wc, Wn = T["W%d" % (t & 1)], T["W%d" % (1 - (t & 1))]
        MO = T.LF if last else T["MO%d" % (t + 1)]
        ZO = T.ZF if last else T["ZO%d" % (t + 1)]
        mc, nw, nb, zn, mn = "MC%d" % (t & 1), "NW%d" % (t & 1), "nb%d" % t, "Z%d" % t, "ML%d" % t
        sl = lambda a, b, o=0: slice(o + QS_ * a, o + QS_ * b)
        lc = lambda a, b, o=0, k=1: slice(o + 4 * k * a, o + 4 * k * b)
        xu = lambda a, b: slice(8 * a, 4 * (a + b))
        xt = lambda a, b: slice(4 * (a + b), 8 * b)
        kr = lambda a, b, i: T.KR[:, span(a, b, i, 32)]
        bk = lambda a, h: CB[a][1 if who[a] == "VV" else h]
        loaded, signed, sums = set(), set(), []

        def gather(kind, a, b):
            lst, src = T.O16[:, 32 * a:32 * b], N("O16", a // 2, (b + 1) // 2)
            if kind[0] == "a":
                out, win, r, w = T.D0[:, 1024 * a + 1:1024 * b:2], T.ADW[:].indirect(lst), "ADW " + src, N("d0a", a, b)
            else:
                out, win, r, w = T.D1[:, 1024 * a:1024 * b:2], T.PRW[:].indirect(lst), "PRW " + src, N("d1p", a, b)
            if kind == "ad":
                act(out, win, F.Copy, r, w, scale=-1.0)
            elif kind == "pr":
                act(out, win, F.Copy, r, w)
            elif kind == "av":
                ts(out, win, -1.0, None, A.mult, None, r, w)
            else:
                tc(out, win, r, w)

        def scan(a, b):
            hi, lo = 32 * QS_ * b - 1, 32 * QS_ * a - 1 if a else None
            sc(T.KR[:, hi:lo:-1], T.D0[:, hi:lo:-1], T.D1[:, hi:lo:-1], T.GB[:, QS_ * b - 1:QS_ * b], A.add, A.max,
               N("GB d0z d1z", a, b) + " " + N("d0a d1p", 2 * a, 2 * b), N("KR K0", a, b))

        def zp(a, b, h):
            bn = bk(a, h)
            for j in range(8):
                if who[a][h] == "V":
                    mm(T[bn][:, j::8], T.IDN[:], Z[:, sl(a, b)], "IDN " + N(zn, a, b), bn, bn)
                else:
                    mm(T[bn][:, j::8], T.IDN[:], Z[:, sl(a, b)], "IDN " + N(zn, a, b), bn, bn, j == 0, False)
            loaded.add((a, h))

        def cmp_(a, b, h):
            kn = N("KR" if h else "KR K0", a, b)
            c0 = 8 * B * h + 8 * QS_ * a
            out, name, bn = T.CMP[:, c0:c0 + 8 * QS_], "cmp%d%d" % (a, h), bk(a, h)
            if who[a][h] == "V":
                tt(out, T.KR[:, span(a, b, 2 * h, 4)], T[bn][:], A.is_le, kn + " " + bn, name, bn)
                return
            for j in range(8):
                if (a, h) in loaded:
                    mm(T[bn][:, j::8], T.NID[:], kr(a, b, 4 * j + 2 * h), "NID %s %s" % (kn, "" if j else bn), bn, bn, False, j == 7)
                else:
                    mm(T[bn][:, j::8], T.NID[:], kr(a, b, 4 * j + 2 * h), "IDN NID %s %s" % (kn, N(zn, a, b)), bn, bn, True, False)
                    mm(T[bn][:, j::8], T.IDN[:], Z[:, sl(a, b)], "IDN " + N(zn, a, b), bn, bn, False, True)
            act(out, T[bn][:], F.Sign, bn + " half", name, bn, bias=cf(21))

        def met(a, b):
            for i, k in enumerate(list(range(1, 16, 2)) + list(range(0, 16, 2))):
                c0 = 8 * B * (k & 1) + 8 * QS_ * a
                mm(T.bM[:, sl(a, b)], slot(T.E0 if who[a][k & 1] == "S" else T.EH, k), T.CMP[:, c0 + k // 2:c0 + 8 * QS_:8], "E0 EH cmp%d%d" % (a, k & 1),
                   N("met", a, b), "bM", i == 0, i == 15)

        def use(a, b):
            o, w = T.bU[:, sl(a, b)], N("use", a, b)
            for k in range(15, -1, -1):
                up = kr(a, b, 2 * k + 2) if k < 15 else T.GB[:, sl(a, b)]
                mm(o, slot(T.EK, k), up, "EK ER " + N("GB KR", a, b), w, "bU", k == 15, False)
                mm(o, slot(T.ER, k), kr(a, b, 2 * k + 1), "ER " + N("KR", a, b), w, "bU", False, False)
            mm(o, T.ONE[:], T.HB[:], "ONE HB0 HB1", w, "bU", False, False)
            mm(o, T.I16[:], T.OF[:, sl(a, b)], "I16 " + N("OF", a, b), w, "bU", False, True)

        def ut(a, b):
            for k in range(15, -1, -1):
                up = kr(a, b, 2 * k + 2) if k < 15 else T.GB[:, sl(a, b)]
                o = T[UB][0:QS_ * (b - a), UC + k:UC + 128:16]
                mm(o, up, T.E0[:, 15:128:16], "E0 EN " + N("GB KR", a, b), UN, UB, True, False)
                mm(o, kr(a, b, 2 * k + 1), T.EN[:], "EN " + N("KR", a, b), UN, UB, False, True)

        def uh(a, b):
            o, w, k = T.bU[:, sl(a, b)], N("use", a, b), QS_ * (b - a)
            mm(o, T.I16[:], T.OF[:, sl(a, b)], "LOW I2K I16 " + N("OF", a, b), w, "bU", True, False)
            mm(o, T.LOW[0:k, :], T.I2K[0:k, 0:k], "LOW I2K", w, "bU", False, True)
            signed.update(range(a, b))

        def ok(a, b):
            c = {"SS": 0.5, "VV": 16.5, "SV": cf(27), "VS": cf(28)}[who[a]]
            ts(T.OK[:, sl(a, b)], T.bM[:, sl(a, b)], T.NB[:, t:t + 1], c, A.add, A.is_ge,
               "%s %s %s" % (N("met", a, b), nb, who[a] if who[a] in "SVS" else ""), N("OK", a, b), "bM")

        def first(a, b):
            mm(T.bM[:, sl(a, b, B)], T.NEG[:], T.GREP[:, sl(a, b)], "NEG UP " + N("OK GREP", a, b), N("first", a, b), "bM", True, False)
            mm(T.bM[:, sl(a, b, B)], T.UP[:], T.OK[:, sl(a, b)], "UP " + N("OK", a, b), N("first", a, b), "bM", False, True)

        def any_(a, b):
            for r in range(16):
                mm(T.bL[:, 33 + 8 * a:32 + 8 * b:2], slot(T.E0, r), T.OH[:, QS_ * a + r:QS_ * b:16], "E0 " + N("OH", a, b), N("any", a, b), "bL", r == 0, r == 15)

        def sm(a, b):
            if not last:
                send("ML", t + 1, a, b, 4 * a, 4 * b, MO, N("MO", a, b))
            elif b == 4:
                dma("Y", T.ym[:], MO[:, 0:16], "o_ym", N("MO", 0, 4), "")

        def vl(a, b):
            o = T.bL[:, lc(a, b, 16)]
            mm(o, T.IDN[:], T.B32[:, lc(a & 1, b - (a & 2))], "IDN B32 WJ " + N("OH", a, b), N("vl", a, b), "bL", True, False)
            for r in range(16):
                mm(o, slot(T.WJ, r), T.OH[:, QS_ * a + r:QS_ * b:16], "WJ " + N("OH", a, b), N("vl", a, b), "bL", False, r == 15)

        def zz(a, b):
            o, w = T.bF[:, sl(a, b)], N("zz", a, b)
            mm(o, T.DT[:, 128 * t:128 * t + 128], T.OH[:, sl(a, b)], "DT NID IDN " + N("OH T1 " + zn, a, b), w, "bF", True, False)
            mm(o, T.NID[:], Z[:, sl(a, b)], "NID " + N(zn, a, b), w, "bF", False, False)
            mm(o, T.IDN[:], T.T1[:, sl(a, b)], "IDN " + N("T1", a, b), w, "bF", False, True)

        def sz(a, b):
            if last:
                dma("Y", T.yz[:, sl(a, b)], ZO[:, sl(a, b)], "o_yz%d" % a, N("ZO", a, b), "")
            else:
                send("Z", t + 1, a, b, QS_ * a, QS_ * b, ZO, N("ZO", a, b))

        def n0(a, b):
            gn = "GI" if a in signed else "GM"
            tt(Wc[:, sl(a, b)], T.bU[:, sl(a, b)], T[gn][:, sl(a, b)], A.min, N(gn + " use", a, b), N(nw, a, b), "bU")
            if last:
                ts(Wc[:, sl(a, b)], Wc[:, sl(a, b)], W - 1, None, A.bitwise_and, None, N(nw, a, b), N(nw, a, b))

        def xl(h):
            s = " ".join("RL%d" % j for j in range(8)) + " RG " + N("CD GREP", 2 * h, 2 * h + 2)
            mm(T.bF[:, B + h:2 * B:2], T.CD[:, 128 * h:128 * h + 128], T.RL[:], s, "xl%d" % h, "bF", True, False)
            mm(T.bF[:, B + h:2 * B:2], T.GREP[:, 128 * h:128 * h + 128], T.RG[:], "RG", "xl%d" % h, "bF", False, True)

        def xh(h):
            s = " ".join("RH%d" % j for j in range(8)) + " " + N("CD", 2 * h, 2 * h + 2)
            mm(T.bX[:, B * h:B * h + B], T.CD[:, 128 * h:128 * h + 128], T.RH[:], s, "bX" if h else "bX0", "bX")

        def lw(a, b):
            st = 1 if b - a == 4 else 2
            hv = range(a // 2, b // 2)
            act(T.LP[:, LPC + a // 2:LPC + B:st], T.bF[:, B + a // 2:2 * B:st], F.Relu, "wcol wbias " + " ".join("xl%d" % h for h in hv),
                " ".join("LW%d" % h for h in hv) + ("" if t else " LP"), "bF", bias=cf(12), scale=cf(10))

        def hh(a, b):
            hv = range(a // 2, b // 2)
            act(T.HH[:, B * a:B * b:2], T.bX[:, 128 * a:128 * b], F.Relu, "m11 " + " ".join("bX" if h else "bX0" for h in hv), " ".join("HH%d" % h for h in hv), "bX", bias=cf(22))

        def hs(h):
            ts(T.HH[:, 512 * h + 1:512 * h + 512:2], T.HH[:, 512 * h:512 * h + 512:2], cf(4 if h else 3), None, A.mult, None, "HH%d pf pf1" % h, "HS%d" % h)

        def hc(h):
            act(T.HH[:, 512 * h + 1:512 * h + 512:2], T.HH[:, 512 * h:512 * h + 512:2], F.Copy, "HH%d pf pf1" % h, "HS%d" % h, scale=cf(4 if h else 3))

        def tm(h):
            o = T.bL[:, 128 + 64 * h:192 + 64 * h]
            mm(o, T.EI[:], T.SR1[:], "EI SR1a SR1b SR2a SR2b LP2 LW{0} HH{0} HS{0}".format(h), "tm%d" % h, "bL", True, False)
            mm(o, T.EI[:], T.SR2[:], "SR2a SR2b", "tm%d" % h, "bL", False, False)
            for j in range(8):
                c0 = LPC - 254 * j + h
                mm(o, T.LP[:, c0:c0 + 2033:16], T.HH[:, 512 * h + 64 * j:512 * h + 64 * j + 64], "LW{0} HH{0} HS{0}".format(h), "tm%d" % h, "bL", False, j == 7)

        def ul(a, b):
            for r in range(16):
                mm(T.bL[:, lc(a, b)], slot(T.WE, r), Z[:, QS_ * a + r:QS_ * b:16], "WE " + N(zn, a, b), N("uL", a, b), "bL", r == 0, r == 15)

        def d16(a, b):
            mm(T.bU[:, sl(a, b, B)], T.IDN[:], Z[:, sl(a, b)], "IDN NID " + N("GB " + zn, a, b), N("d16", a, b), "bU", True, False)
            mm(T.bU[:, sl(a, b, B)], T.NID[:], T.GB[:, sl(a, b)], "NID " + N("GB", a, b), N("d16", a, b), "bU", False, True)

        def grep(a, b):
            act(T.GREP[:, sl(a, b)], T.bU[:, sl(a, b, B)], F.Sign, N("d16", a, b) + " " + nb, N("GREP AC", a, b), "bU", bias=T.NB[:, t:t + 1], accum_out=T.AC[:, a:a + 1])
            sums.append(a)

        def asum():
            for a in sums:
                mm(T.bL[:, 64:65], T.O32[:], T.AC[:, a:a + 1], "O32 " + N("AC", 0, 4), "as1", "bL", a == sums[0], a == sums[-1])

        def mc_():
            r = "OFF %s %s" % (mc, N(nw, 0, 4))
            if last:
                for h in range(2):
                    tc(T.YM[:, B * h:B * h + B], Wc[:].indirect(T.OFF[:, 16 * h:16 * h + 16]), r, "YM%d" % h)
                    dma("Y", T.ymc[:, B * h:B * h + B], T.YM[:, B * h:B * h + B], "o_ymc%d" % h, "YM%d" % h, "")
            else:
                ts(Wn[:, B:B + M], Wc[:].indirect(T.OFF[:]), W - 1, None, A.bitwise_and, None, r, "MC%d" % (1 - (t & 1)))

        per = {
            "o16": lambda a, b: tc(T.O16[:, sl(a, b)], Wc[:, B:B + M].indirect(ML[:, lc(a, b)]), mc + " " + N(mn, a, b), N("O16", a, b)),
            "of": lambda a, b: tc(T.OF[:, sl(a, b)], T.O16[:, sl(a, b)], N("O16", a, b), N("OF", a, b)),
            "og": lambda a, b: aff(T.OF[:, sl(a, b)], T.O16[:, sl(a, b)], [[0, QS_ * (b - a)]], A.is_ge, 0.0, 0, 0, N("O16", a, b), N("OF", a, b)),
            "gb": lambda a, b: act(T.GB[:, sl(a, b)], T.GLW[:].indirect(ML[:, lc(a, b)]), F.Copy, "GLW " + N(mn, a, b), N("GB", a, b)),
            "p0": lambda a, b: mm(T.bL[:, sl(a, b, B)], T.IDN[:], T.D1[:, span(a, b, 0, 32)], "IDN " + N("d1p", 2 * a, 2 * b), N("P0", a, b), "bL"),
            "gw": lambda a, b: tc(T.D1[:, span(a, b, 32, 32)], T.GB[:, QS_ * a:QS_ * b - 1], N("GB", a, b), N("d1p", 2 * a, 2 * b)),
            "gg": lambda a, b: aff(T.D1[:, span(a, b, 32, 32)], T.GB[:, QS_ * a:QS_ * b - 1], [[0, QS_ * (b - a) - 1]], A.is_ge, 0.0, 0, 0,
                                   N("GB", a, b), N("d1p", 2 * a, 2 * b)),
            "k0": lambda a, b: tt(kr(a, b, 0), T.bL[:, sl(a, b, B)], kr(a, b, 1), A.max, N("P0 KR", a, b), N("K0", a, b), "bL"),
            "zh": lambda a, b: zp(a, b, 1), "zl": lambda a, b: zp(a, b, 0), "ch": lambda a, b: cmp_(a, b, 1), "cl": lambda a, b: cmp_(a, b, 0),
            "oh": lambda a, b: ts(T.OH[:, sl(a, b)], T.bM[:, sl(a, b, B)], 1.0, None, A.is_ge, None, N("first", a, b), N("OH", a, b), "bM"),
            "os": lambda a, b: act(T.OH[:, sl(a, b)], T.bM[:, sl(a, b, B)], F.Relu, "m2 " + N("first", a, b), N("OH", a, b), "bM", bias=cf(18), scale=2.0),
            "ms": lambda a, b: sc(T.MN[:, lc(a, b, 0, 2)], T.bL[:, lc(a, b, 32, 2)], T.DM[:, lc(a, b, 0, 2)], 0.0, A.mult, A.add, N("dm tof any", a, b), N("MN", a, b), "bL"),
            "mo": lambda a, b: tc(MO[:, lc(a, b)], T.MN[:, 8 * a + 1:8 * b:2], N("MN", a, b), N("MO", a, b)),
            "ao": lambda a, b: ts(T.AOFF[:, lc(a, b)], T.bL[:, lc(a, b, 16)], 2.0, None, A.add, None, N("vl", a, b), N("AOFF", a, b), "bL"),
            "t1": lambda a, b: tt(T.T1[:, sl(a, b)], T.D0[:, span(a & 2, b, 0, 1)].indirect(T.AOFF[:, lc(a, b)]), T.ZM[:, sl(a, b)], A.max,
                                  "%s %s %s" % (N("AOFF ZM", a, b), N("d0z", a & 2, b), N("d0a", 2 * (a & 2), 2 * b)), N("T1", a, b)),
            "an": lambda a, b: tt(T.AN[:, 8 * a + 1:8 * b:2], T.bL[:, lc(a, b, 16)], T.LF[:, lc(a & 1, b - (a & 2), 40)], A.not_equal, "b32 " + N("vl", a, b), N("any", a, b), "bL"),
            "mt": lambda a, b: sc(T.MN[:, lc(a, b, 0, 2)], T.AN[:, lc(a, b, 0, 2)], T.DM[:, lc(a, b, 0, 2)], 0.0, A.mult, A.add, N("dm tof any", a, b), N("MN", a, b)),
            "ab": lambda a, b: act(ZO[:, sl(a, b)], T.bF[:, sl(a, b)], F.Abs, N("zz", a, b), N("ZO", a, b), "bF"),
            "m37": lambda a, b: ts(T.LF[:, lc(a, b, 16)], ML[:, lc(a, b)], 37.0, None, A.mult, None, N(mn, a, b), N("m37", a, b)),
            "mi": lambda a, b: tc(T.LI[:, lc(a, b)], ML[:, lc(a, b)], N(mn, a, b), N("mI", a, b)),
            "to0": lambda a, b: tt(T.LI[:, lc(a, b, 16)], T.bL[:, lc(a, b)], T.LF[:, lc(a, b, 16)], A.add, N("uL m37", a, b), N("to0", a, b), "bL"),
            "ui": lambda a, b: tc(T.LI[:, lc(a, b, 32)], T.bL[:, lc(a, b)], N("uL", a, b), N("ui", a, b), "bL"),
            "to": lambda a, b: ts(T.XI[:, xt(a, b)], T.LI[:, lc(a, b, 16)], M - 1, None, A.bitwise_and, None, N("to0", a, b), N("to", a, b)),
            "u": lambda a, b: ts(T.XI[:, xu(a, b)], T.LI[:, lc(a, b, 32)], W - 1, None, A.bitwise_and, None, N("ui", a, b), N("u", a, b)),
            "tof": lambda a, b: tc(T.DM[:, 8 * a + 1:8 * b:2], T.XI[:, xt(a, b)], N("to", a, b), N("tof", a, b)),
            "xu": lambda a, b: tc(T.XU[:, 8 * a:8 * b], T.XI[:, 8 * a:8 * b], N("to u", a, b), N("XU", a, b)),
            "dm": lambda a, b: tt(T.DM[:, 8 * a:8 * b:2], T.LI[:, lc(a, b)], T.XI[:, xt(a, b)], A.subtract, N("mI to", a, b), N("dm", a, b)),
            "c16": lambda a, b: act(T.C16[:, sl(a, b)], T.bU[:, sl(a, b, B)], F.Sign, "half " + N("d16", a, b), N("C16", a, b), "bU", bias=cf(21)),
            "gr": lambda a, b: mm(T.bU[:, sl(a, b, B)], T.BO[:], T.C16[:, sl(a, b)], "BO " + N("C16", a, b), N("d16", a, b), "bU"),
            "code": lambda a, b: act(T.CD[:, sl(a, b)], T.CT[:].indirect(T.XU[:, xt(a, b)]), F.Copy, "CT " + N("XU", a, b), N("CD", a, b)),
            "zm": lambda a, b: ts(T.ZM[:, sl(a, b)], Z[:, sl(a, b)], -255.0, None, A.add, None, N(zn, a, b), N("ZM", a, b)),
            "zs": lambda a, b: act(T.ZM[:, sl(a, b)], Z[:, sl(a, b)], F.Identity, "m255 " + N(zn, a, b), N("ZM", a, b), bias=cf(19)),
            "fq": lambda a, b: tt(T.FQ[:, sl(a, b)], T.UT[:].indirect(T.XU[:, xu(a, b)]), T.OF[:, sl(a, b)], A.mult, "UT " + N("XU OF", a, b), N("FQ", a, b)),
            "g": lambda a, b: ts(T.GI[:, sl(a, b)], T.FQ[:, sl(a, b)], 0.03125, cf(16), A.mult, A.add, "ck " + N("FQ", a, b), N("GI", a, b)),
            "gm": lambda a, b: ts(T.GM[:, sl(a, b)], T.GI[:, sl(a, b)], W - 1, None, A.bitwise_and, None, N("GI", a, b), N("GM", a, b)),
            "lo": lambda a, b: act(T.LOW[0:QS_ * (b - a), :], T[UB][0:QS_ * (b - a), UC:UC + 128], F.Sign, UN + " th", "LOW", UB,
                                   bias=T.CF[0:QS_ * (b - a), 20:21], scale=-1.0),
            "ut": ut, "uh": uh, "scan": scan, "met": met, "use": use, "ok": ok, "first": first, "any": any_, "sm": sm, "vl": vl, "zz": zz, "sz": sz, "n0": n0,
            "ul": ul, "d16": d16, "grep": grep, "lw": lw, "hh": hh}
        one = {
            "rec": lambda: op("V", lambda: V.reciprocal(T.RC[:], T.bL[:, 128:256:2]), "tm0 tm1", "RC", "bL"),
            "rt": lambda: tt(T.RT[:], T.bL[:, 129:256:2], T.RC[:], A.mult, "tm0 tm1 RC", "RT", "bL"),
            "rm": lambda: tt(T.LI[:, 48:80], T.RT[:, 0:32], T.RT[:, 32:64], A.min, "RT", "rm"),
            "off": lambda: tc(T.OFF[:], T.LI[:, 48:80], "rm", "OFF"),
            "mc": mc_}
        ahead = {
            "as": asum,
            "ai": lambda: tc(T.AI[:, 0:1], T.bL[:, 64:65], "as1", "as2", "bL"),
            "ap": lambda: ts(T.AI[:, 1:2], T.AI[:, 0:1], 1, None, A.bitwise_and, None, "as2", "as3"),
            "nb": lambda: ts(T.NB[:, t + 1:t + 2], T.AI[:, 1:2], -2.0, 17.0 - 2 * QU, A.mult, A.add, "as3", "nb%d" % (t + 1))}
        half = {"xl": xl, "xh": xh, "hs": hs, "hc": hc, "tm": tm}

        def run(x):
            a, _, b = x.partition(":")
            if a in per:
                per[a](int(b[:1] or 0), int(b[1:] or 4))
            elif a in ("ad", "pr", "av", "pv"):
                gather(a, int(b[0]), int(b[1]))
            elif a in half:
                half[a](int(b))
            elif a in one:
                one[a]()
            elif a in ahead:
                if not last:
                    ahead[a]()
            elif t == 0:
                const(int(a[1:]))
        return run

    runs = [step(t) for t in range(T_STEPS)]
    for x in FIRST:
        runs[0](x)
    for t in range(T_STEPS - 1):
        for x in ORDER:
            runs[t + (x[0] == "+")](x.lstrip("+"))
    for x in LAST:
        runs[-1](x)
    need("G", [(s, cnt[s]) for s in ("V", "S", "T", "G")])
    need("G", [("l_" + x, 16) for x in LOADS] + [("o_" + x, 16) for x in OUTS])
    for t in range(1, T_STEPS):
        for q in SENDS:
            need("G", [("r%s%d%s" % (q[0], t, q[1]), len(eng(prv, core))), ("s%s%d%s" % (q[0], t, q[1]), len(eng(core, nxt)))])
